import numpy as np
import ml_dtypes


def mxq(x, axis, fmt="e4m3"):
    dtype, down = {"e4m3": (ml_dtypes.float8_e4m3fn, 7), "e5m2": (ml_dtypes.float8_e5m2, 14)}[fmt]
    v = np.moveaxis(np.asarray(x, np.float32).astype(ml_dtypes.bfloat16).astype(np.float64), axis, -1)
    blocks = v.reshape(v.shape[:-1] + (-1, 32))
    amax = np.abs(blocks).max(-1, keepdims=True)
    byte = np.maximum(np.where(amax > 0, np.frexp(amax)[1] - 1 + 127, 0) - down, 1)
    scale = np.exp2(byte - 127.0)
    codes = (blocks / scale).astype(np.float32).astype(dtype).astype(np.float64)
    return np.moveaxis((codes * scale).reshape(v.shape), -1, axis)


WIDE = False


def mx_kscale(k):
    if not WIDE:
        return np.ones(k)
    levels = np.array([10, -10, 5, -5, 0])
    if k % 512:
        return np.exp2(np.random.permutation(np.resize(levels, k // 32))).repeat(32)
    a = np.empty((k // 512, 16))
    for p in range(k // 512):
        a[p, :8] = np.random.permutation(np.resize(levels, 8))
        for g in range(8):
            far = levels[np.abs(levels - a[p, g]) >= 10]
            a[p, g + 8] = far[np.random.randint(len(far))]
    return np.exp2(a.ravel()).repeat(32)


BF16 = ml_dtypes.bfloat16


def bf(x):
    return np.asarray(x, np.float32).astype(BF16)


def f64(x):
    return np.asarray(x).astype(np.float64)


E2M1 = np.array([0.0, 0.5, 1.0, 1.5, 2.0, 3.0, 4.0, 6.0, -0.0, -0.5, -1.0, -1.5, -2.0, -3.0, -4.0, -6.0])


def pack_weight(w, fmt):
    k, n = w.shape
    w = f64(bf(w)).reshape(k // 32, 32, n)
    amax = np.abs(w).max(1)
    if fmt == "e4m3":
        byte = np.frexp(amax)[1] - 1 + 127 - 7
    else:
        mant, ex = np.frexp(amax / 6.0)
        byte = np.where(mant > 0.5, ex, ex - 1) + 127
    byte = np.clip(np.where(amax > 0, byte, 1), 1, 254)
    scaled = (w * np.exp2(127.0 - byte)[:, None, :]).reshape(k, n).astype(np.float32)
    by_word = np.ascontiguousarray(scaled.reshape(k // 512, 128, 4, n).transpose(0, 1, 3, 2))
    if fmt == "e4m3":
        words = by_word.astype(ml_dtypes.float8_e4m3fn).view(np.uint8)
    else:
        c = by_word.astype(ml_dtypes.float4_e2m1fn).view(np.uint8) & 0xF
        words = c[..., 0::2] | (c[..., 1::2] << 4)
    return np.ascontiguousarray(words), np.ascontiguousarray(byte.astype(np.uint8).reshape(k // 512, 16, n))


def unpack_weight(words, scales, fmt):
    g, p, n, _ = words.shape
    if fmt == "e4m3":
        vals = np.ascontiguousarray(words).view(ml_dtypes.float8_e4m3fn).astype(np.float64)
    else:
        nib = np.empty((g, p, n, 4), np.uint8)
        nib[..., 0::2] = words & 0xF
        nib[..., 1::2] = words >> 4
        vals = E2M1[nib]
    vals = vals * np.repeat(np.exp2(scales.astype(np.float64) - 127.0), 8, axis=1)[..., None]
    return vals.transpose(0, 1, 3, 2).reshape(g * 512, n)
def pack4(w):
    words, scales = pack_weight(w, "e2m1")
    return words.reshape(words.shape[0], 128, -1), scales


def unpack4(words, scales):
    return unpack_weight(words.reshape(words.shape[0], 128, -1, 2), scales, "e2m1")


BITS, D, Q, DOCS = 1024, 1536, 1024, 2048


def draw0():
    s, t = mx_kscale(D), mx_kscale(BITS)
    planes = 2.0 * np.random.standard_normal((BITS, D)) / np.sqrt(D) / s
    queries = np.random.standard_normal((Q, D)) * s
    offset = 0.5 * np.random.standard_normal(BITS)
    bit_gain = (1 + 0.1 * np.random.standard_normal(BITS)) * t
    codes = np.random.standard_normal((BITS, DOCS)) / np.sqrt(BITS) / t[:, None]
    codes_words, codes_scales = pack4(codes)
    return {"planes": bf(planes),
            "queries": bf(queries),
            "offset": bf(offset),
            "bit_gain": bf(bit_gain),
            "codes_words": codes_words,
            "codes_scales": codes_scales}


def core(planes, queries, offset, bit_gain, codes_words, codes_scales):
    h = mxq(f64(planes), 1, "e4m3") @ mxq(f64(queries), 1, "e4m3").T
    z = np.tanh(h + f64(offset)[:, None]) * f64(bit_gain)[:, None]
    return mxq(z, 0, "e4m3").T @ unpack4(codes_words, codes_scales)


def e4m3fn_bytes(y):
    return np.clip(np.asarray(y, np.float64), -448.0, 448.0).astype(np.float32).astype(ml_dtypes.float8_e4m3fn).view(np.uint8)


def e4m3fn_values(b):
    return np.asarray(b, np.uint8).view(ml_dtypes.float8_e4m3fn).astype(np.float64)


def setup_inputs():
    d = draw0()
    x0 = np.asarray(d['queries']).astype(np.float64)
    s = (np.max(np.abs(x0), axis=(0,), keepdims=True) / 448.0).astype(np.float32)
    out = {}
    for k, v in d.items():
        if k == 'queries':
            out['queries_bytes'] = e4m3fn_bytes(x0 / s.astype(np.float64))
            out['queries_scale'] = s
        else:
            out[k] = v
    return out


def reference(planes, queries_bytes, queries_scale, offset, bit_gain, codes_words, codes_scales):
    return core(planes, e4m3fn_values(queries_bytes) * queries_scale.astype(np.float64), offset, bit_gain, codes_words, codes_scales)

@@ -1,0 +1,327 @@
+from contextlib import ExitStack
+
+import concourse.mybir as mybir
+from concourse.masks import make_identity
+
+BITS, D, Q, DOCS = 1024, 1536, 1024, 2048
+FLOPS = 2 * BITS * D * Q + 2 * Q * BITS * DOCS
+
+F32 = mybir.dt.float32
+BF16 = mybir.dt.bfloat16
+I32 = mybir.dt.int32
+U32 = mybir.dt.uint32
+U8 = mybir.dt.uint8
+FP8 = mybir.dt.float8_e4m3fn
+FP8X4 = mybir.dt.float8_e4m3fn_x4
+FP4X4 = mybir.dt.float4_e2m1fn_x4
+ACT = mybir.ActivationFunctionType
+MULT = mybir.AluOpType.mult
+
+P = 128
+KD = D // 512
+KB = BITS // 512
+SLAB = 256
+NS = Q // SLAB
+NB = 512
+ND = DOCS // NB
+
+
+def tile_soft_hyperplane_hashing_s13_kernel(tc, planes, queries_bytes, queries_scale, offset, bit_gain, codes_words, codes_scales, out):
+    nc = tc.nc
+    with ExitStack() as ctx:
+        keep = ctx.enter_context(tc.tile_pool(name="keep", bufs=1))
+        work = ctx.enter_context(tc.tile_pool(name="work", bufs=3))
+        psum = ctx.enter_context(tc.psum_pool(name="psum", bufs=3))
+
+        ident = keep.tile([P, P], F32, name="ident")
+        zeros = keep.tile([P, 512], BF16, name="zeros")
+        ones = keep.tile([P, 1], F32, name="ones")
+        warm = keep.tile([P, 1], F32, name="warm")
+        q_scale = keep.tile([P, KD * 4], F32, name="q_scale")
+        off = keep.tile([P, KB * 4], BF16, name="off")
+        gain = keep.tile([P, KB * 4], BF16, name="gain")
+        q_bytes = [keep.tile([P, 2 * D], U8, name="q_bytes%d" % s) for s in range(NS)]
+        p_raw = [[keep.tile([P, 2, D], BF16, name="p_raw%d%d" % (g, h)) for h in range(2)] for g in range(KB)]
+        p_codes = [keep.tile([P, BITS], U32, name="p_codes%d" % g, align_bytes=64) for g in range(KD)]
+        p_scales = [keep.tile([P, BITS], U8, name="p_scales%d" % g, align_bytes=64) for g in range(KD)]
+        q_codes = [keep.tile([P, KD, SLAB], U32, name="q_codes%d" % s, align_bytes=64) for s in range(NS)]
+        q_scales = [keep.tile([P, KD, SLAB], U8, name="q_scales%d" % s, align_bytes=64) for s in range(NS)]
+        z_codes = [keep.tile([P, KB, SLAB], U32, name="z_codes%d" % s, align_bytes=64) for s in range(NS)]
+        z_scales = [keep.tile([P, KB, SLAB], U8, name="z_scales%d" % s, align_bytes=64) for s in range(NS)]
+        c_codes = keep.tile([P, KB, 2 * DOCS], U8, name="c_codes", align_bytes=64)
+        c_scales = keep.tile([P, KB, DOCS], U8, name="c_scales", align_bytes=64)
+
+        q_view = queries_bytes.rearrange("(s p i) k -> s p (i k)", p=P, i=2)
+        p_view = planes.rearrange("(g m t) k -> g m t k", m=P, t=4)
+        out_view = out.rearrange("(s p i) d -> s i p d", p=P, i=2)
+
+        def load_q(s, parts=1):
+            w = 2 * D // parts
+            for i in range(parts):
+                nc.sync.dma_start(out=q_bytes[s][:, i * w : (i + 1) * w], in_=q_view[s][:, i * w : (i + 1) * w])
+
+        def load_p(g, h):
+            nc.sync.dma_start(out=p_raw[g][h][:], in_=p_view[g][:, 2 * h : 2 * h + 2, :])
+
+        q_cast = {}
+        banks = {}
+        p_group = {}
+        q_group = {}
+        tanh_out = {}
+        z_group = {}
+
+        def dummy(n):
+            bank = psum.tile([P, 512], F32, name="hbank", bufs=2)
+            for j in range(n):
+                nc.tensor.matmul(bank[:], lhsT=zeros[:, 0:P], rhs=zeros[:], start=True, stop=True)
+
+        def cast(s, parts=1):
+            q_cast[s] = work.tile([P, 2, 2 * KD * P, 2], BF16, name="q_cast")
+            w = 2 * KD * P // parts
+            for i in range(parts):
+                nc.vector.tensor_scalar(
+                    out=q_cast[s][:, :, i * w : (i + 1) * w, :].rearrange("p u w e -> p w u e"),
+                    in0=q_bytes[s][:, 4 * i * w : 4 * (i + 1) * w].bitcast(FP8).rearrange("p (w u e) -> p w u e", u=2, e=2),
+                    scalar1=ones[:, 0:1],
+                    scalar2=None,
+                    op0=MULT,
+                )
+
+        def q_transpose(s):
+            words = q_cast[s][:].rearrange("p u w e -> p (u w e)").bitcast(F32)
+            for g in range(KD):
+                bank = psum.tile([P, 512], F32, name="tbank")
+                for u in range(2):
+                    for i in range(2):
+                        w0 = u * 2 * KD * P + i * KD * P + g * P
+                        nc.tensor.transpose(bank[:, u * 256 + i * P : u * 256 + (i + 1) * P], words[:, w0 : w0 + P], ident[:])
+                banks["q", s, g] = bank
+
+        def q_exit(s, g):
+            grouped = work.tile([P, SLAB, 2, 2], BF16, name="q_group", align_bytes=64)
+            bank = banks["q", s, g]
+            nc.vector.tensor_tensor(
+                out=grouped[:],
+                in0=bank[:].bitcast(BF16).rearrange("p (u c e) -> p c u e", u=2, e=2),
+                in1=q_scale[:, 4 * g : 4 * g + 4].rearrange("p (o u e) -> p o u e", o=1, u=2).to_broadcast([P, SLAB, 2, 2]),
+                op=MULT,
+            )
+            q_group[s, g] = grouped
+
+        def q_quant(s, g):
+            nc.vector.quantize_mx(
+                out=q_codes[s][:, g, :].bitcast(FP8X4),
+                scales=q_scales[s][:, g, :],
+                in_=q_group[s, g][:].rearrange("p c u e -> p (c u e)"),
+            )
+
+        def p_transpose(gb, h, dum=()):
+            for g in range(KD):
+                if g in dum:
+                    dummy(2)
+                bank = psum.tile([P, 512], F32, name="obank")
+                for u in range(2):
+                    for i in range(2):
+                        words = p_raw[gb][h][:, i, :].bitcast(F32)
+                        nc.tensor.transpose(
+                            bank[:, u * 256 + i * P : u * 256 + (i + 1) * P],
+                            words[:, 256 * g + u : 256 * (g + 1) : 2],
+                            ident[:],
+                        )
+                banks["p", gb, h, g] = bank
+
+        def p_exit(gb, h, g, eng):
+            grouped = work.tile([P, 256, 4], BF16, name="p_group", align_bytes=64, bufs=8)
+            dst = grouped[:].rearrange("p c t -> p (c t)").bitcast(F32).rearrange("p (c u) -> p c u", u=2)
+            bank_view = banks["p", gb, h, g][:].rearrange("p (u c) -> p c u", u=2)
+            if eng == "s":
+                nc.scalar.copy(out=dst, in_=bank_view)
+            else:
+                nc.vector.tensor_copy(out=dst, in_=bank_view)
+            p_group[gb, h, g] = grouped
+
+        def p_quant(gb, h, g):
+            cols = slice(gb * 512 + h * 256, gb * 512 + h * 256 + 256)
+            nc.vector.quantize_mx(
+                out=p_codes[g][:, cols].bitcast(FP8X4),
+                scales=p_scales[g][:, cols],
+                in_=p_group[gb, h, g][:].rearrange("p c t -> p (c t)"),
+            )
+
+        def project(s, gb):
+            th = work.tile([P, 4, SLAB], F32, name="th")
+            for tp in range(2):
+                bank = psum.tile([P, 2, SLAB], F32, name="hbank", bufs=2)
+                for t2 in range(2):
+                    c0 = gb * 512 + (tp * 2 + t2) * P
+                    for g in range(KD):
+                        nc.tensor.matmul_mx(
+                            out=bank[:, t2, :],
+                            lhsT=p_codes[g][:, c0 : c0 + P].bitcast(FP8X4),
+                            lhsT_scale=p_scales[g][:, c0 : c0 + P],
+                            rhs=q_codes[s][:, g, :].bitcast(FP8X4),
+                            rhs_scale=q_scales[s][:, g, :],
+                            start=(g == 0),
+                            stop=(g == KD - 1),
+                        )
+                for t2 in range(2):
+                    t = tp * 2 + t2
+                    nc.scalar.activation(out=th[:, t, :], in_=bank[:, t2, :], func=ACT.Tanh, bias=off[:, gb * 4 + t : gb * 4 + t + 1])
+            tanh_out[s, gb] = th
+
+        def weight(s, gb):
+            zg = work.tile([P, SLAB, 4], BF16, name="z_group", align_bytes=64)
+            nc.vector.tensor_tensor(
+                out=zg[:].rearrange("p (c i) t -> p c t i", i=4),
+                in0=tanh_out[s, gb][:].rearrange("p t (c i) -> p c t i", i=4),
+                in1=gain[:, gb * 4 : gb * 4 + 4].rearrange("p (o t i) -> p o t i", o=1, i=1).to_broadcast([P, SLAB // 4, 4, 4]),
+                op=MULT,
+            )
+            z_group[s, gb] = zg
+
+        def z_quant(s, gb):
+            nc.vector.quantize_mx(
+                out=z_codes[s][:, gb, :].bitcast(FP8X4),
+                scales=z_scales[s][:, gb, :],
+                in_=z_group[s, gb][:].rearrange("p n t -> p (n t)"),
+            )
+
+        def score(s, i, engines):
+            for half in range(2):
+                ot = work.tile([P, 2, NB], F32, name="ot", bufs=8)
+                for b in range(2):
+                    d = half * 2 + b
+                    bank = psum.tile([P, NB], F32, name="obank")
+                    for gb in range(KB):
+                        nc.tensor.matmul_mx(
+                            out=bank[:],
+                            lhsT=z_codes[s][:, gb, i * P : (i + 1) * P].bitcast(FP8X4),
+                            lhsT_scale=z_scales[s][:, gb, i * P : (i + 1) * P],
+                            rhs=c_codes[:, gb, d * 2 * NB : (d + 1) * 2 * NB].bitcast(FP4X4),
+                            rhs_scale=c_scales[:, gb, d * NB : (d + 1) * NB],
+                            start=(gb == 0),
+                            stop=(gb == KB - 1),
+                        )
+                    if engines[d] == "s":
+                        nc.scalar.copy(out=ot[:, b, :], in_=bank[:])
+                    else:
+                        nc.vector.tensor_copy(out=ot[:, b, :], in_=bank[:])
+                    if s == NS - 1 and i == 1:
+                        nc.sync.dma_start(out=out_view[s, i][:, d * NB : (d + 1) * NB], in_=ot[:, b, :])
+                if not (s == NS - 1 and i == 1):
+                    nc.sync.dma_start(out=out_view[s, i][:, half * 1024 : (half + 1) * 1024], in_=ot[:].rearrange("p b n -> p (b n)"))
+
+        with tc.manual_schedule():
+            load_q(0, 2)
+            nc.scalar.dma_start(out=q_scale[:].rearrange("p (g t) -> p g t", t=4), in_=queries_scale.rearrange("o (g p t) -> p (o g) t", p=P, t=4))
+            nc.vector.memset(zeros[:], 0.0)
+            dummy(8)
+            nc.vector.memset(ones[:], 1.0)
+            nc.scalar.activation(out=warm[:], in_=ones[:], func=ACT.Tanh)
+            make_identity(nc, ident[:])
+            nc.gpsimd.memset(c_scales[:].rearrange("p g n -> p (g n)").bitcast(U32), 0)
+            load_q(1)
+            load_p(0, 0)
+            load_p(0, 1)
+            load_p(1, 0)
+            load_p(1, 1)
+            nc.sync.dma_start(out=off[:].rearrange("p (g t) -> p g t", t=4), in_=offset.rearrange("(g p t) -> p g t", p=P, t=4))
+            nc.sync.dma_start(out=gain[:].rearrange("p (g t) -> p g t", t=4), in_=bit_gain.rearrange("(g p t) -> p g t", p=P, t=4))
+            load_q(2)
+            nc.sync.dma_start(out=c_codes[:].rearrange("p g n -> p g n").bitcast(I32), in_=codes_words.rearrange("g p n -> p g n").bitcast(I32))
+            for qd in range(4):
+                nc.sync.dma_start(
+                    out=c_scales[32 * qd : 32 * qd + 4, :, :].bitcast(I32),
+                    in_=codes_scales.rearrange("g q n -> q g n")[4 * qd : 4 * qd + 4].bitcast(I32),
+                )
+            load_q(3)
+
+            def exits(gb, h, engs="sss"):
+                for g in range(KD):
+                    p_exit(gb, h, g, engs[g])
+
+            def quants(gb, h):
+                for g in range(KD):
+                    p_quant(gb, h, g)
+
+            def xq(s, a):
+                for g in a:
+                    q_exit(s, g)
+                    if g > 0:
+                        q_quant(s, g - 1)
+            cast(0, parts=2)
+            q_transpose(0)
+            cast(1)
+            p_transpose(0, 0)
+            exits(0, 0)
+            q_exit(0, 0)
+            q_exit(0, 1)
+            q_quant(0, 0)
+            q_exit(0, 2)
+            q_quant(0, 1)
+            quants(0, 0)
+            q_quant(0, 2)
+            p_transpose(0, 1, (0,))
+            exits(0, 1)
+            quants(0, 1)
+            q_transpose(1)
+            p_transpose(1, 0)
+            exits(1, 0)
+            quants(1, 0)
+            p_transpose(1, 1, (0,))
+            exits(1, 1)
+            project(0, 0)
+            q_exit(1, 0)
+            quants(1, 1)
+            project(0, 1)
+            q_exit(1, 1)
+            q_quant(1, 0)
+            q_exit(1, 2)
+            q_quant(1, 1)
+            q_quant(1, 2)
+            project(1, 0)
+            cast(2)
+            weight(0, 0)
+            project(1, 1)
+            q_transpose(2)
+            weight(0, 1)
+            z_quant(0, 0)
+            z_quant(0, 1)
+            q_exit(2, 0)
+            q_exit(2, 1)
+            q_quant(2, 0)
+            cast(3)
+            score(0, 0, "ssss")
+            q_exit(2, 2)
+            q_quant(2, 1)
+            q_quant(2, 2)
+            weight(1, 0)
+            weight(1, 1)
+            z_quant(1, 0)
+            score(0, 1, "ssss")
+            q_transpose(3)
+            project(2, 0)
+            z_quant(1, 1)
+            q_exit(3, 0)
+            project(2, 1)
+            q_exit(3, 1)
+            q_quant(3, 0)
+            q_exit(3, 2)
+            q_quant(3, 1)
+            score(1, 0, "ssss")
+            q_quant(3, 2)
+            weight(2, 0)
+            weight(2, 1)
+            z_quant(2, 0)
+            score(1, 1, "ssss")
+            project(3, 0)
+            z_quant(2, 1)
+            project(3, 1)
+            weight(3, 0)
+            score(2, 0, "ssss")
+            weight(3, 1)
+            z_quant(3, 0)
+            z_quant(3, 1)
+            score(2, 1, "ssvs")
+            score(3, 0, "svsv")
+            score(3, 1, "svsv")

@@ -20,10 +20,10 @@ MULT = mybir.AluOpType.mult
 P = 128
 KD = D // 512
 KB = BITS // 512
-SLAB = 256
-NS = Q // SLAB
+NBLK = Q // P
 NB = 512
 ND = DOCS // NB
+WALK = 4
 
 
 def tile_soft_hyperplane_hashing_s13_kernel(tc, planes, queries_bytes, queries_scale, offset, bit_gain, codes_words, codes_scales, out):
@@ -40,29 +40,21 @@ def tile_soft_hyperplane_hashing_s13_kernel(tc, planes, queries_bytes, queries_s
         q_scale = keep.tile([P, KD * 4], F32, name="q_scale")
         off = keep.tile([P, KB * 4], BF16, name="off")
         gain = keep.tile([P, KB * 4], BF16, name="gain")
-        q_bytes = [keep.tile([P, 2 * D], U8, name="q_bytes%d" % s) for s in range(NS)]
-        p_raw = [[keep.tile([P, 2, D], BF16, name="p_raw%d%d" % (g, h)) for h in range(2)] for g in range(KB)]
         p_codes = [keep.tile([P, BITS], U32, name="p_codes%d" % g, align_bytes=64) for g in range(KD)]
         p_scales = [keep.tile([P, BITS], U8, name="p_scales%d" % g, align_bytes=64) for g in range(KD)]
-        q_codes = [keep.tile([P, KD, SLAB], U32, name="q_codes%d" % s, align_bytes=64) for s in range(NS)]
-        q_scales = [keep.tile([P, KD, SLAB], U8, name="q_scales%d" % s, align_bytes=64) for s in range(NS)]
-        z_codes = [keep.tile([P, KB, SLAB], U32, name="z_codes%d" % s, align_bytes=64) for s in range(NS)]
-        z_scales = [keep.tile([P, KB, SLAB], U8, name="z_scales%d" % s, align_bytes=64) for s in range(NS)]
+        q_codes = [keep.tile([P, Q], U32, name="q_codes%d" % g, align_bytes=64) for g in range(KD)]
+        q_scales = [keep.tile([P, Q], U8, name="q_scales%d" % g, align_bytes=64) for g in range(KD)]
+        z_codes = [keep.tile([P, Q], U32, name="z_codes%d" % g, align_bytes=64) for g in range(KB)]
+        z_scales = [keep.tile([P, Q], U8, name="z_scales%d" % g, align_bytes=64) for g in range(KB)]
         c_codes = keep.tile([P, KB, 2 * DOCS], U8, name="c_codes", align_bytes=64)
         c_scales = keep.tile([P, KB, DOCS], U8, name="c_scales", align_bytes=64)
 
-        q_view = queries_bytes.rearrange("(s p i) k -> s p (i k)", p=P, i=2)
+        q_view = queries_bytes.rearrange("(b p) k -> p b k", p=P)
         p_view = planes.rearrange("(g m t) k -> g m t k", m=P, t=4)
-        out_view = out.rearrange("(s p i) d -> s i p d", p=P, i=2)
+        out_view = out.rearrange("(b p) d -> b p d", p=P)
 
-        def load_q(s, parts=1):
-            w = 2 * D // parts
-            for i in range(parts):
-                nc.sync.dma_start(out=q_bytes[s][:, i * w : (i + 1) * w], in_=q_view[s][:, i * w : (i + 1) * w])
-
-        def load_p(g, h):
-            nc.sync.dma_start(out=p_raw[g][h][:], in_=p_view[g][:, 2 * h : 2 * h + 2, :])
-
+        q_bytes = {}
+        p_raw = {}
         q_cast = {}
         banks = {}
         p_group = {}
@@ -70,258 +62,281 @@ def tile_soft_hyperplane_hashing_s13_kernel(tc, planes, queries_bytes, queries_s
         tanh_out = {}
         z_group = {}
 
+        def load_q(b, n):
+            raw = keep.tile([P, n, D], U8, name="q_bytes%d" % b)
+            nc.sync.dma_start(out=raw[:], in_=q_view[:, b : b + n, :])
+            for i in range(n):
+                q_bytes[b + i] = (raw, i)
+
+        def load_p(j, g0, g1):
+            raw = keep.tile([P, 2, (g1 - g0) * 512], BF16, name="p_raw%d%d" % (j, g0))
+            nc.sync.dma_start(out=raw[:], in_=p_view[j // 2][:, 2 * (j % 2) : 2 * (j % 2) + 2, g0 * 512 : g1 * 512])
+            for g in range(g0, g1):
+                p_raw[j, g] = (raw, g - g0)
+
         def dummy(n):
-            bank = psum.tile([P, 512], F32, name="hbank", bufs=2)
+            bank = psum.tile([P, 512], F32, name="hbank", bufs=5)
             for j in range(n):
                 nc.tensor.matmul(bank[:], lhsT=zeros[:, 0:P], rhs=zeros[:], start=True, stop=True)
 
-        def cast(s, parts=1):
-            q_cast[s] = work.tile([P, 2, 2 * KD * P, 2], BF16, name="q_cast")
-            w = 2 * KD * P // parts
-            for i in range(parts):
-                nc.vector.tensor_scalar(
-                    out=q_cast[s][:, :, i * w : (i + 1) * w, :].rearrange("p u w e -> p w u e"),
-                    in0=q_bytes[s][:, 4 * i * w : 4 * (i + 1) * w].bitcast(FP8).rearrange("p (w u e) -> p w u e", u=2, e=2),
-                    scalar1=ones[:, 0:1],
-                    scalar2=None,
-                    op0=MULT,
-                )
+        def cast(b, g0=0, g1=KD):
+            raw, i = q_bytes[b]
+            wide = work.tile([P, 2, (g1 - g0) * P, 2], BF16, name="q_cast", bufs=4)
+            nc.vector.tensor_scalar(
+                out=wide[:].rearrange("p u w e -> p w u e"),
+                in0=raw[:, i, g0 * 512 : g1 * 512].bitcast(FP8).rearrange("p (w u e) -> p w u e", u=2, e=2),
+                scalar1=ones[:, 0:1],
+                scalar2=None,
+                op0=MULT,
+            )
+            for g in range(g0, g1):
+                q_cast[b, g] = (wide, g - g0)
 
-        def q_transpose(s):
-            words = q_cast[s][:].rearrange("p u w e -> p (u w e)").bitcast(F32)
+        def cast_plain(b):
+            raw, i = q_bytes[b]
+            wide = work.tile([P, D], BF16, name="q_plain", bufs=2)
+            nc.scalar.copy(out=wide[:], in_=raw[:, i, :].bitcast(FP8))
             for g in range(KD):
-                bank = psum.tile([P, 512], F32, name="tbank")
-                for u in range(2):
-                    for i in range(2):
-                        w0 = u * 2 * KD * P + i * KD * P + g * P
-                        nc.tensor.transpose(bank[:, u * 256 + i * P : u * 256 + (i + 1) * P], words[:, w0 : w0 + P], ident[:])
-                banks["q", s, g] = bank
+                q_cast[b, g] = (wide, None)
 
-        def q_exit(s, g):
-            grouped = work.tile([P, SLAB, 2, 2], BF16, name="q_group", align_bytes=64)
-            bank = banks["q", s, g]
+        def q_transpose(b, n, gs=range(KD)):
+            for g in gs:
+                bank = psum.tile([P, 2, n * P], F32, name="hbank", bufs=5)
+                for i in range(n):
+                    wide, gl = q_cast[b + i, g]
+                    for u in range(2):
+                        if gl is None:
+                            words = wide[:].bitcast(F32)[:, 256 * g + u : 256 * (g + 1) : 2]
+                        else:
+                            words = wide[:, u, :, :].rearrange("p w e -> p (w e)").bitcast(F32)[:, gl * P : (gl + 1) * P]
+                        nc.tensor.transpose(bank[:, u, i * P : (i + 1) * P], words, ident[:])
+                banks["q", b, g] = bank
+
+        def q_exit(b, n, g):
+            grouped = work.tile([P, n * P, 2, 2], BF16, name="q_group", align_bytes=64)
             nc.vector.tensor_tensor(
                 out=grouped[:],
-                in0=bank[:].bitcast(BF16).rearrange("p (u c e) -> p c u e", u=2, e=2),
-                in1=q_scale[:, 4 * g : 4 * g + 4].rearrange("p (o u e) -> p o u e", o=1, u=2).to_broadcast([P, SLAB, 2, 2]),
+                in0=banks["q", b, g][:].rearrange("p u c -> p (u c)").bitcast(BF16).rearrange("p (u c e) -> p c u e", u=2, e=2),
+                in1=q_scale[:, 4 * g : 4 * g + 4].rearrange("p (o u e) -> p o u e", o=1, u=2).to_broadcast([P, n * P, 2, 2]),
                 op=MULT,
             )
-            q_group[s, g] = grouped
+            q_group[b, g] = grouped
 
-        def q_quant(s, g):
+        def q_quant(b, n, g):
+            cols = slice(b * P, (b + n) * P)
             nc.vector.quantize_mx(
-                out=q_codes[s][:, g, :].bitcast(FP8X4),
-                scales=q_scales[s][:, g, :],
-                in_=q_group[s, g][:].rearrange("p c u e -> p (c u e)"),
+                out=q_codes[g][:, cols].bitcast(FP8X4),
+                scales=q_scales[g][:, cols],
+                in_=q_group[b, g][:].rearrange("p c u e -> p (c u e)"),
             )
 
-        def p_transpose(gb, h, dum=()):
-            for g in range(KD):
-                if g in dum:
-                    dummy(2)
-                bank = psum.tile([P, 512], F32, name="obank")
-                for u in range(2):
-                    for i in range(2):
-                        words = p_raw[gb][h][:, i, :].bitcast(F32)
-                        nc.tensor.transpose(
-                            bank[:, u * 256 + i * P : u * 256 + (i + 1) * P],
-                            words[:, 256 * g + u : 256 * (g + 1) : 2],
-                            ident[:],
-                        )
-                banks["p", gb, h, g] = bank
-
-        def p_exit(gb, h, g, eng):
-            grouped = work.tile([P, 256, 4], BF16, name="p_group", align_bytes=64, bufs=8)
+        def p_transpose(j, g):
+            raw, gl = p_raw[j, g]
+            bank = psum.tile([P, 512], F32, name="obank")
+            for u in range(2):
+                for i in range(2):
+                    words = raw[:, i, :].bitcast(F32)
+                    nc.tensor.transpose(bank[:, u * 256 + i * P : u * 256 + (i + 1) * P], words[:, 256 * gl + u : 256 * (gl + 1) : 2], ident[:])
+            grouped = work.tile([P, 256, 4], BF16, name="p_group", align_bytes=64, bufs=6)
             dst = grouped[:].rearrange("p c t -> p (c t)").bitcast(F32).rearrange("p (c u) -> p c u", u=2)
-            bank_view = banks["p", gb, h, g][:].rearrange("p (u c) -> p c u", u=2)
-            if eng == "s":
-                nc.scalar.copy(out=dst, in_=bank_view)
-            else:
-                nc.vector.tensor_copy(out=dst, in_=bank_view)
-            p_group[gb, h, g] = grouped
+            nc.scalar.copy(out=dst, in_=bank[:].rearrange("p (u c) -> p c u", u=2))
+            p_group[j, g] = grouped
 
-        def p_quant(gb, h, g):
-            cols = slice(gb * 512 + h * 256, gb * 512 + h * 256 + 256)
+        def p_quant(j, g):
+            cols = slice(j * 256, (j + 1) * 256)
             nc.vector.quantize_mx(
                 out=p_codes[g][:, cols].bitcast(FP8X4),
                 scales=p_scales[g][:, cols],
-                in_=p_group[gb, h, g][:].rearrange("p c t -> p (c t)"),
+                in_=p_group[j, g][:].rearrange("p c t -> p (c t)"),
             )
 
-        def project(s, gb):
-            th = work.tile([P, 4, SLAB], F32, name="th")
-            for tp in range(2):
-                bank = psum.tile([P, 2, SLAB], F32, name="hbank", bufs=2)
-                for t2 in range(2):
-                    c0 = gb * 512 + (tp * 2 + t2) * P
-                    for g in range(KD):
-                        nc.tensor.matmul_mx(
-                            out=bank[:, t2, :],
-                            lhsT=p_codes[g][:, c0 : c0 + P].bitcast(FP8X4),
-                            lhsT_scale=p_scales[g][:, c0 : c0 + P],
-                            rhs=q_codes[s][:, g, :].bitcast(FP8X4),
-                            rhs_scale=q_scales[s][:, g, :],
-                            start=(g == 0),
-                            stop=(g == KD - 1),
-                        )
-                for t2 in range(2):
-                    t = tp * 2 + t2
-                    nc.scalar.activation(out=th[:, t, :], in_=bank[:, t2, :], func=ACT.Tanh, bias=off[:, gb * 4 + t : gb * 4 + t + 1])
-            tanh_out[s, gb] = th
+        def project(b, n, j, tag="hbank", nbufs=5):
+            if j % 2 == 0:
+                th = work.tile([P, 4, n * P], F32, name="th", bufs=4)
+                for i in range(n):
+                    tanh_out[b + i, j // 2] = (th, i)
+            th = tanh_out[b, j // 2][0]
+            cols = slice(b * P, (b + n) * P)
+            bank = psum.tile([P, 2, n * P], F32, name=tag, bufs=nbufs)
+            for t2 in range(2):
+                c0 = j * 256 + t2 * P
+                for g in range(KD):
+                    nc.tensor.matmul_mx(
+                        out=bank[:, t2, :],
+                        lhsT=p_codes[g][:, c0 : c0 + P].bitcast(FP8X4),
+                        lhsT_scale=p_scales[g][:, c0 : c0 + P],
+                        rhs=q_codes[g][:, cols].bitcast(FP8X4),
+                        rhs_scale=q_scales[g][:, cols],
+                        start=(g == 0),
+                        stop=(g == KD - 1),
+                    )
+            for t2 in range(2):
+                t = 2 * j + t2
+                nc.scalar.activation(out=th[:, t % 4, :], in_=bank[:, t2, :], func=ACT.Tanh, bias=off[:, t : t + 1])
 
-        def weight(s, gb):
-            zg = work.tile([P, SLAB, 4], BF16, name="z_group", align_bytes=64)
+        def weight(b, n, gb):
+            th, i0 = tanh_out[b, gb]
+            lo = i0 * P
+            zg = work.tile([P, n * P, 4], BF16, name="z_group", align_bytes=64)
             nc.vector.tensor_tensor(
-                out=zg[:].rearrange("p (c i) t -> p c t i", i=4),
-                in0=tanh_out[s, gb][:].rearrange("p t (c i) -> p c t i", i=4),
-                in1=gain[:, gb * 4 : gb * 4 + 4].rearrange("p (o t i) -> p o t i", o=1, i=1).to_broadcast([P, SLAB // 4, 4, 4]),
+                out=zg[:].rearrange("p (c i) t -> p c t i", i=WALK),
+                in0=th[:, :, lo : lo + n * P].rearrange("p t (c i) -> p c t i", i=WALK),
+                in1=gain[:, gb * 4 : gb * 4 + 4].rearrange("p (o t i) -> p o t i", o=1, i=1).to_broadcast([P, n * P // WALK, 4, WALK]),
                 op=MULT,
             )
-            z_group[s, gb] = zg
+            z_group[b, gb] = zg
 
-        def z_quant(s, gb):
+        def z_quant(b, n, gb):
+            cols = slice(b * P, (b + n) * P)
             nc.vector.quantize_mx(
-                out=z_codes[s][:, gb, :].bitcast(FP8X4),
-                scales=z_scales[s][:, gb, :],
-                in_=z_group[s, gb][:].rearrange("p n t -> p (n t)"),
+                out=z_codes[gb][:, cols].bitcast(FP8X4),
+                scales=z_scales[gb][:, cols],
+                in_=z_group[b, gb][:].rearrange("p n t -> p (n t)"),
             )
 
-        def score(s, i, engines):
-            for half in range(2):
-                ot = work.tile([P, 2, NB], F32, name="ot", bufs=8)
-                for b in range(2):
-                    d = half * 2 + b
-                    bank = psum.tile([P, NB], F32, name="obank")
-                    for gb in range(KB):
-                        nc.tensor.matmul_mx(
-                            out=bank[:],
-                            lhsT=z_codes[s][:, gb, i * P : (i + 1) * P].bitcast(FP8X4),
-                            lhsT_scale=z_scales[s][:, gb, i * P : (i + 1) * P],
-                            rhs=c_codes[:, gb, d * 2 * NB : (d + 1) * 2 * NB].bitcast(FP4X4),
-                            rhs_scale=c_scales[:, gb, d * NB : (d + 1) * NB],
-                            start=(gb == 0),
-                            stop=(gb == KB - 1),
-                        )
-                    if engines[d] == "s":
-                        nc.scalar.copy(out=ot[:, b, :], in_=bank[:])
-                    else:
-                        nc.vector.tensor_copy(out=ot[:, b, :], in_=bank[:])
-                    if s == NS - 1 and i == 1:
-                        nc.sync.dma_start(out=out_view[s, i][:, d * NB : (d + 1) * NB], in_=ot[:, b, :])
-                if not (s == NS - 1 and i == 1):
-                    nc.sync.dma_start(out=out_view[s, i][:, half * 1024 : (half + 1) * 1024], in_=ot[:].rearrange("p b n -> p (b n)"))
+        def score(b, half, engines="ss", single=False):
+            cols = slice(b * P, (b + 1) * P)
+            ot = work.tile([P, 2, NB], F32, name="ot", bufs=6)
+            for e in range(2):
+                d = half * 2 + e
+                bank = psum.tile([P, NB], F32, name="obank")
+                for gb in range(KB):
+                    nc.tensor.matmul_mx(
+                        out=bank[:],
+                        lhsT=z_codes[gb][:, cols].bitcast(FP8X4),
+                        lhsT_scale=z_scales[gb][:, cols],
+                        rhs=c_codes[:, gb, d * 2 * NB : (d + 1) * 2 * NB].bitcast(FP4X4),
+                        rhs_scale=c_scales[:, gb, d * NB : (d + 1) * NB],
+                        start=(gb == 0),
+                        stop=(gb == KB - 1),
+                    )
+                if engines[e] == "s":
+                    nc.scalar.copy(out=ot[:, e, :], in_=bank[:])
+                else:
+                    nc.vector.tensor_copy(out=ot[:, e, :], in_=bank[:])
+                if single:
+                    nc.sync.dma_start(out=out_view[b][:, d * NB : (d + 1) * NB], in_=ot[:, e, :])
+            if not single:
+                nc.sync.dma_start(out=out_view[b][:, half * 1024 : (half + 1) * 1024], in_=ot[:].rearrange("p e n -> p (e n)"))
 
-        with tc.manual_schedule():
-            load_q(0, 2)
-            nc.scalar.dma_start(out=q_scale[:].rearrange("p (g t) -> p g t", t=4), in_=queries_scale.rearrange("o (g p t) -> p (o g) t", p=P, t=4))
-            nc.vector.memset(zeros[:], 0.0)
-            dummy(8)
-            nc.vector.memset(ones[:], 1.0)
-            nc.scalar.activation(out=warm[:], in_=ones[:], func=ACT.Tanh)
-            make_identity(nc, ident[:])
-            nc.gpsimd.memset(c_scales[:].rearrange("p g n -> p (g n)").bitcast(U32), 0)
-            load_q(1)
-            load_p(0, 0)
-            load_p(0, 1)
-            load_p(1, 0)
-            load_p(1, 1)
-            nc.sync.dma_start(out=off[:].rearrange("p (g t) -> p g t", t=4), in_=offset.rearrange("(g p t) -> p g t", p=P, t=4))
-            nc.sync.dma_start(out=gain[:].rearrange("p (g t) -> p g t", t=4), in_=bit_gain.rearrange("(g p t) -> p g t", p=P, t=4))
-            load_q(2)
-            nc.sync.dma_start(out=c_codes[:].rearrange("p g n -> p g n").bitcast(I32), in_=codes_words.rearrange("g p n -> p g n").bitcast(I32))
+        def load_vec(dst, src):
+            nc.sync.dma_start(out=dst[:].rearrange("p (g t) -> p g t", t=4), in_=src.rearrange("(g p t) -> p g t", p=P, t=4))
+
+        def load_c():
+            nc.sync.dma_start(out=c_codes[:].bitcast(I32), in_=codes_words.rearrange("g p n -> p g n").bitcast(I32))
             for qd in range(4):
                 nc.sync.dma_start(
                     out=c_scales[32 * qd : 32 * qd + 4, :, :].bitcast(I32),
                     in_=codes_scales.rearrange("g q n -> q g n")[4 * qd : 4 * qd + 4].bitcast(I32),
                 )
-            load_q(3)
 
-            def exits(gb, h, engs="sss"):
-                for g in range(KD):
-                    p_exit(gb, h, g, engs[g])
+        def setup():
+            nc.scalar.dma_start(out=q_scale[:].rearrange("p (g t) -> p g t", t=4), in_=queries_scale.rearrange("o (g p t) -> p (o g) t", p=P, t=4))
+            nc.vector.memset(zeros[:], 0.0)
+            nc.vector.memset(ones[:], 1.0)
+            nc.scalar.activation(out=warm[:], in_=ones[:], func=ACT.Tanh)
+            make_identity(nc, ident[:])
+            nc.gpsimd.memset(c_scales[:].rearrange("p g n -> p (g n)").bitcast(U32), 0)
 
-            def quants(gb, h):
-                for g in range(KD):
-                    p_quant(gb, h, g)
+        def q_chain(b, n):
+            for g in range(KD):
+                q_exit(b, n, g)
+                if g > 0:
+                    q_quant(b, n, g - 1)
+            q_quant(b, n, KD - 1)
 
-            def xq(s, a):
-                for g in a:
-                    q_exit(s, g)
-                    if g > 0:
-                        q_quant(s, g - 1)
-            cast(0, parts=2)
-            q_transpose(0)
-            cast(1)
+        def planes_in(j):
+            for g in range(KD):
+                p_transpose(j, g)
+
+        def planes_quant(j):
+            for g in range(KD):
+                p_quant(j, g)
+
+        with tc.manual_schedule():
+            load_q(0, 1)
+            setup()
+            load_q(1, 1)
+            load_p(0, 0, 1)
+            load_p(0, 1, 3)
+            load_p(1, 0, 3)
+            load_p(2, 0, 3)
+            load_q(2, 2)
+            load_vec(off, offset)
+            load_p(3, 0, 3)
+            load_vec(gain, bit_gain)
+            load_q(4, 2)
+            load_c()
+            load_q(6, 2)
+            dummy(6)
+            cast(0)
+            cast(1, 0, 1)
+            cast(1, 1, 3)
+            q_transpose(0, 2, [0])
             p_transpose(0, 0)
-            exits(0, 0)
-            q_exit(0, 0)
-            q_exit(0, 1)
-            q_quant(0, 0)
-            q_exit(0, 2)
-            q_quant(0, 1)
-            quants(0, 0)
-            q_quant(0, 2)
-            p_transpose(0, 1, (0,))
-            exits(0, 1)
-            quants(0, 1)
-            q_transpose(1)
-            p_transpose(1, 0)
-            exits(1, 0)
-            quants(1, 0)
-            p_transpose(1, 1, (0,))
-            exits(1, 1)
-            project(0, 0)
-            q_exit(1, 0)
-            quants(1, 1)
-            project(0, 1)
-            q_exit(1, 1)
-            q_quant(1, 0)
-            q_exit(1, 2)
-            q_quant(1, 1)
-            q_quant(1, 2)
-            project(1, 0)
+            q_transpose(0, 2, [1, 2])
+            dummy(1)
+            p_transpose(0, 1)
+            p_transpose(0, 2)
+            dummy(1)
+            q_exit(0, 2, 0)
+            q_exit(0, 2, 1)
+            q_quant(0, 2, 0)
+            q_exit(0, 2, 2)
+            q_quant(0, 2, 1)
+            p_quant(0, 0)
+            p_quant(0, 1)
+            q_quant(0, 2, 2)
+            p_quant(0, 2)
             cast(2)
-            weight(0, 0)
-            project(1, 1)
-            q_transpose(2)
-            weight(0, 1)
-            z_quant(0, 0)
-            z_quant(0, 1)
-            q_exit(2, 0)
-            q_exit(2, 1)
-            q_quant(2, 0)
             cast(3)
-            score(0, 0, "ssss")
-            q_exit(2, 2)
-            q_quant(2, 1)
-            q_quant(2, 2)
-            weight(1, 0)
-            weight(1, 1)
-            z_quant(1, 0)
-            score(0, 1, "ssss")
-            q_transpose(3)
-            project(2, 0)
-            z_quant(1, 1)
-            q_exit(3, 0)
-            project(2, 1)
-            q_exit(3, 1)
-            q_quant(3, 0)
-            q_exit(3, 2)
-            q_quant(3, 1)
-            score(1, 0, "ssss")
-            q_quant(3, 2)
-            weight(2, 0)
-            weight(2, 1)
-            z_quant(2, 0)
-            score(1, 1, "ssss")
-            project(3, 0)
-            z_quant(2, 1)
-            project(3, 1)
-            weight(3, 0)
-            score(2, 0, "ssss")
-            weight(3, 1)
-            z_quant(3, 0)
-            z_quant(3, 1)
-            score(2, 1, "ssvs")
-            score(3, 0, "svsv")
-            score(3, 1, "svsv")
+            p_transpose(1, 0)
+            p_transpose(1, 1)
+            dummy(1)
+            p_transpose(1, 2)
+            p_transpose(2, 0)
+            planes_quant(1)
+            project(0, 2, 0)
+            p_transpose(2, 1)
+            q_transpose(2, 2)
+            p_transpose(2, 2)
+            project(0, 2, 1)
+            q_exit(2, 2, 0)
+            planes_quant(2)
+            planes_in(3)
+            q_exit(2, 2, 1)
+            q_quant(2, 2, 0)
+            project(0, 2, 2)
+            q_exit(2, 2, 2)
+            q_quant(2, 2, 1)
+            p_quant(3, 0)
+            q_quant(2, 2, 2)
+            p_quant(3, 1)
+            p_quant(3, 2)
+            project(2, 2, 0)
+            project(0, 2, 3)
+            for s in range(1, 4):
+                b = 2 * s
+                if s < 3:
+                    cast(b + 2)
+                    cast(b + 3)
+                for j in range(1 if s == 1 else 0, 4):
+                    project(b, 2, j)
+                weight(b - 2, 2, 0)
+                weight(b - 2, 2, 1)
+                z_quant(b - 2, 2, 0)
+                z_quant(b - 2, 2, 1)
+                if s < 3:
+                    q_transpose(b + 2, 2)
+                    q_chain(b + 2, 2)
+                else:
+                    weight(b, 2, 0)
+                    weight(b, 2, 1)
+                    z_quant(b, 2, 0)
+                    z_quant(b, 2, 1)
+                for i in range(2):
+                    for half in range(2):
+                        score(b - 2 + i, half)
+            for i in range(2):
+                for half in range(2):
+                    score(6 + i, half, "sv", i == 1)

@@ -20,7 +20,9 @@ MULT = mybir.AluOpType.mult
 P = 128
 KD = D // 512
 KB = BITS // 512
-NBLK = Q // P
+SLAB = 256
+NS = Q // SLAB
+PARTS = ((0, 2), (2, 3))
 NB = 512
 ND = DOCS // NB
 WALK = 4
@@ -40,12 +42,12 @@ def tile_soft_hyperplane_hashing_s13_kernel(tc, planes, queries_bytes, queries_s
         q_scale = keep.tile([P, KD * 4], F32, name="q_scale")
         off = keep.tile([P, KB * 4], BF16, name="off")
         gain = keep.tile([P, KB * 4], BF16, name="gain")
-        p_codes = [keep.tile([P, BITS], U32, name="p_codes%d" % g, align_bytes=64) for g in range(KD)]
-        p_scales = [keep.tile([P, BITS], U8, name="p_scales%d" % g, align_bytes=64) for g in range(KD)]
-        q_codes = [keep.tile([P, Q], U32, name="q_codes%d" % g, align_bytes=64) for g in range(KD)]
-        q_scales = [keep.tile([P, Q], U8, name="q_scales%d" % g, align_bytes=64) for g in range(KD)]
-        z_codes = [keep.tile([P, Q], U32, name="z_codes%d" % g, align_bytes=64) for g in range(KB)]
-        z_scales = [keep.tile([P, Q], U8, name="z_scales%d" % g, align_bytes=64) for g in range(KB)]
+        p_codes = [keep.tile([P, KD, 256], U32, name="p_codes%d" % j, align_bytes=64) for j in range(4)]
+        p_scales = [keep.tile([P, KD, 256], U8, name="p_scales%d" % j, align_bytes=64) for j in range(4)]
+        q_codes = [keep.tile([P, KD, SLAB], U32, name="q_codes%d" % s, align_bytes=64) for s in range(NS)]
+        q_scales = [keep.tile([P, KD, SLAB], U8, name="q_scales%d" % s, align_bytes=64) for s in range(NS)]
+        z_codes = [keep.tile([P, KB, SLAB], U32, name="z_codes%d" % s, align_bytes=64) for s in range(NS)]
+        z_scales = [keep.tile([P, KB, SLAB], U8, name="z_scales%d" % s, align_bytes=64) for s in range(NS)]
         c_codes = keep.tile([P, KB, 2 * DOCS], U8, name="c_codes", align_bytes=64)
         c_scales = keep.tile([P, KB, DOCS], U8, name="c_scales", align_bytes=64)
 
@@ -81,7 +83,7 @@ def tile_soft_hyperplane_hashing_s13_kernel(tc, planes, queries_bytes, queries_s
 
         def cast(b, g0=0, g1=KD):
             raw, i = q_bytes[b]
-            wide = work.tile([P, 2, (g1 - g0) * P, 2], BF16, name="q_cast", bufs=4)
+            wide = work.tile([P, 2, (g1 - g0) * P, 2], BF16, name="q_cast", bufs=3)
             nc.vector.tensor_scalar(
                 out=wide[:].rearrange("p u w e -> p w u e"),
                 in0=raw[:, i, g0 * 512 : g1 * 512].bitcast(FP8).rearrange("p (w u e) -> p w u e", u=2, e=2),
@@ -92,6 +94,20 @@ def tile_soft_hyperplane_hashing_s13_kernel(tc, planes, queries_bytes, queries_s
             for g in range(g0, g1):
                 q_cast[b, g] = (wide, g - g0)
 
+        def cast_slab(s):
+            raw = q_bytes[2 * s][0]
+            wide = work.tile([P, 2, 2 * KD * P, 2], BF16, name="q_cast", bufs=3)
+            nc.vector.tensor_scalar(
+                out=wide[:].rearrange("p u w e -> p w u e"),
+                in0=raw[:].rearrange("p n k -> p (n k)").bitcast(FP8).rearrange("p (w u e) -> p w u e", u=2, e=2),
+                scalar1=ones[:, 0:1],
+                scalar2=None,
+                op0=MULT,
+            )
+            for i in range(2):
+                for g in range(KD):
+                    q_cast[2 * s + i, g] = (wide, i * KD + g)
+
         def cast_plain(b):
             raw, i = q_bytes[b]
             wide = work.tile([P, D], BF16, name="q_plain", bufs=2)
@@ -99,36 +115,43 @@ def tile_soft_hyperplane_hashing_s13_kernel(tc, planes, queries_bytes, queries_s
             for g in range(KD):
                 q_cast[b, g] = (wide, None)
 
-        def q_transpose(b, n, gs=range(KD)):
+        def q_transpose(s, gs=range(KD)):
             for g in gs:
-                bank = psum.tile([P, 2, n * P], F32, name="hbank", bufs=5)
-                for i in range(n):
-                    wide, gl = q_cast[b + i, g]
+                bank = psum.tile([P, 2, SLAB], F32, name="hbank", bufs=5)
+                for i in range(2):
+                    wide, gl = q_cast[2 * s + i, g]
                     for u in range(2):
                         if gl is None:
                             words = wide[:].bitcast(F32)[:, 256 * g + u : 256 * (g + 1) : 2]
                         else:
                             words = wide[:, u, :, :].rearrange("p w e -> p (w e)").bitcast(F32)[:, gl * P : (gl + 1) * P]
                         nc.tensor.transpose(bank[:, u, i * P : (i + 1) * P], words, ident[:])
-                banks["q", b, g] = bank
+                banks["q", s, g] = bank
 
-        def q_exit(b, n, g):
-            grouped = work.tile([P, n * P, 2, 2], BF16, name="q_group", align_bytes=64)
+        def group_tile(store, key, g, name, nbufs):
+            g0, g1 = PARTS[g // 2]
+            if (key, g0) not in store:
+                store[key, g0] = work.tile([P, g1 - g0, 1024], BF16, name="%s%d" % (name, g0), align_bytes=64, bufs=nbufs)
+            return store[key, g0][:, g - g0, :]
+
+        def q_exit(s, g):
             nc.vector.tensor_tensor(
-                out=grouped[:],
-                in0=banks["q", b, g][:].rearrange("p u c -> p (u c)").bitcast(BF16).rearrange("p (u c e) -> p c u e", u=2, e=2),
-                in1=q_scale[:, 4 * g : 4 * g + 4].rearrange("p (o u e) -> p o u e", o=1, u=2).to_broadcast([P, n * P, 2, 2]),
+                out=group_tile(q_group, s, g, "q_group", 2).rearrange("p (c u e) -> p c u e", u=2, e=2),
+                in0=banks["q", s, g][:].rearrange("p u c -> p (u c)").bitcast(BF16).rearrange("p (u c e) -> p c u e", u=2, e=2),
+                in1=q_scale[:, 4 * g : 4 * g + 4].rearrange("p (o u e) -> p o u e", o=1, u=2).to_broadcast([P, SLAB, 2, 2]),
                 op=MULT,
             )
-            q_group[b, g] = grouped
 
-        def q_quant(b, n, g):
-            cols = slice(b * P, (b + n) * P)
+        def quantise(codes, scales, grouped):
             nc.vector.quantize_mx(
-                out=q_codes[g][:, cols].bitcast(FP8X4),
-                scales=q_scales[g][:, cols],
-                in_=q_group[b, g][:].rearrange("p c u e -> p (c u e)"),
+                out=codes.rearrange("p g c -> p (g c)").bitcast(FP8X4),
+                scales=scales.rearrange("p g c -> p (g c)"),
+                in_=grouped.rearrange("p g c -> p (g c)"),
             )
+
+        def q_quant(s, part):
+            g0, g1 = PARTS[part]
+            quantise(q_codes[s][:, g0:g1, :], q_scales[s][:, g0:g1, :], q_group[s, g0][:])
 
         def p_transpose(j, g):
             raw, gl = p_raw[j, g]
@@ -137,36 +160,26 @@ def tile_soft_hyperplane_hashing_s13_kernel(tc, planes, queries_bytes, queries_s
                 for i in range(2):
                     words = raw[:, i, :].bitcast(F32)
                     nc.tensor.transpose(bank[:, u * 256 + i * P : u * 256 + (i + 1) * P], words[:, 256 * gl + u : 256 * (gl + 1) : 2], ident[:])
-            grouped = work.tile([P, 256, 4], BF16, name="p_group", align_bytes=64, bufs=6)
-            dst = grouped[:].rearrange("p c t -> p (c t)").bitcast(F32).rearrange("p (c u) -> p c u", u=2)
+            dst = group_tile(p_group, j, g, "p_group", 3).bitcast(F32).rearrange("p (c u) -> p c u", u=2)
             nc.scalar.copy(out=dst, in_=bank[:].rearrange("p (u c) -> p c u", u=2))
-            p_group[j, g] = grouped
 
-        def p_quant(j, g):
-            cols = slice(j * 256, (j + 1) * 256)
-            nc.vector.quantize_mx(
-                out=p_codes[g][:, cols].bitcast(FP8X4),
-                scales=p_scales[g][:, cols],
-                in_=p_group[j, g][:].rearrange("p c t -> p (c t)"),
-            )
+        def p_quant(j, part):
+            g0, g1 = PARTS[part]
+            quantise(p_codes[j][:, g0:g1, :], p_scales[j][:, g0:g1, :], p_group[j, g0][:])
 
-        def project(b, n, j, tag="hbank", nbufs=5):
+        def project(s, j):
             if j % 2 == 0:
-                th = work.tile([P, 4, n * P], F32, name="th", bufs=4)
-                for i in range(n):
-                    tanh_out[b + i, j // 2] = (th, i)
-            th = tanh_out[b, j // 2][0]
-            cols = slice(b * P, (b + n) * P)
-            bank = psum.tile([P, 2, n * P], F32, name=tag, bufs=nbufs)
+                tanh_out[s, j // 2] = work.tile([P, 4, SLAB], F32, name="th", bufs=4)
+            th = tanh_out[s, j // 2]
+            bank = psum.tile([P, 2, SLAB], F32, name="hbank", bufs=5)
             for t2 in range(2):
-                c0 = j * 256 + t2 * P
                 for g in range(KD):
                     nc.tensor.matmul_mx(
                         out=bank[:, t2, :],
-                        lhsT=p_codes[g][:, c0 : c0 + P].bitcast(FP8X4),
-                        lhsT_scale=p_scales[g][:, c0 : c0 + P],
-                        rhs=q_codes[g][:, cols].bitcast(FP8X4),
-                        rhs_scale=q_scales[g][:, cols],
+                        lhsT=p_codes[j][:, g, t2 * P : (t2 + 1) * P].bitcast(FP8X4),
+                        lhsT_scale=p_scales[j][:, g, t2 * P : (t2 + 1) * P],
+                        rhs=q_codes[s][:, g, :].bitcast(FP8X4),
+                        rhs_scale=q_scales[s][:, g, :],
                         start=(g == 0),
                         stop=(g == KD - 1),
                     )
@@ -174,28 +187,21 @@ def tile_soft_hyperplane_hashing_s13_kernel(tc, planes, queries_bytes, queries_s
                 t = 2 * j + t2
                 nc.scalar.activation(out=th[:, t % 4, :], in_=bank[:, t2, :], func=ACT.Tanh, bias=off[:, t : t + 1])
 
-        def weight(b, n, gb):
-            th, i0 = tanh_out[b, gb]
-            lo = i0 * P
-            zg = work.tile([P, n * P, 4], BF16, name="z_group", align_bytes=64)
+        def weight(s, gb):
+            if gb == 0:
+                z_group[s] = work.tile([P, KB, 4 * SLAB], BF16, name="z_group", align_bytes=64, bufs=2)
             nc.vector.tensor_tensor(
-                out=zg[:].rearrange("p (c i) t -> p c t i", i=WALK),
-                in0=th[:, :, lo : lo + n * P].rearrange("p t (c i) -> p c t i", i=WALK),
-                in1=gain[:, gb * 4 : gb * 4 + 4].rearrange("p (o t i) -> p o t i", o=1, i=1).to_broadcast([P, n * P // WALK, 4, WALK]),
+                out=z_group[s][:, gb, :].rearrange("p (c i t) -> p c t i", i=WALK, t=4),
+                in0=tanh_out[s, gb][:].rearrange("p t (c i) -> p c t i", i=WALK),
+                in1=gain[:, gb * 4 : gb * 4 + 4].rearrange("p (o t i) -> p o t i", o=1, i=1).to_broadcast([P, SLAB // WALK, 4, WALK]),
                 op=MULT,
             )
-            z_group[b, gb] = zg
 
-        def z_quant(b, n, gb):
-            cols = slice(b * P, (b + n) * P)
-            nc.vector.quantize_mx(
-                out=z_codes[gb][:, cols].bitcast(FP8X4),
-                scales=z_scales[gb][:, cols],
-                in_=z_group[b, gb][:].rearrange("p n t -> p (n t)"),
-            )
+        def z_quant(s, gb):
+            quantise(z_codes[s][:, gb : gb + 1, :], z_scales[s][:, gb : gb + 1, :], z_group[s][:, gb : gb + 1, :])
 
         def score(b, half, engines="ss", single=False):
-            cols = slice(b * P, (b + 1) * P)
+            s, cols = b // 2, slice((b % 2) * P, (b % 2 + 1) * P)
             ot = work.tile([P, 2, NB], F32, name="ot", bufs=6)
             for e in range(2):
                 d = half * 2 + e
@@ -203,8 +209,8 @@ def tile_soft_hyperplane_hashing_s13_kernel(tc, planes, queries_bytes, queries_s
                 for gb in range(KB):
                     nc.tensor.matmul_mx(
                         out=bank[:],
-                        lhsT=z_codes[gb][:, cols].bitcast(FP8X4),
-                        lhsT_scale=z_scales[gb][:, cols],
+                        lhsT=z_codes[s][:, gb, cols].bitcast(FP8X4),
+                        lhsT_scale=z_scales[s][:, gb, cols],
                         rhs=c_codes[:, gb, d * 2 * NB : (d + 1) * 2 * NB].bitcast(FP4X4),
                         rhs_scale=c_scales[:, gb, d * NB : (d + 1) * NB],
                         start=(gb == 0),
@@ -238,30 +244,24 @@ def tile_soft_hyperplane_hashing_s13_kernel(tc, planes, queries_bytes, queries_s
             make_identity(nc, ident[:])
             nc.gpsimd.memset(c_scales[:].rearrange("p g n -> p (g n)").bitcast(U32), 0)
 
-        def q_chain(b, n):
-            for g in range(KD):
-                q_exit(b, n, g)
-                if g > 0:
-                    q_quant(b, n, g - 1)
-            q_quant(b, n, KD - 1)
-
         def planes_in(j):
             for g in range(KD):
                 p_transpose(j, g)
 
         def planes_quant(j):
-            for g in range(KD):
-                p_quant(j, g)
+            for part in range(2):
+                p_quant(j, part)
 
         with tc.manual_schedule():
             load_q(0, 1)
             setup()
             load_q(1, 1)
+            load_q(2, 1)
             load_p(0, 0, 1)
             load_p(0, 1, 3)
             load_p(1, 0, 3)
             load_p(2, 0, 3)
-            load_q(2, 2)
+            load_q(3, 1)
             load_vec(off, offset)
             load_p(3, 0, 3)
             load_vec(gain, bit_gain)
@@ -272,23 +272,20 @@ def tile_soft_hyperplane_hashing_s13_kernel(tc, planes, queries_bytes, queries_s
             cast(0)
             cast(1, 0, 1)
             cast(1, 1, 3)
-            q_transpose(0, 2, [0])
+            cast_plain(2)
+            q_transpose(0)
             p_transpose(0, 0)
-            q_transpose(0, 2, [1, 2])
             dummy(1)
             p_transpose(0, 1)
             p_transpose(0, 2)
             dummy(1)
-            q_exit(0, 2, 0)
-            q_exit(0, 2, 1)
-            q_quant(0, 2, 0)
-            q_exit(0, 2, 2)
-            q_quant(0, 2, 1)
+            q_exit(0, 0)
+            q_exit(0, 1)
+            q_exit(0, 2)
+            q_quant(0, 0)
             p_quant(0, 0)
+            q_quant(0, 1)
             p_quant(0, 1)
-            q_quant(0, 2, 2)
-            p_quant(0, 2)
-            cast(2)
             cast(3)
             p_transpose(1, 0)
             p_transpose(1, 1)
@@ -296,47 +293,47 @@ def tile_soft_hyperplane_hashing_s13_kernel(tc, planes, queries_bytes, queries_s
             p_transpose(1, 2)
             p_transpose(2, 0)
             planes_quant(1)
-            project(0, 2, 0)
+            project(0, 0)
+            q_transpose(1)
             p_transpose(2, 1)
-            q_transpose(2, 2)
+            project(0, 1)
+            q_exit(1, 0)
+            q_exit(1, 1)
             p_transpose(2, 2)
-            project(0, 2, 1)
-            q_exit(2, 2, 0)
-            planes_quant(2)
             planes_in(3)
-            q_exit(2, 2, 1)
-            q_quant(2, 2, 0)
-            project(0, 2, 2)
-            q_exit(2, 2, 2)
-            q_quant(2, 2, 1)
-            p_quant(3, 0)
-            q_quant(2, 2, 2)
-            p_quant(3, 1)
-            p_quant(3, 2)
-            project(2, 2, 0)
-            project(0, 2, 3)
-            for s in range(1, 4):
-                b = 2 * s
-                if s < 3:
-                    cast(b + 2)
-                    cast(b + 3)
+            q_exit(1, 2)
+            p_quant(2, 0)
+            q_quant(1, 0)
+            p_quant(2, 1)
+            q_quant(1, 1)
+            project(0, 2)
+            planes_quant(3)
+            project(1, 0)
+            project(0, 3)
+            for s in range(1, NS):
+                more = s + 1 < NS
+                if more:
+                    cast_slab(s + 1)
                 for j in range(1 if s == 1 else 0, 4):
-                    project(b, 2, j)
-                weight(b - 2, 2, 0)
-                weight(b - 2, 2, 1)
-                z_quant(b - 2, 2, 0)
-                z_quant(b - 2, 2, 1)
-                if s < 3:
-                    q_transpose(b + 2, 2)
-                    q_chain(b + 2, 2)
+                    project(s, j)
+                weight(s - 1, 0)
+                weight(s - 1, 1)
+                z_quant(s - 1, 0)
+                z_quant(s - 1, 1)
+                if more:
+                    q_transpose(s + 1)
+                    for g in range(KD):
+                        q_exit(s + 1, g)
+                    q_quant(s + 1, 0)
+                    q_quant(s + 1, 1)
                 else:
-                    weight(b, 2, 0)
-                    weight(b, 2, 1)
-                    z_quant(b, 2, 0)
-                    z_quant(b, 2, 1)
+                    weight(s, 0)
+                    weight(s, 1)
+                    z_quant(s, 0)
+                    z_quant(s, 1)
                 for i in range(2):
                     for half in range(2):
-                        score(b - 2 + i, half)
+                        score(2 * s - 2 + i, half, "ss" if more or i == 0 else "sv")
             for i in range(2):
                 for half in range(2):
                     score(6 + i, half, "sv", i == 1)

@@ -256,65 +256,54 @@ def tile_soft_hyperplane_hashing_s13_kernel(tc, planes, queries_bytes, queries_s
             load_q(0, 1)
             setup()
             load_q(1, 1)
-            load_q(2, 1)
+            load_q(2, 2)
             load_p(0, 0, 1)
             load_p(0, 1, 3)
             load_p(1, 0, 3)
             load_p(2, 0, 3)
-            load_q(3, 1)
             load_vec(off, offset)
             load_p(3, 0, 3)
             load_vec(gain, bit_gain)
             load_q(4, 2)
             load_c()
             load_q(6, 2)
-            dummy(6)
+            dummy(7)
             cast(0)
             cast(1, 0, 1)
             cast(1, 1, 3)
-            cast_plain(2)
+            cast_slab(1)
             q_transpose(0)
             p_transpose(0, 0)
-            dummy(1)
+            dummy(2)
             p_transpose(0, 1)
             p_transpose(0, 2)
-            dummy(1)
             q_exit(0, 0)
+            q_transpose(1)
             q_exit(0, 1)
             q_exit(0, 2)
+            planes_in(1)
             q_quant(0, 0)
-            p_quant(0, 0)
             q_quant(0, 1)
-            p_quant(0, 1)
-            cast(3)
-            p_transpose(1, 0)
-            p_transpose(1, 1)
-            dummy(1)
-            p_transpose(1, 2)
-            p_transpose(2, 0)
-            planes_quant(1)
-            project(0, 0)
-            q_transpose(1)
-            p_transpose(2, 1)
-            project(0, 1)
+            planes_quant(0)
+            planes_in(2)
             q_exit(1, 0)
-            q_exit(1, 1)
-            p_transpose(2, 2)
+            planes_quant(1)
             planes_in(3)
-            q_exit(1, 2)
-            p_quant(2, 0)
-            q_quant(1, 0)
-            p_quant(2, 1)
-            q_quant(1, 1)
+            q_exit(1, 1)
+            planes_quant(2)
+            project(0, 0)
+            project(0, 1)
             project(0, 2)
+            q_exit(1, 2)
             planes_quant(3)
-            project(1, 0)
             project(0, 3)
+            q_quant(1, 0)
+            q_quant(1, 1)
             for s in range(1, NS):
                 more = s + 1 < NS
                 if more:
                     cast_slab(s + 1)
-                for j in range(1 if s == 1 else 0, 4):
+                for j in range(4):
                     project(s, j)
                 weight(s - 1, 0)
                 weight(s - 1, 1)

@@ -25,7 +25,7 @@ NS = Q // SLAB
 PARTS = ((0, 2), (2, 3))
 NB = 512
 ND = DOCS // NB
-WALK = 4
+WALK = 2
 
 
 def tile_soft_hyperplane_hashing_s13_kernel(tc, planes, queries_bytes, queries_scale, offset, bit_gain, codes_words, codes_scales, out):

@@ -51,9 +51,9 @@ def tile_soft_hyperplane_hashing_s13_kernel(tc, planes, queries_bytes, queries_s
         c_codes = keep.tile([P, KB, 2 * DOCS], U8, name="c_codes", align_bytes=64)
         c_scales = keep.tile([P, KB, DOCS], U8, name="c_scales", align_bytes=64)
 
-        q_view = queries_bytes.rearrange("(b p) k -> p b k", p=P)
+        q_view = queries_bytes.rearrange("(s p i) k -> s p i k", p=P, i=2)
         p_view = planes.rearrange("(g m t) k -> g m t k", m=P, t=4)
-        out_view = out.rearrange("(b p) d -> b p d", p=P)
+        out_view = out.rearrange("(s p i) d -> s i p d", p=P, i=2)
 
         q_bytes = {}
         p_raw = {}
@@ -66,7 +66,7 @@ def tile_soft_hyperplane_hashing_s13_kernel(tc, planes, queries_bytes, queries_s
 
         def load_q(b, n):
             raw = keep.tile([P, n, D], U8, name="q_bytes%d" % b)
-            nc.sync.dma_start(out=raw[:], in_=q_view[:, b : b + n, :])
+            nc.sync.dma_start(out=raw[:], in_=q_view[b // 2][:, b % 2 : b % 2 + n, :])
             for i in range(n):
                 q_bytes[b + i] = (raw, i)
 
@@ -115,10 +115,12 @@ def tile_soft_hyperplane_hashing_s13_kernel(tc, planes, queries_bytes, queries_s
             for g in range(KD):
                 q_cast[b, g] = (wide, None)
 
-        def q_transpose(s, gs=range(KD)):
+        def q_transpose(s, gs=range(KD), blocks=(0, 1)):
             for g in gs:
-                bank = psum.tile([P, 2, SLAB], F32, name="hbank", bufs=5)
-                for i in range(2):
+                if blocks[0] == 0:
+                    banks["q", s, g] = psum.tile([P, 2, SLAB], F32, name="hbank", bufs=5)
+                bank = banks["q", s, g]
+                for i in blocks:
                     wide, gl = q_cast[2 * s + i, g]
                     for u in range(2):
                         if gl is None:
@@ -126,7 +128,6 @@ def tile_soft_hyperplane_hashing_s13_kernel(tc, planes, queries_bytes, queries_s
                         else:
                             words = wide[:, u, :, :].rearrange("p w e -> p (w e)").bitcast(F32)[:, gl * P : (gl + 1) * P]
                         nc.tensor.transpose(bank[:, u, i * P : (i + 1) * P], words, ident[:])
-                banks["q", s, g] = bank
 
         def group_tile(store, key, g, name, nbufs):
             g0, g1 = PARTS[g // 2]
@@ -203,7 +204,7 @@ def tile_soft_hyperplane_hashing_s13_kernel(tc, planes, queries_bytes, queries_s
         def score(b, half, engines="ss", single=False):
             s, cols = b // 2, slice((b % 2) * P, (b % 2 + 1) * P)
             ot = work.tile([P, 2, NB], F32, name="ot", bufs=6)
-            for e in range(2):
+            for e in range(len(engines)):
                 d = half * 2 + e
                 bank = psum.tile([P, NB], F32, name="obank")
                 for gb in range(KB):
@@ -221,9 +222,32 @@ def tile_soft_hyperplane_hashing_s13_kernel(tc, planes, queries_bytes, queries_s
                 else:
                     nc.vector.tensor_copy(out=ot[:, e, :], in_=bank[:])
                 if single:
-                    nc.sync.dma_start(out=out_view[b][:, d * NB : (d + 1) * NB], in_=ot[:, e, :])
+                    nc.sync.dma_start(out=out_view[s, b % 2][:, d * NB : (d + 1) * NB], in_=ot[:, e, :])
             if not single:
-                nc.sync.dma_start(out=out_view[b][:, half * 1024 : (half + 1) * 1024], in_=ot[:].rearrange("p e n -> p (e n)"))
+                nc.sync.dma_start(out=out_view[s, b % 2][:, half * 1024 : (half + 1) * 1024], in_=ot[:].rearrange("p e n -> p (e n)"))
+
+        def score_last(b):
+            s, cols = b // 2, slice((b % 2) * P, (b % 2 + 1) * P)
+            for e in range(2):
+                bank = psum.tile([P, 2, P], F32, name="obank")
+                n0 = DOCS - NB + e * 2 * P
+                for c in range(2):
+                    for gb in range(KB):
+                        nc.tensor.matmul_mx(
+                            out=bank[:, c, :],
+                            lhsT=z_codes[s][:, gb, cols].bitcast(FP8X4),
+                            lhsT_scale=z_scales[s][:, gb, cols],
+                            rhs=c_codes[:, gb, 2 * (n0 + c * P) : 2 * (n0 + (c + 1) * P)].bitcast(FP4X4),
+                            rhs_scale=c_scales[:, gb, n0 + c * P : n0 + (c + 1) * P],
+                            start=(gb == 0),
+                            stop=(gb == KB - 1),
+                        )
+                ot = work.tile([P, 2 * P], F32, name="ot_last", bufs=2)
+                if e == 0:
+                    nc.vector.tensor_copy(out=ot[:], in_=bank[:].rearrange("p c n -> p (c n)"))
+                else:
+                    nc.scalar.copy(out=ot[:], in_=bank[:].rearrange("p c n -> p (c n)"))
+                nc.sync.dma_start(out=out_view[s, b % 2][:, n0 : n0 + 2 * P], in_=ot[:])
 
         def load_vec(dst, src):
             nc.sync.dma_start(out=dst[:].rearrange("p (g t) -> p g t", t=4), in_=src.rearrange("(g p t) -> p g t", p=P, t=4))
@@ -256,29 +280,32 @@ def tile_soft_hyperplane_hashing_s13_kernel(tc, planes, queries_bytes, queries_s
             load_q(0, 1)
             setup()
             load_q(1, 1)
-            load_q(2, 2)
+            load_q(2, 1)
+            load_q(3, 1)
             load_p(0, 0, 1)
             load_p(0, 1, 3)
             load_p(1, 0, 3)
             load_p(2, 0, 3)
-            load_vec(off, offset)
             load_p(3, 0, 3)
+            load_vec(off, offset)
             load_vec(gain, bit_gain)
             load_q(4, 2)
             load_c()
             load_q(6, 2)
-            dummy(7)
+            dummy(6)
             cast(0)
             cast(1, 0, 1)
             cast(1, 1, 3)
-            cast_slab(1)
-            q_transpose(0)
+            cast_plain(2)
+            cast_plain(3)
+            q_transpose(0, blocks=(0,))
+            q_transpose(0, blocks=(1,))
             p_transpose(0, 0)
-            dummy(2)
+            q_exit(0, 0)
+            q_transpose(1, blocks=(0,))
             p_transpose(0, 1)
             p_transpose(0, 2)
-            q_exit(0, 0)
-            q_transpose(1)
+            q_transpose(1, blocks=(1,))
             q_exit(0, 1)
             q_exit(0, 2)
             planes_in(1)

@@ -16,16 +16,16 @@ FP8X4 = mybir.dt.float8_e4m3fn_x4
 FP4X4 = mybir.dt.float4_e2m1fn_x4
 ACT = mybir.ActivationFunctionType
 MULT = mybir.AluOpType.mult
+ADD = mybir.AluOpType.add
 
 P = 128
 KD = D // 512
 KB = BITS // 512
-SLAB = 256
-NS = Q // SLAB
-PARTS = ((0, 2), (2, 3))
 NB = 512
 ND = DOCS // NB
 WALK = 2
+NT = BITS // P
+UNITS = ((0, 1), (2, 3), (4, 5), (6, 7))
 
 
 def tile_soft_hyperplane_hashing_s13_kernel(tc, planes, queries_bytes, queries_scale, offset, bit_gain, codes_words, codes_scales, out):
@@ -33,7 +33,7 @@ def tile_soft_hyperplane_hashing_s13_kernel(tc, planes, queries_bytes, queries_s
     with ExitStack() as ctx:
         keep = ctx.enter_context(tc.tile_pool(name="keep", bufs=1))
         work = ctx.enter_context(tc.tile_pool(name="work", bufs=3))
-        psum = ctx.enter_context(tc.psum_pool(name="psum", bufs=3))
+        psum = ctx.enter_context(tc.psum_pool(name="psum", bufs=4))
 
         ident = keep.tile([P, P], F32, name="ident")
         zeros = keep.tile([P, 512], BF16, name="zeros")
@@ -42,12 +42,13 @@ def tile_soft_hyperplane_hashing_s13_kernel(tc, planes, queries_bytes, queries_s
         q_scale = keep.tile([P, KD * 4], F32, name="q_scale")
         off = keep.tile([P, KB * 4], BF16, name="off")
         gain = keep.tile([P, KB * 4], BF16, name="gain")
-        p_codes = [keep.tile([P, KD, 256], U32, name="p_codes%d" % j, align_bytes=64) for j in range(4)]
-        p_scales = [keep.tile([P, KD, 256], U8, name="p_scales%d" % j, align_bytes=64) for j in range(4)]
-        q_codes = [keep.tile([P, KD, SLAB], U32, name="q_codes%d" % s, align_bytes=64) for s in range(NS)]
-        q_scales = [keep.tile([P, KD, SLAB], U8, name="q_scales%d" % s, align_bytes=64) for s in range(NS)]
-        z_codes = [keep.tile([P, KB, SLAB], U32, name="z_codes%d" % s, align_bytes=64) for s in range(NS)]
-        z_scales = [keep.tile([P, KB, SLAB], U8, name="z_scales%d" % s, align_bytes=64) for s in range(NS)]
+        width = [P * len(blocks) for blocks in UNITS]
+        p_codes = [keep.tile([P, KD * P], U32, name="p_codes%d" % r, align_bytes=64) for r in range(NT)]
+        p_scales = [keep.tile([P, KD * P], U8, name="p_scales%d" % r, align_bytes=64) for r in range(NT)]
+        q_codes = [keep.tile([P, KD * w], U32, name="q_codes%d" % s, align_bytes=64) for s, w in enumerate(width)]
+        q_scales = [keep.tile([P, KD * w], U8, name="q_scales%d" % s, align_bytes=64) for s, w in enumerate(width)]
+        z_codes = [keep.tile([P, KB * w], U32, name="z_codes%d" % s, align_bytes=64) for s, w in enumerate(width)]
+        z_scales = [keep.tile([P, KB * w], U8, name="z_scales%d" % s, align_bytes=64) for s, w in enumerate(width)]
         c_codes = keep.tile([P, KB, 2 * DOCS], U8, name="c_codes", align_bytes=64)
         c_scales = keep.tile([P, KB, DOCS], U8, name="c_scales", align_bytes=64)
 
@@ -57,197 +58,213 @@ def tile_soft_hyperplane_hashing_s13_kernel(tc, planes, queries_bytes, queries_s
 
         q_bytes = {}
         p_raw = {}
+        p_rows = {}
         q_cast = {}
-        banks = {}
+        q_banks = {}
+        p_bank = {}
         p_group = {}
         q_group = {}
+        h_bank = {}
         tanh_out = {}
         z_group = {}
+        o_tile = {}
 
         def load_q(b, n):
             raw = keep.tile([P, n, D], U8, name="q_bytes%d" % b)
             nc.sync.dma_start(out=raw[:], in_=q_view[b // 2][:, b % 2 : b % 2 + n, :])
             for i in range(n):
-                q_bytes[b + i] = (raw, i)
+                q_bytes[b + i] = raw[:, i, :]
 
-        def load_p(j, g0, g1):
-            raw = keep.tile([P, 2, (g1 - g0) * 512], BF16, name="p_raw%d%d" % (j, g0))
-            nc.sync.dma_start(out=raw[:], in_=p_view[j // 2][:, 2 * (j % 2) : 2 * (j % 2) + 2, g0 * 512 : g1 * 512])
-            for g in range(g0, g1):
-                p_raw[j, g] = (raw, g - g0)
+        def load_p(r, n, g0=0, g1=KD):
+            raw = keep.tile([P, n * (g1 - g0) * 512], BF16, name="p_raw%d%d" % (r, g0))
+            nc.sync.dma_start(out=raw[:].rearrange("p (n k) -> p n k", n=n), in_=p_view[r // 4][:, r % 4 : r % 4 + n, g0 * 512 : g1 * 512])
+            for i in range(n):
+                if g1 - g0 == KD:
+                    p_rows[r + i] = raw[:, i * D : (i + 1) * D]
+                for g in range(g0, g1):
+                    w0 = (i * (g1 - g0) + g - g0) * 256
+                    p_raw[r + i, g] = [raw[:].bitcast(F32)[:, w0 + u : w0 + 256 : 2] for u in range(2)]
 
-        def dummy(n):
-            bank = psum.tile([P, 512], F32, name="hbank", bufs=5)
+        def sort_p(r, engine):
+            wide = work.tile([P, 2, KD * P, 2], BF16, name="p_sorted", bufs=4)
+            engine.tensor_scalar(
+                out=wide[:],
+                in0=p_rows[r].rearrange("p (w u e) -> p u w e", u=2, e=2),
+                scalar1=1.0,
+                scalar2=0.0,
+                op0=MULT,
+                op1=ADD,
+            )
+            for g in range(KD):
+                p_raw[r, g] = [wide[:, u, :, :].rearrange("p w e -> p (w e)").bitcast(F32)[:, g * P : (g + 1) * P] for u in range(2)]
+
+        def warm_up(n):
+            bank = psum.tile([P, 512], F32, name="hbank", bufs=8)
             for j in range(n):
                 nc.tensor.matmul(bank[:], lhsT=zeros[:, 0:P], rhs=zeros[:], start=True, stop=True)
 
-        def cast(b, g0=0, g1=KD):
-            raw, i = q_bytes[b]
-            wide = work.tile([P, 2, (g1 - g0) * P, 2], BF16, name="q_cast", bufs=3)
+        def cast(b):
+            wide = work.tile([P, 2, KD * P, 2], BF16, name="q_cast", bufs=4)
             nc.vector.tensor_scalar(
                 out=wide[:].rearrange("p u w e -> p w u e"),
-                in0=raw[:, i, g0 * 512 : g1 * 512].bitcast(FP8).rearrange("p (w u e) -> p w u e", u=2, e=2),
+                in0=q_bytes[b].bitcast(FP8).rearrange("p (w u e) -> p w u e", u=2, e=2),
                 scalar1=ones[:, 0:1],
                 scalar2=None,
                 op0=MULT,
             )
-            for g in range(g0, g1):
-                q_cast[b, g] = (wide, g - g0)
-
-        def cast_slab(s):
-            raw = q_bytes[2 * s][0]
-            wide = work.tile([P, 2, 2 * KD * P, 2], BF16, name="q_cast", bufs=3)
-            nc.vector.tensor_scalar(
-                out=wide[:].rearrange("p u w e -> p w u e"),
-                in0=raw[:].rearrange("p n k -> p (n k)").bitcast(FP8).rearrange("p (w u e) -> p w u e", u=2, e=2),
-                scalar1=ones[:, 0:1],
-                scalar2=None,
-                op0=MULT,
-            )
-            for i in range(2):
-                for g in range(KD):
-                    q_cast[2 * s + i, g] = (wide, i * KD + g)
+            for g in range(KD):
+                q_cast[b, g] = [wide[:, u, :, :].rearrange("p w e -> p (w e)").bitcast(F32)[:, g * P : (g + 1) * P] for u in range(2)]
 
         def cast_plain(b):
-            raw, i = q_bytes[b]
             wide = work.tile([P, D], BF16, name="q_plain", bufs=2)
-            nc.scalar.copy(out=wide[:], in_=raw[:, i, :].bitcast(FP8))
+            nc.scalar.copy(out=wide[:], in_=q_bytes[b].bitcast(FP8))
             for g in range(KD):
-                q_cast[b, g] = (wide, None)
+                q_cast[b, g] = [wide[:].bitcast(F32)[:, 256 * g + u : 256 * (g + 1) : 2] for u in range(2)]
 
-        def q_transpose(s, gs=range(KD), blocks=(0, 1)):
-            for g in gs:
-                if blocks[0] == 0:
-                    banks["q", s, g] = psum.tile([P, 2, SLAB], F32, name="hbank", bufs=5)
-                bank = banks["q", s, g]
-                for i in blocks:
-                    wide, gl = q_cast[2 * s + i, g]
-                    for u in range(2):
-                        if gl is None:
-                            words = wide[:].bitcast(F32)[:, 256 * g + u : 256 * (g + 1) : 2]
-                        else:
-                            words = wide[:, u, :, :].rearrange("p w e -> p (w e)").bitcast(F32)[:, gl * P : (gl + 1) * P]
-                        nc.tensor.transpose(bank[:, u, i * P : (i + 1) * P], words, ident[:])
+        def q_parts(s):
+            if s == 0:
+                return [[(0, 0), (1, 0)], [(0, 1), (1, 1)], [(2, 0), (2, 1)]]
+            if len(UNITS[s]) == 2:
+                return [[(g, 0), (g, 1)] for g in range(KD)]
+            return [[(0, 0), (1, 0)], [(2, 0)]]
 
-        def group_tile(store, key, g, name, nbufs):
-            g0, g1 = PARTS[g // 2]
-            if (key, g0) not in store:
-                store[key, g0] = work.tile([P, g1 - g0, 1024], BF16, name="%s%d" % (name, g0), align_bytes=64, bufs=nbufs)
-            return store[key, g0][:, g - g0, :]
+        def q_turn(s, n):
+            bank = psum.tile([P, 2, 2 * P], F32, name="hbank", bufs=8)
+            q_banks[s, n] = bank
+            for x, (g, i) in enumerate(q_parts(s)[n]):
+                for u in range(2):
+                    nc.tensor.transpose(bank[:, u, x * P : (x + 1) * P], q_cast[UNITS[s][i], g][u], ident[:])
 
-        def q_exit(s, g):
+        def q_exit(s, n):
+            if s not in q_group:
+                q_group[s] = work.tile([P, KD * 4 * width[s]], BF16, name="q_group", align_bytes=64, bufs=2)
+            parts = q_parts(s)[n]
+            nx = len(parts)
+            nb = len(UNITS[s])
+            pieces = q_group[s][:].rearrange("p (g i c u e) -> p g i c u e", g=KD, i=nb, u=2, e=2)
+            scale = q_scale[:].rearrange("p (g o u e) -> p g o u e", o=1, u=2, e=2)
+            g0, i0 = parts[0]
+            if parts[-1][0] == g0:
+                dst = pieces[:, g0, i0 : i0 + nx]
+            else:
+                dst = pieces[:, g0 : g0 + nx, i0]
             nc.vector.tensor_tensor(
-                out=group_tile(q_group, s, g, "q_group", 2).rearrange("p (c u e) -> p c u e", u=2, e=2),
-                in0=banks["q", s, g][:].rearrange("p u c -> p (u c)").bitcast(BF16).rearrange("p (u c e) -> p c u e", u=2, e=2),
-                in1=q_scale[:, 4 * g : 4 * g + 4].rearrange("p (o u e) -> p o u e", o=1, u=2).to_broadcast([P, SLAB, 2, 2]),
+                out=dst,
+                in0=q_banks[s, n][:].rearrange("p u c -> p (u c)").bitcast(BF16).rearrange("p (u x c e) -> p x c u e", u=2, x=2, e=2)[:, 0:nx],
+                in1=scale[:, g0 : parts[-1][0] + 1].to_broadcast([P, nx, P, 2, 2]),
                 op=MULT,
             )
 
-        def quantise(codes, scales, grouped):
-            nc.vector.quantize_mx(
-                out=codes.rearrange("p g c -> p (g c)").bitcast(FP8X4),
-                scales=scales.rearrange("p g c -> p (g c)"),
-                in_=grouped.rearrange("p g c -> p (g c)"),
-            )
+        def quantise(codes, scales, grouped, c0, c1):
+            nc.vector.quantize_mx(out=codes[:, c0:c1].bitcast(FP8X4), scales=scales[:, c0:c1], in_=grouped[:, 4 * c0 : 4 * c1])
 
-        def q_quant(s, part):
-            g0, g1 = PARTS[part]
-            quantise(q_codes[s][:, g0:g1, :], q_scales[s][:, g0:g1, :], q_group[s, g0][:])
+        def q_quant(s, g0, g1):
+            quantise(q_codes[s], q_scales[s], q_group[s], g0 * width[s], g1 * width[s])
 
-        def p_transpose(j, g):
-            raw, gl = p_raw[j, g]
-            bank = psum.tile([P, 512], F32, name="obank")
-            for u in range(2):
-                for i in range(2):
-                    words = raw[:, i, :].bitcast(F32)
-                    nc.tensor.transpose(bank[:, u * 256 + i * P : u * 256 + (i + 1) * P], words[:, 256 * gl + u : 256 * (gl + 1) : 2], ident[:])
-            dst = group_tile(p_group, j, g, "p_group", 3).bitcast(F32).rearrange("p (c u) -> p c u", u=2)
-            nc.scalar.copy(out=dst, in_=bank[:].rearrange("p (u c) -> p c u", u=2))
+        def p_turn(n):
+            bank = psum.tile([P, 512], F32, name="hbank", bufs=8)
+            for x in range(2):
+                r, g = divmod(2 * n + x, KD)
+                for u in range(2):
+                    nc.tensor.transpose(bank[:, u * 256 + x * P : u * 256 + (x + 1) * P], p_raw[r, g][u], ident[:])
+            if n % 3 == 0:
+                p_group[n // 3] = work.tile([P, 2 * D], BF16, name="p_group", align_bytes=64, bufs=3)
+            dst = p_group[n // 3][:].bitcast(F32)[:, (n % 3) * 512 : (n % 3 + 1) * 512]
+            nc.scalar.copy(out=dst.rearrange("p (c u) -> p c u", u=2), in_=bank[:].rearrange("p (u c) -> p c u", u=2))
 
-        def p_quant(j, part):
-            g0, g1 = PARTS[part]
-            quantise(p_codes[j][:, g0:g1, :], p_scales[j][:, g0:g1, :], p_group[j, g0][:])
+        def p_quant(r):
+            nc.vector.quantize_mx(out=p_codes[r][:].bitcast(FP8X4), scales=p_scales[r][:], in_=p_group[r // 2][:, (r % 2) * D : (r % 2 + 1) * D])
 
-        def project(s, j):
-            if j % 2 == 0:
-                tanh_out[s, j // 2] = work.tile([P, 4, SLAB], F32, name="th", bufs=4)
-            th = tanh_out[s, j // 2]
-            bank = psum.tile([P, 2, SLAB], F32, name="hbank", bufs=5)
-            for t2 in range(2):
-                for g in range(KD):
+        def project(s, r0, n, tag="hbank", g0=0, g1=KD):
+            w = width[s]
+            if g0 == 0:
+                h_bank[s, r0] = psum.tile([P, n, w], F32, name="hbank", bufs=8)
+            bank = h_bank[s, r0]
+            for x in range(n):
+                r = r0 + x
+                for g in range(g0, g1):
                     nc.tensor.matmul_mx(
-                        out=bank[:, t2, :],
-                        lhsT=p_codes[j][:, g, t2 * P : (t2 + 1) * P].bitcast(FP8X4),
-                        lhsT_scale=p_scales[j][:, g, t2 * P : (t2 + 1) * P],
-                        rhs=q_codes[s][:, g, :].bitcast(FP8X4),
-                        rhs_scale=q_scales[s][:, g, :],
-                        start=(g == 0),
-                        stop=(g == KD - 1),
+                        out=bank[:, x, :],
+                        lhsT=p_codes[r][:, g * P : (g + 1) * P].bitcast(FP8X4),
+                        lhsT_scale=p_scales[r][:, g * P : (g + 1) * P],
+                        rhs=q_codes[s][:, g * w : (g + 1) * w].bitcast(FP8X4),
+                        rhs_scale=q_scales[s][:, g * w : (g + 1) * w],
+                        start=(x == 0 and g == 0),
+                        stop=(x == n - 1 and g == KD - 1),
                     )
-            for t2 in range(2):
-                t = 2 * j + t2
-                nc.scalar.activation(out=th[:, t % 4, :], in_=bank[:, t2, :], func=ACT.Tanh, bias=off[:, t : t + 1])
+            for x in range(n if g1 == KD else 0):
+                r = r0 + x
+                if r % 4 == 0:
+                    tanh_out[s, r // 4] = work.tile([P, 4, w], F32, name="th", bufs=4)
+                nc.scalar.activation(out=tanh_out[s, r // 4][:, r % 4, :], in_=bank[:, x, :], func=ACT.Tanh, bias=off[:, r : r + 1])
 
-        def weight(s, gb):
-            if gb == 0:
-                z_group[s] = work.tile([P, KB, 4 * SLAB], BF16, name="z_group", align_bytes=64, bufs=2)
-            nc.vector.tensor_tensor(
-                out=z_group[s][:, gb, :].rearrange("p (c i t) -> p c t i", i=WALK, t=4),
-                in0=tanh_out[s, gb][:].rearrange("p t (c i) -> p c t i", i=WALK),
-                in1=gain[:, gb * 4 : gb * 4 + 4].rearrange("p (o t i) -> p o t i", o=1, i=1).to_broadcast([P, SLAB // WALK, 4, WALK]),
+        def weight(s, gb, engine, c0=0, c1=None):
+            w = width[s]
+            c1 = w if c1 is None else c1
+            if c0 == 0:
+                z_group[s, gb] = work.tile([P, 4 * w], BF16, name="z_group", align_bytes=64, bufs=4)
+            engine.tensor_tensor(
+                out=z_group[s, gb][:, 4 * c0 : 4 * c1].rearrange("p (c i t) -> p c t i", i=WALK, t=4),
+                in0=tanh_out[s, gb][:, :, c0:c1].rearrange("p t (c i) -> p c t i", i=WALK),
+                in1=gain[:, gb * 4 : gb * 4 + 4].rearrange("p (o t i) -> p o t i", o=1, i=1).to_broadcast([P, (c1 - c0) // WALK, 4, WALK]),
                 op=MULT,
             )
 
-        def z_quant(s, gb):
-            quantise(z_codes[s][:, gb : gb + 1, :], z_scales[s][:, gb : gb + 1, :], z_group[s][:, gb : gb + 1, :])
+        def z_quant(s, gb, c0=0, c1=None):
+            w = width[s]
+            c1 = w if c1 is None else c1
+            cols = slice(gb * w + c0, gb * w + c1)
+            nc.vector.quantize_mx(out=z_codes[s][:, cols].bitcast(FP8X4), scales=z_scales[s][:, cols], in_=z_group[s, gb][:, 4 * c0 : 4 * c1])
 
-        def score(b, half, engines="ss", single=False):
-            s, cols = b // 2, slice((b % 2) * P, (b % 2 + 1) * P)
-            ot = work.tile([P, 2, NB], F32, name="ot", bufs=6)
-            for e in range(len(engines)):
-                d = half * 2 + e
-                bank = psum.tile([P, NB], F32, name="obank")
-                for gb in range(KB):
-                    nc.tensor.matmul_mx(
-                        out=bank[:],
-                        lhsT=z_codes[s][:, gb, cols].bitcast(FP8X4),
-                        lhsT_scale=z_scales[s][:, gb, cols],
-                        rhs=c_codes[:, gb, d * 2 * NB : (d + 1) * 2 * NB].bitcast(FP4X4),
-                        rhs_scale=c_scales[:, gb, d * NB : (d + 1) * NB],
-                        start=(gb == 0),
-                        stop=(gb == KB - 1),
-                    )
-                if engines[e] == "s":
-                    nc.scalar.copy(out=ot[:, e, :], in_=bank[:])
-                else:
-                    nc.vector.tensor_copy(out=ot[:, e, :], in_=bank[:])
-                if single:
-                    nc.sync.dma_start(out=out_view[s, b % 2][:, d * NB : (d + 1) * NB], in_=ot[:, e, :])
-            if not single:
-                nc.sync.dma_start(out=out_view[s, b % 2][:, half * 1024 : (half + 1) * 1024], in_=ot[:].rearrange("p e n -> p (e n)"))
+        def score_part(s, i, n0, n, engine):
+            w = width[s]
+            b = UNITS[s][i]
+            part = work.tile([P, n], F32, name="ot_part", bufs=4)
+            bank = psum.tile([P, n], F32, name="hbank", bufs=8)
+            for gb in range(KB):
+                cols = slice(gb * w + i * P, gb * w + (i + 1) * P)
+                nc.tensor.matmul_mx(
+                    out=bank[:],
+                    lhsT=z_codes[s][:, cols].bitcast(FP8X4),
+                    lhsT_scale=z_scales[s][:, cols],
+                    rhs=c_codes[:, gb, 2 * n0 : 2 * (n0 + n)].bitcast(FP4X4),
+                    rhs_scale=c_scales[:, gb, n0 : n0 + n],
+                    start=(gb == 0),
+                    stop=(gb == KB - 1),
+                )
+            if engine == "s":
+                nc.scalar.copy(out=part[:], in_=bank[:])
+            else:
+                nc.vector.tensor_copy(out=part[:], in_=bank[:])
+            nc.sync.dma_start(out=out_view[b // 2, b % 2][:, n0 : n0 + n], in_=part[:])
 
-        def score_last(b):
-            s, cols = b // 2, slice((b % 2) * P, (b % 2 + 1) * P)
-            for e in range(2):
-                bank = psum.tile([P, 2, P], F32, name="obank")
-                n0 = DOCS - NB + e * 2 * P
-                for c in range(2):
-                    for gb in range(KB):
-                        nc.tensor.matmul_mx(
-                            out=bank[:, c, :],
-                            lhsT=z_codes[s][:, gb, cols].bitcast(FP8X4),
-                            lhsT_scale=z_scales[s][:, gb, cols],
-                            rhs=c_codes[:, gb, 2 * (n0 + c * P) : 2 * (n0 + (c + 1) * P)].bitcast(FP4X4),
-                            rhs_scale=c_scales[:, gb, n0 + c * P : n0 + (c + 1) * P],
-                            start=(gb == 0),
-                            stop=(gb == KB - 1),
-                        )
-                ot = work.tile([P, 2 * P], F32, name="ot_last", bufs=2)
-                if e == 0:
-                    nc.vector.tensor_copy(out=ot[:], in_=bank[:].rearrange("p c n -> p (c n)"))
-                else:
-                    nc.scalar.copy(out=ot[:], in_=bank[:].rearrange("p c n -> p (c n)"))
-                nc.sync.dma_start(out=out_view[s, b % 2][:, n0 : n0 + 2 * P], in_=ot[:])
+        def score(s, i, d, engine, run):
+            w = width[s]
+            b = UNITS[s][i]
+            if d % run == 0:
+                o_tile[b] = work.tile([P, run, NB], F32, name="ot%d" % run, bufs={1: 4, 2: 5, 4: 2}[run])
+            bank = psum.tile([P, NB], F32, name="hbank", bufs=8)
+            for gb in range(KB):
+                cols = slice(gb * w + i * P, gb * w + (i + 1) * P)
+                nc.tensor.matmul_mx(
+                    out=bank[:],
+                    lhsT=z_codes[s][:, cols].bitcast(FP8X4),
+                    lhsT_scale=z_scales[s][:, cols],
+                    rhs=c_codes[:, gb, d * 2 * NB : (d + 1) * 2 * NB].bitcast(FP4X4),
+                    rhs_scale=c_scales[:, gb, d * NB : (d + 1) * NB],
+                    start=(gb == 0),
+                    stop=(gb == KB - 1),
+                )
+            if engine == "s":
+                nc.scalar.copy(out=o_tile[b][:, d % run, :], in_=bank[:])
+            else:
+                nc.vector.tensor_copy(out=o_tile[b][:, d % run, :], in_=bank[:])
+            if d % run == run - 1:
+                nc.sync.dma_start(out=out_view[b // 2, b % 2][:, (d + 1 - run) * NB : (d + 1) * NB], in_=o_tile[b][:].rearrange("p e n -> p (e n)"))
+
+        def scores(s, i, engines="ssss", run=2):
+            for d in range(ND):
+                score(s, i, d, engines[d], run)
 
         def load_vec(dst, src):
             nc.sync.dma_start(out=dst[:].rearrange("p (g t) -> p g t", t=4), in_=src.rearrange("(g p t) -> p g t", p=P, t=4))
@@ -266,90 +283,119 @@ def tile_soft_hyperplane_hashing_s13_kernel(tc, planes, queries_bytes, queries_s
             nc.vector.memset(ones[:], 1.0)
             nc.scalar.activation(out=warm[:], in_=ones[:], func=ACT.Tanh)
             make_identity(nc, ident[:])
-            nc.gpsimd.memset(c_scales[:].rearrange("p g n -> p (g n)").bitcast(U32), 0)
+            nc.vector.memset(c_scales[:].rearrange("p g n -> p (g n)").bitcast(U32), 0)
 
-        def planes_in(j):
-            for g in range(KD):
-                p_transpose(j, g)
-
-        def planes_quant(j):
-            for part in range(2):
-                p_quant(j, part)
-
+        V, G = nc.vector, nc.gpsimd
         with tc.manual_schedule():
             load_q(0, 1)
             setup()
-            load_q(1, 1)
             load_q(2, 1)
+            load_q(1, 1)
+            load_p(0, 1, 0, 2)
             load_q(3, 1)
-            load_p(0, 0, 1)
-            load_p(0, 1, 3)
-            load_p(1, 0, 3)
-            load_p(2, 0, 3)
-            load_p(3, 0, 3)
+            load_p(0, 1, 2, 3)
+            load_p(1, 1)
+            load_p(2, 1)
+            load_p(3, 1)
+            load_p(4, 2)
+            load_p(6, 1)
+            load_p(7, 1)
             load_vec(off, offset)
-            load_vec(gain, bit_gain)
             load_q(4, 2)
+            load_vec(gain, bit_gain)
             load_c()
             load_q(6, 2)
-            dummy(6)
+            warm_up(6)
             cast(0)
-            cast(1, 0, 1)
-            cast(1, 1, 3)
             cast_plain(2)
+            cast(1)
             cast_plain(3)
-            q_transpose(0, blocks=(0,))
-            q_transpose(0, blocks=(1,))
-            p_transpose(0, 0)
-            q_exit(0, 0)
-            q_transpose(1, blocks=(0,))
-            p_transpose(0, 1)
-            p_transpose(0, 2)
-            q_transpose(1, blocks=(1,))
-            q_exit(0, 1)
-            q_exit(0, 2)
-            planes_in(1)
-            q_quant(0, 0)
-            q_quant(0, 1)
-            planes_quant(0)
-            planes_in(2)
-            q_exit(1, 0)
-            planes_quant(1)
-            planes_in(3)
-            q_exit(1, 1)
-            planes_quant(2)
-            project(0, 0)
-            project(0, 1)
-            project(0, 2)
-            q_exit(1, 2)
-            planes_quant(3)
-            project(0, 3)
-            q_quant(1, 0)
-            q_quant(1, 1)
-            for s in range(1, NS):
-                more = s + 1 < NS
-                if more:
-                    cast_slab(s + 1)
-                for j in range(4):
-                    project(s, j)
-                weight(s - 1, 0)
-                weight(s - 1, 1)
-                z_quant(s - 1, 0)
-                z_quant(s - 1, 1)
-                if more:
-                    q_transpose(s + 1)
-                    for g in range(KD):
-                        q_exit(s + 1, g)
-                    q_quant(s + 1, 0)
-                    q_quant(s + 1, 1)
-                else:
-                    weight(s, 0)
-                    weight(s, 1)
-                    z_quant(s, 0)
-                    z_quant(s, 1)
-                for i in range(2):
-                    for half in range(2):
-                        score(2 * s - 2 + i, half, "ss" if more or i == 0 else "sv")
-            for i in range(2):
-                for half in range(2):
-                    score(6 + i, half, "sv", i == 1)
+            q_turn(0, 0)
+            p_turn(0)
+            q_turn(0, 1)
+            q_turn(0, 2)
+            p_turn(1)
+            p_turn(2)
+            for n in range(3):
+                q_exit(0, n)
+            q_turn(1, 0)
+            p_turn(3)
+            q_turn(1, 1)
+            p_turn(4)
+            q_turn(1, 2)
+            p_turn(5)
+            for n in range(3):
+                q_exit(1, n)
+            for n in range(6, 9):
+                p_turn(n)
+            q_quant(0, 0, 2)
+            p_quant(0)
+            q_quant(0, 2, 3)
+            for r in range(1, 4):
+                p_quant(r)
+            for n in range(9, 12):
+                p_turn(n)
+            for r in range(4, 8):
+                p_quant(r)
+            q_quant(1, 0, 2)
+            q_quant(1, 2, 3)
+            for r in range(0, 8, 2):
+                project(0, r, 2)
+
+            for r in range(0, 8, 2):
+                project(1, r, 2)
+            cast(4)
+            cast(5)
+            weight(0, 0, V)
+            weight(0, 1, V)
+            z_quant(0, 0)
+            z_quant(0, 1)
+            for n in range(3):
+                q_turn(2, n)
+            for n in range(3):
+                q_exit(2, n)
+            q_quant(2, 0, 2)
+            q_quant(2, 2, 3)
+            scores(0, 0)
+            scores(0, 1)
+            weight(1, 0, V)
+            cast(6)
+            cast(7)
+            weight(1, 1, V)
+            z_quant(1, 0)
+            z_quant(1, 1)
+            for r in range(0, 8, 2):
+                project(2, r, 2)
+            for n in range(3):
+                q_turn(3, n)
+            for n in range(3):
+                q_exit(3, n)
+            q_quant(3, 0, 2)
+            q_quant(3, 2, 3)
+            scores(1, 0)
+            score(1, 1, 0, "s", 2)
+            score(1, 1, 1, "s", 2)
+            score(1, 1, 2, "s", 2)
+            weight(2, 0, V)
+            weight(2, 1, V)
+            z_quant(2, 0)
+            z_quant(2, 1)
+            project(3, 0, 2)
+            project(3, 2, 2)
+            score(1, 1, 3, "s", 2)
+            project(3, 4, 2)
+            weight(3, 0, V)
+            score(2, 0, 0, "s", 2)
+            score(2, 0, 1, "s", 2)
+            project(3, 6, 2)
+            z_quant(3, 0)
+            score(2, 0, 2, "v", 2)
+            score(2, 0, 3, "s", 2)
+            weight(3, 1, V)
+            z_quant(3, 1)
+            scores(2, 1, "ssss")
+            scores(3, 0, "vsvs")
+            score(3, 1, 0, "v", 2)
+            score(3, 1, 1, "s", 2)
+            score(3, 1, 2, "v", 1)
+            score(3, 1, 3, "s", 1)

@@ -57,6 +57,8 @@ def tile_soft_hyperplane_hashing_s13_kernel(tc, planes, queries_bytes, queries_s
         out_view = out.rearrange("(s p i) d -> s i p d", p=P, i=2)
 
         q_bytes = {}
+        q_load = {}
+        q_single = {}
         p_raw = {}
         p_rows = {}
         q_cast = {}
@@ -69,11 +71,13 @@ def tile_soft_hyperplane_hashing_s13_kernel(tc, planes, queries_bytes, queries_s
         z_group = {}
         o_tile = {}
 
-        def load_q(b, n):
-            raw = keep.tile([P, n, D], U8, name="q_bytes%d" % b)
-            nc.sync.dma_start(out=raw[:], in_=q_view[b // 2][:, b % 2 : b % 2 + n, :])
-            for i in range(n):
-                q_bytes[b + i] = raw[:, i, :]
+        def load_q(b, n, g0=0, g1=KD):
+            raw = keep.tile([P, n * (g1 - g0) * 512], U8, name="q_bytes%d%d" % (b, g0))
+            nc.sync.dma_start(out=raw[:].rearrange("p (n k) -> p n k", n=n), in_=q_view[b // 2][:, b % 2 : b % 2 + n, g0 * 512 : g1 * 512])
+            q_load[b, g0] = (raw, n, g1)
+            if g1 - g0 == KD:
+                for i in range(n):
+                    q_bytes[b + i] = raw[:, i * D : (i + 1) * D]
 
         def load_p(r, n, g0=0, g1=KD):
             raw = keep.tile([P, n * (g1 - g0) * 512], BF16, name="p_raw%d%d" % (r, g0))
@@ -85,18 +89,11 @@ def tile_soft_hyperplane_hashing_s13_kernel(tc, planes, queries_bytes, queries_s
                     w0 = (i * (g1 - g0) + g - g0) * 256
                     p_raw[r + i, g] = [raw[:].bitcast(F32)[:, w0 + u : w0 + 256 : 2] for u in range(2)]
 
-        def sort_p(r, engine):
-            wide = work.tile([P, 2, KD * P, 2], BF16, name="p_sorted", bufs=4)
-            engine.tensor_scalar(
-                out=wide[:],
-                in0=p_rows[r].rearrange("p (w u e) -> p u w e", u=2, e=2),
-                scalar1=1.0,
-                scalar2=0.0,
-                op0=MULT,
-                op1=ADD,
-            )
+        def sort_p(r):
+            wide = work.tile([P, 2, KD * P], F32, name="p_sorted", bufs=3)
+            nc.scalar.copy(out=wide[:], in_=p_rows[r].bitcast(F32).rearrange("p (w u) -> p u w", u=2))
             for g in range(KD):
-                p_raw[r, g] = [wide[:, u, :, :].rearrange("p w e -> p (w e)").bitcast(F32)[:, g * P : (g + 1) * P] for u in range(2)]
+                p_raw[r, g] = [wide[:, u, g * P : (g + 1) * P] for u in range(2)]
 
         def warm_up(n):
             bank = psum.tile([P, 512], F32, name="hbank", bufs=8)
@@ -113,6 +110,8 @@ def tile_soft_hyperplane_hashing_s13_kernel(tc, planes, queries_bytes, queries_s
                 op0=MULT,
             )
             for g in range(KD):
+                q_single[b, g] = [wide[:, t // 2, g * P : (g + 1) * P, t % 2] for t in range(4)]
+            for g in range(KD):
                 q_cast[b, g] = [wide[:, u, :, :].rearrange("p w e -> p (w e)").bitcast(F32)[:, g * P : (g + 1) * P] for u in range(2)]
 
         def cast_plain(b):
@@ -122,7 +121,7 @@ def tile_soft_hyperplane_hashing_s13_kernel(tc, planes, queries_bytes, queries_s
                 q_cast[b, g] = [wide[:].bitcast(F32)[:, 256 * g + u : 256 * (g + 1) : 2] for u in range(2)]
 
         def q_parts(s):
-            if s == 0:
+            if s == 0 and len(UNITS[s]) == 2:
                 return [[(0, 0), (1, 0)], [(0, 1), (1, 1)], [(2, 0), (2, 1)]]
             if len(UNITS[s]) == 2:
                 return [[(g, 0), (g, 1)] for g in range(KD)]
@@ -161,8 +160,10 @@ def tile_soft_hyperplane_hashing_s13_kernel(tc, planes, queries_bytes, queries_s
         def q_quant(s, g0, g1):
             quantise(q_codes[s], q_scales[s], q_group[s], g0 * width[s], g1 * width[s])
 
-        def p_turn(n):
+        def p_turn(n, keep_warm=False):
             bank = psum.tile([P, 512], F32, name="hbank", bufs=8)
+            if keep_warm:
+                nc.tensor.matmul(bank[:], lhsT=zeros[:, 0:P], rhs=zeros[:], start=True, stop=True)
             for x in range(2):
                 r, g = divmod(2 * n + x, KD)
                 for u in range(2):
@@ -216,33 +217,11 @@ def tile_soft_hyperplane_hashing_s13_kernel(tc, planes, queries_bytes, queries_s
             cols = slice(gb * w + c0, gb * w + c1)
             nc.vector.quantize_mx(out=z_codes[s][:, cols].bitcast(FP8X4), scales=z_scales[s][:, cols], in_=z_group[s, gb][:, 4 * c0 : 4 * c1])
 
-        def score_part(s, i, n0, n, engine):
-            w = width[s]
-            b = UNITS[s][i]
-            part = work.tile([P, n], F32, name="ot_part", bufs=4)
-            bank = psum.tile([P, n], F32, name="hbank", bufs=8)
-            for gb in range(KB):
-                cols = slice(gb * w + i * P, gb * w + (i + 1) * P)
-                nc.tensor.matmul_mx(
-                    out=bank[:],
-                    lhsT=z_codes[s][:, cols].bitcast(FP8X4),
-                    lhsT_scale=z_scales[s][:, cols],
-                    rhs=c_codes[:, gb, 2 * n0 : 2 * (n0 + n)].bitcast(FP4X4),
-                    rhs_scale=c_scales[:, gb, n0 : n0 + n],
-                    start=(gb == 0),
-                    stop=(gb == KB - 1),
-                )
-            if engine == "s":
-                nc.scalar.copy(out=part[:], in_=bank[:])
-            else:
-                nc.vector.tensor_copy(out=part[:], in_=bank[:])
-            nc.sync.dma_start(out=out_view[b // 2, b % 2][:, n0 : n0 + n], in_=part[:])
-
-        def score(s, i, d, engine, run):
+        def score(s, i, d, engine, run, own_queue=False):
             w = width[s]
             b = UNITS[s][i]
             if d % run == 0:
-                o_tile[b] = work.tile([P, run, NB], F32, name="ot%d" % run, bufs={1: 4, 2: 5, 4: 2}[run])
+                o_tile[b] = work.tile([P, run, NB], F32, name="ot%d" % run, bufs={1: 8, 2: 5, 4: 2}[run])
             bank = psum.tile([P, NB], F32, name="hbank", bufs=8)
             for gb in range(KB):
                 cols = slice(gb * w + i * P, gb * w + (i + 1) * P)
@@ -260,7 +239,8 @@ def tile_soft_hyperplane_hashing_s13_kernel(tc, planes, queries_bytes, queries_s
             else:
                 nc.vector.tensor_copy(out=o_tile[b][:, d % run, :], in_=bank[:])
             if d % run == run - 1:
-                nc.sync.dma_start(out=out_view[b // 2, b % 2][:, (d + 1 - run) * NB : (d + 1) * NB], in_=o_tile[b][:].rearrange("p e n -> p (e n)"))
+                queue = nc.scalar if own_queue else nc.sync
+                queue.dma_start(out=out_view[b // 2, b % 2][:, (d + 1 - run) * NB : (d + 1) * NB], in_=o_tile[b][:].rearrange("p e n -> p (e n)"))
 
         def scores(s, i, engines="ssss", run=2):
             for d in range(ND):
@@ -277,8 +257,10 @@ def tile_soft_hyperplane_hashing_s13_kernel(tc, planes, queries_bytes, queries_s
                     in_=codes_scales.rearrange("g q n -> q g n")[4 * qd : 4 * qd + 4].bitcast(I32),
                 )
 
+        def load_scale(queue):
+            queue.dma_start(out=q_scale[:].rearrange("p (g t) -> p g t", t=4), in_=queries_scale.rearrange("o (g p t) -> p (o g) t", p=P, t=4))
+
         def setup():
-            nc.scalar.dma_start(out=q_scale[:].rearrange("p (g t) -> p g t", t=4), in_=queries_scale.rearrange("o (g p t) -> p (o g) t", p=P, t=4))
             nc.vector.memset(zeros[:], 0.0)
             nc.vector.memset(ones[:], 1.0)
             nc.scalar.activation(out=warm[:], in_=ones[:], func=ACT.Tanh)
@@ -289,64 +271,68 @@ def tile_soft_hyperplane_hashing_s13_kernel(tc, planes, queries_bytes, queries_s
         with tc.manual_schedule():
             load_q(0, 1)
             setup()
-            load_q(2, 1)
             load_q(1, 1)
-            load_p(0, 1, 0, 2)
+            load_q(2, 1)
             load_q(3, 1)
+            load_scale(nc.sync)
+            load_p(0, 1, 0, 2)
             load_p(0, 1, 2, 3)
-            load_p(1, 1)
-            load_p(2, 1)
-            load_p(3, 1)
-            load_p(4, 2)
-            load_p(6, 1)
-            load_p(7, 1)
+            for r in (1, 2, 3, 4, 5, 7, 6):
+                load_p(r, 1)
             load_vec(off, offset)
             load_q(4, 2)
             load_vec(gain, bit_gain)
             load_c()
             load_q(6, 2)
-            warm_up(6)
+            warm_up(7)
             cast(0)
-            cast_plain(2)
             cast(1)
-            cast_plain(3)
-            q_turn(0, 0)
+            cast_plain(2)
+            cast(3)
+            for n in range(3):
+                q_turn(0, n)
             p_turn(0)
-            q_turn(0, 1)
-            q_turn(0, 2)
+            q_turn(1, 0)
             p_turn(1)
             p_turn(2)
             for n in range(3):
                 q_exit(0, n)
-            q_turn(1, 0)
-            p_turn(3)
             q_turn(1, 1)
+            p_turn(3)
             p_turn(4)
+            q_exit(1, 0)
             q_turn(1, 2)
             p_turn(5)
-            for n in range(3):
-                q_exit(1, n)
-            for n in range(6, 9):
-                p_turn(n)
-            q_quant(0, 0, 2)
             p_quant(0)
+            q_quant(0, 0, 2)
+            q_exit(1, 1)
             q_quant(0, 2, 3)
-            for r in range(1, 4):
-                p_quant(r)
+            p_quant(1)
+            p_turn(6)
+            sort_p(7)
+            p_turn(7)
+            p_turn(8)
+            q_exit(1, 2)
+            project(0, 0, 2)
+            p_quant(2)
+            p_quant(3)
+            q_quant(1, 0, 2)
             for n in range(9, 12):
                 p_turn(n)
-            for r in range(4, 8):
-                p_quant(r)
-            q_quant(1, 0, 2)
+            p_quant(4)
             q_quant(1, 2, 3)
-            for r in range(0, 8, 2):
-                project(0, r, 2)
-
-            for r in range(0, 8, 2):
-                project(1, r, 2)
+            p_quant(5)
             cast(4)
-            cast(5)
+            p_quant(6)
+            p_quant(7)
+            project(0, 2, 2)
+            project(1, 0, 2)
+            project(0, 4, 2)
+            project(0, 6, 2)
+            for r in range(2, 8, 2):
+                project(1, r, 2)
             weight(0, 0, V)
+            cast(5)
             weight(0, 1, V)
             z_quant(0, 0)
             z_quant(0, 1)
@@ -397,5 +383,5 @@ def tile_soft_hyperplane_hashing_s13_kernel(tc, planes, queries_bytes, queries_s
             scores(3, 0, "vsvs")
             score(3, 1, 0, "v", 2)
             score(3, 1, 1, "s", 2)
-            score(3, 1, 2, "v", 1)
-            score(3, 1, 3, "s", 1)
+            score(3, 1, 2, "v", 2)
+            score(3, 1, 3, "s", 2)

@@ -203,11 +203,12 @@ def tile_soft_hyperplane_hashing_s13_kernel(tc, planes, queries_bytes, queries_s
             w = width[s]
             c1 = w if c1 is None else c1
             if c0 == 0:
-                z_group[s, gb] = work.tile([P, 4 * w], BF16, name="z_group", align_bytes=64, bufs=4)
+                z_group[s, gb] = work.tile([P, 4 * w], BF16, name="z_group", align_bytes=64, bufs=2)
+            walk = WALK if engine is V else 1
             engine.tensor_tensor(
-                out=z_group[s, gb][:, 4 * c0 : 4 * c1].rearrange("p (c i t) -> p c t i", i=WALK, t=4),
-                in0=tanh_out[s, gb][:, :, c0:c1].rearrange("p t (c i) -> p c t i", i=WALK),
-                in1=gain[:, gb * 4 : gb * 4 + 4].rearrange("p (o t i) -> p o t i", o=1, i=1).to_broadcast([P, (c1 - c0) // WALK, 4, WALK]),
+                out=z_group[s, gb][:, 4 * c0 : 4 * c1].rearrange("p (c i t) -> p c t i", i=walk, t=4),
+                in0=tanh_out[s, gb][:, :, c0:c1].rearrange("p t (c i) -> p c t i", i=walk),
+                in1=gain[:, gb * 4 : gb * 4 + 4].rearrange("p (o t i) -> p o t i", o=1, i=1).to_broadcast([P, (c1 - c0) // walk, 4, walk]),
                 op=MULT,
             )
 
@@ -336,6 +337,7 @@ def tile_soft_hyperplane_hashing_s13_kernel(tc, planes, queries_bytes, queries_s
             weight(0, 1, V)
             z_quant(0, 0)
             z_quant(0, 1)
+            weight(1, 0, G)
             for n in range(3):
                 q_turn(2, n)
             for n in range(3):
@@ -344,7 +346,6 @@ def tile_soft_hyperplane_hashing_s13_kernel(tc, planes, queries_bytes, queries_s
             q_quant(2, 2, 3)
             scores(0, 0)
             scores(0, 1)
-            weight(1, 0, V)
             cast(6)
             cast(7)
             weight(1, 1, V)
@@ -352,6 +353,7 @@ def tile_soft_hyperplane_hashing_s13_kernel(tc, planes, queries_bytes, queries_s
             z_quant(1, 1)
             for r in range(0, 8, 2):
                 project(2, r, 2)
+            weight(2, 0, G)
             for n in range(3):
                 q_turn(3, n)
             for n in range(3):
@@ -362,7 +364,6 @@ def tile_soft_hyperplane_hashing_s13_kernel(tc, planes, queries_bytes, queries_s
             score(1, 1, 0, "s", 2)
             score(1, 1, 1, "s", 2)
             score(1, 1, 2, "s", 2)
-            weight(2, 0, V)
             weight(2, 1, V)
             z_quant(2, 0)
             z_quant(2, 1)

@@ -114,9 +114,12 @@ def tile_soft_hyperplane_hashing_s13_kernel(tc, planes, queries_bytes, queries_s
             for g in range(KD):
                 q_cast[b, g] = [wide[:, u, :, :].rearrange("p w e -> p (w e)").bitcast(F32)[:, g * P : (g + 1) * P] for u in range(2)]
 
-        def cast_plain(b):
-            wide = work.tile([P, D], BF16, name="q_plain", bufs=2)
-            nc.scalar.copy(out=wide[:], in_=q_bytes[b].bitcast(FP8))
+        def cast_plain(b, engine="s"):
+            wide = work.tile([P, D], BF16, name="q_plain", bufs=3)
+            if engine == "s":
+                nc.scalar.copy(out=wide[:], in_=q_bytes[b].bitcast(FP8))
+            else:
+                nc.vector.tensor_copy(out=wide[:], in_=q_bytes[b].bitcast(FP8))
             for g in range(KD):
                 q_cast[b, g] = [wide[:].bitcast(F32)[:, 256 * g + u : 256 * (g + 1) : 2] for u in range(2)]
 
@@ -272,13 +275,12 @@ def tile_soft_hyperplane_hashing_s13_kernel(tc, planes, queries_bytes, queries_s
         with tc.manual_schedule():
             load_q(0, 1)
             setup()
-            load_q(1, 1)
-            load_q(2, 1)
-            load_q(3, 1)
+            for b in range(1, 4):
+                load_q(b, 1)
             load_scale(nc.sync)
             load_p(0, 1, 0, 2)
             load_p(0, 1, 2, 3)
-            for r in (1, 2, 3, 4, 5, 7, 6):
+            for r in range(1, 8):
                 load_p(r, 1)
             load_vec(off, offset)
             load_q(4, 2)
@@ -290,48 +292,49 @@ def tile_soft_hyperplane_hashing_s13_kernel(tc, planes, queries_bytes, queries_s
             cast(1)
             cast_plain(2)
             cast(3)
-            for n in range(3):
-                q_turn(0, n)
+            q_turn(0, 0)
+            q_turn(0, 2)
+            q_turn(0, 1)
             p_turn(0)
             q_turn(1, 0)
-            p_turn(1)
-            p_turn(2)
-            for n in range(3):
-                q_exit(0, n)
+            q_exit(0, 0)
+            q_exit(0, 2)
+            q_exit(0, 1)
+            for n in range(1, 4):
+                p_turn(n)
             q_turn(1, 1)
-            p_turn(3)
-            p_turn(4)
             q_exit(1, 0)
-            q_turn(1, 2)
-            p_turn(5)
-            p_quant(0)
+            for n in range(4, 7):
+                p_turn(n)
             q_quant(0, 0, 2)
-            q_exit(1, 1)
+            p_quant(0)
             q_quant(0, 2, 3)
             p_quant(1)
-            p_turn(6)
-            sort_p(7)
+            q_exit(1, 1)
+            sort_p(6)
+            q_turn(1, 2)
             p_turn(7)
+            sort_p(7)
             p_turn(8)
-            q_exit(1, 2)
             project(0, 0, 2)
             p_quant(2)
             p_quant(3)
+            q_exit(1, 2)
+            p_quant(4)
+            p_quant(5)
             q_quant(1, 0, 2)
+            q_quant(1, 2, 3)
             for n in range(9, 12):
                 p_turn(n)
-            p_quant(4)
-            q_quant(1, 2, 3)
-            p_quant(5)
-            cast(4)
             p_quant(6)
             p_quant(7)
             project(0, 2, 2)
-            project(1, 0, 2)
             project(0, 4, 2)
+            project(1, 0, 2)
             project(0, 6, 2)
             for r in range(2, 8, 2):
                 project(1, r, 2)
+            cast(4)
             weight(0, 0, V)
             cast(5)
             weight(0, 1, V)
@@ -351,7 +354,7 @@ def tile_soft_hyperplane_hashing_s13_kernel(tc, planes, queries_bytes, queries_s
             weight(1, 1, V)
             z_quant(1, 0)
             z_quant(1, 1)
-            for r in range(0, 8, 2):
+            for r in range(0, 6, 2):
                 project(2, r, 2)
             weight(2, 0, G)
             for n in range(3):
@@ -361,19 +364,17 @@ def tile_soft_hyperplane_hashing_s13_kernel(tc, planes, queries_bytes, queries_s
             q_quant(3, 0, 2)
             q_quant(3, 2, 3)
             scores(1, 0)
-            score(1, 1, 0, "s", 2)
-            score(1, 1, 1, "s", 2)
-            score(1, 1, 2, "s", 2)
+            project(2, 6, 2)
+            scores(1, 1)
             weight(2, 1, V)
             z_quant(2, 0)
             z_quant(2, 1)
             project(3, 0, 2)
             project(3, 2, 2)
-            score(1, 1, 3, "s", 2)
-            project(3, 4, 2)
+            score(2, 0, 0, "v", 2)
+            score(2, 0, 1, "v", 2)
             weight(3, 0, V)
-            score(2, 0, 0, "s", 2)
-            score(2, 0, 1, "s", 2)
+            project(3, 4, 2)
             project(3, 6, 2)
             z_quant(3, 0)
             score(2, 0, 2, "v", 2)
@@ -382,7 +383,4 @@ def tile_soft_hyperplane_hashing_s13_kernel(tc, planes, queries_bytes, queries_s
             z_quant(3, 1)
             scores(2, 1, "ssss")
             scores(3, 0, "vsvs")
-            score(3, 1, 0, "v", 2)
-            score(3, 1, 1, "s", 2)
-            score(3, 1, 2, "v", 2)
-            score(3, 1, 3, "s", 2)
+            scores(3, 1, "vsvs")

@@ -246,9 +246,9 @@ def tile_soft_hyperplane_hashing_s13_kernel(tc, planes, queries_bytes, queries_s
                 queue = nc.scalar if own_queue else nc.sync
                 queue.dma_start(out=out_view[b // 2, b % 2][:, (d + 1 - run) * NB : (d + 1) * NB], in_=o_tile[b][:].rearrange("p e n -> p (e n)"))
 
-        def scores(s, i, engines="ssss", run=2):
+        def scores(s, i, engines="ssss", run=2, two_queues=False):
             for d in range(ND):
-                score(s, i, d, engines[d], run)
+                score(s, i, d, engines[d], run, two_queues and d == 1)
 
         def load_vec(dst, src):
             nc.sync.dma_start(out=dst[:].rearrange("p (g t) -> p g t", t=4), in_=src.rearrange("(g p t) -> p g t", p=P, t=4))
@@ -381,6 +381,6 @@ def tile_soft_hyperplane_hashing_s13_kernel(tc, planes, queries_bytes, queries_s
             score(2, 0, 3, "s", 2)
             weight(3, 1, V)
             z_quant(3, 1)
-            scores(2, 1, "ssss")
-            scores(3, 0, "vsvs")
-            scores(3, 1, "vsvs")
+            scores(2, 1, "ssss", 2, True)
+            scores(3, 0, "vsvs", 2, True)
+            scores(3, 1, "vsvs", 2, True)

@@ -381,6 +381,6 @@ def tile_soft_hyperplane_hashing_s13_kernel(tc, planes, queries_bytes, queries_s
             score(2, 0, 3, "s", 2)
             weight(3, 1, V)
             z_quant(3, 1)
-            scores(2, 1, "ssss", 2, True)
+            scores(2, 1, "ssvs", 2, True)
             scores(3, 0, "vsvs", 2, True)
             scores(3, 1, "vsvs", 2, True)

@@ -25,30 +25,32 @@ NB = 512
 ND = DOCS // NB
 WALK = 2
 NT = BITS // P
-UNITS = ((0, 1), (2, 3), (4, 5), (6, 7))
+NS = Q // (2 * P)
+W = 2 * P
 
 
 def tile_soft_hyperplane_hashing_s13_kernel(tc, planes, queries_bytes, queries_scale, offset, bit_gain, codes_words, codes_scales, out):
     nc = tc.nc
+    V, S, G = nc.vector, nc.scalar, nc.gpsimd
     with ExitStack() as ctx:
         keep = ctx.enter_context(tc.tile_pool(name="keep", bufs=1))
         work = ctx.enter_context(tc.tile_pool(name="work", bufs=3))
-        psum = ctx.enter_context(tc.psum_pool(name="psum", bufs=4))
+        psum = ctx.enter_context(tc.psum_pool(name="psum", bufs=8))
 
         ident = keep.tile([P, P], F32, name="ident")
         zeros = keep.tile([P, 512], BF16, name="zeros")
         ones = keep.tile([P, 1], F32, name="ones")
         warm = keep.tile([P, 1], F32, name="warm")
         q_scale = keep.tile([P, KD * 4], F32, name="q_scale")
+        spread = [keep.tile([P, 512], F32, name="spread%d" % g) for g in range(KD)]
         off = keep.tile([P, KB * 4], BF16, name="off")
         gain = keep.tile([P, KB * 4], BF16, name="gain")
-        width = [P * len(blocks) for blocks in UNITS]
         p_codes = [keep.tile([P, KD * P], U32, name="p_codes%d" % r, align_bytes=64) for r in range(NT)]
         p_scales = [keep.tile([P, KD * P], U8, name="p_scales%d" % r, align_bytes=64) for r in range(NT)]
-        q_codes = [keep.tile([P, KD * w], U32, name="q_codes%d" % s, align_bytes=64) for s, w in enumerate(width)]
-        q_scales = [keep.tile([P, KD * w], U8, name="q_scales%d" % s, align_bytes=64) for s, w in enumerate(width)]
-        z_codes = [keep.tile([P, KB * w], U32, name="z_codes%d" % s, align_bytes=64) for s, w in enumerate(width)]
-        z_scales = [keep.tile([P, KB * w], U8, name="z_scales%d" % s, align_bytes=64) for s, w in enumerate(width)]
+        q_codes = [keep.tile([P, KD * W], U32, name="q_codes%d" % s, align_bytes=64) for s in range(NS)]
+        q_scales = [keep.tile([P, KD * W], U8, name="q_scales%d" % s, align_bytes=64) for s in range(NS)]
+        z_codes = [keep.tile([P, KB * W], U32, name="z_codes%d" % s, align_bytes=64) for s in range(NS)]
+        z_scales = [keep.tile([P, KB * W], U8, name="z_scales%d" % s, align_bytes=64) for s in range(NS)]
         c_codes = keep.tile([P, KB, 2 * DOCS], U8, name="c_codes", align_bytes=64)
         c_scales = keep.tile([P, KB, DOCS], U8, name="c_scales", align_bytes=64)
 
@@ -57,13 +59,9 @@ def tile_soft_hyperplane_hashing_s13_kernel(tc, planes, queries_bytes, queries_s
         out_view = out.rearrange("(s p i) d -> s i p d", p=P, i=2)
 
         q_bytes = {}
-        q_load = {}
-        q_single = {}
-        p_raw = {}
         p_rows = {}
-        q_cast = {}
-        q_banks = {}
-        p_bank = {}
+        words = {}
+        banks = {}
         p_group = {}
         q_group = {}
         h_bank = {}
@@ -71,142 +69,161 @@ def tile_soft_hyperplane_hashing_s13_kernel(tc, planes, queries_bytes, queries_s
         z_group = {}
         o_tile = {}
 
-        def load_q(b, n, g0=0, g1=KD):
+        def copy(engine, dst, src):
+            if engine is S:
+                S.copy(out=dst, in_=src)
+            else:
+                engine.tensor_copy(out=dst, in_=src)
+
+        def load_q(b, n, g0=0, g1=KD, queue=nc.sync):
             raw = keep.tile([P, n * (g1 - g0) * 512], U8, name="q_bytes%d%d" % (b, g0))
-            nc.sync.dma_start(out=raw[:].rearrange("p (n k) -> p n k", n=n), in_=q_view[b // 2][:, b % 2 : b % 2 + n, g0 * 512 : g1 * 512])
-            q_load[b, g0] = (raw, n, g1)
-            if g1 - g0 == KD:
-                for i in range(n):
-                    q_bytes[b + i] = raw[:, i * D : (i + 1) * D]
+            queue.dma_start(out=raw[:].rearrange("p (n k) -> p n k", n=n), in_=q_view[b // 2][:, b % 2 : b % 2 + n, g0 * 512 : g1 * 512])
+            for i in range(n):
+                for g in range(g0, g1):
+                    q_bytes[b + i, g] = (raw, (i * (g1 - g0) + g - g0) * 512)
 
         def load_p(r, n, g0=0, g1=KD):
             raw = keep.tile([P, n * (g1 - g0) * 512], BF16, name="p_raw%d%d" % (r, g0))
             nc.sync.dma_start(out=raw[:].rearrange("p (n k) -> p n k", n=n), in_=p_view[r // 4][:, r % 4 : r % 4 + n, g0 * 512 : g1 * 512])
             for i in range(n):
-                if g1 - g0 == KD:
-                    p_rows[r + i] = raw[:, i * D : (i + 1) * D]
                 for g in range(g0, g1):
                     w0 = (i * (g1 - g0) + g - g0) * 256
-                    p_raw[r + i, g] = [raw[:].bitcast(F32)[:, w0 + u : w0 + 256 : 2] for u in range(2)]
+                    p_rows[r + i, g] = (raw, w0)
+                    words["p", r + i, g] = [raw[:].bitcast(F32)[:, w0 + u : w0 + 256 : 2] for u in range(2)]
 
-        def sort_p(r):
-            wide = work.tile([P, 2, KD * P], F32, name="p_sorted", bufs=3)
-            nc.scalar.copy(out=wide[:], in_=p_rows[r].bitcast(F32).rearrange("p (w u) -> p u w", u=2))
-            for g in range(KD):
-                p_raw[r, g] = [wide[:, u, g * P : (g + 1) * P] for u in range(2)]
+        def sort_p(r, engine, g0=0, g1=KD):
+            n = g1 - g0
+            wide = work.tile([P, 2, n * P], F32, name="p_sorted%d" % n, bufs=4)
+            raw, w0 = p_rows[r, g0]
+            if engine is G:
+                G.tensor_scalar(
+                    out=wide[:].rearrange("p u w -> p (u w)").bitcast(BF16).rearrange("p (u w e) -> p u w e", u=2, e=2),
+                    in0=raw[:, 2 * w0 : 2 * w0 + n * 512].rearrange("p (w u e) -> p u w e", u=2, e=2),
+                    scalar1=1.0,
+                    scalar2=0.0,
+                    op0=MULT,
+                    op1=ADD,
+                )
+            else:
+                copy(engine, wide[:], raw[:].bitcast(F32)[:, w0 : w0 + n * 256].rearrange("p (w u) -> p u w", u=2))
+            for g in range(g0, g1):
+                words["p", r, g] = [wide[:, u, (g - g0) * P : (g - g0 + 1) * P] for u in range(2)]
 
         def warm_up(n):
-            bank = psum.tile([P, 512], F32, name="hbank", bufs=8)
+            bank = psum.tile([P, 512], F32, name="bank")
             for j in range(n):
                 nc.tensor.matmul(bank[:], lhsT=zeros[:, 0:P], rhs=zeros[:], start=True, stop=True)
 
-        def cast(b):
-            wide = work.tile([P, 2, KD * P, 2], BF16, name="q_cast", bufs=4)
-            nc.vector.tensor_scalar(
+        def spread_turn(g):
+            bank = psum.tile([P, 4, P], F32, name="bank")
+            banks["s", g] = bank
+            for t in range(4):
+                nc.tensor.transpose(bank[:, t, :], q_scale[:, 4 * g + t : 4 * g + t + 1].to_broadcast([P, P]), ident[:])
+
+        def cast(b, g0=0, g1=KD):
+            n = g1 - g0
+            wide = work.tile([P, 2, n * P, 2], BF16, name="q_cast%d" % n, bufs=4)
+            raw, c0 = q_bytes[b, g0]
+            V.tensor_scalar(
                 out=wide[:].rearrange("p u w e -> p w u e"),
-                in0=q_bytes[b].bitcast(FP8).rearrange("p (w u e) -> p w u e", u=2, e=2),
+                in0=raw[:, c0 : c0 + n * 512].bitcast(FP8).rearrange("p (w u e) -> p w u e", u=2, e=2),
                 scalar1=ones[:, 0:1],
                 scalar2=None,
                 op0=MULT,
             )
-            for g in range(KD):
-                q_single[b, g] = [wide[:, t // 2, g * P : (g + 1) * P, t % 2] for t in range(4)]
-            for g in range(KD):
-                q_cast[b, g] = [wide[:, u, :, :].rearrange("p w e -> p (w e)").bitcast(F32)[:, g * P : (g + 1) * P] for u in range(2)]
+            for g in range(g0, g1):
+                words["q", b, g] = [wide[:, u, :, :].rearrange("p w e -> p (w e)").bitcast(F32)[:, (g - g0) * P : (g - g0 + 1) * P] for u in range(2)]
 
-        def cast_plain(b, engine="s"):
-            wide = work.tile([P, D], BF16, name="q_plain", bufs=3)
-            if engine == "s":
-                nc.scalar.copy(out=wide[:], in_=q_bytes[b].bitcast(FP8))
-            else:
-                nc.vector.tensor_copy(out=wide[:], in_=q_bytes[b].bitcast(FP8))
-            for g in range(KD):
-                q_cast[b, g] = [wide[:].bitcast(F32)[:, 256 * g + u : 256 * (g + 1) : 2] for u in range(2)]
+        def cast_plain(b, g0=0, g1=KD):
+            n = g1 - g0
+            wide = work.tile([P, n * 512], BF16, name="q_plain%d" % n, bufs=3)
+            raw, c0 = q_bytes[b, g0]
+            S.copy(out=wide[:], in_=raw[:, c0 : c0 + n * 512].bitcast(FP8))
+            for g in range(g0, g1):
+                words["q", b, g] = [wide[:].bitcast(F32)[:, 256 * (g - g0) + u : 256 * (g - g0 + 1) : 2] for u in range(2)]
 
-        def q_parts(s):
-            if s == 0 and len(UNITS[s]) == 2:
-                return [[(0, 0), (1, 0)], [(0, 1), (1, 1)], [(2, 0), (2, 1)]]
-            if len(UNITS[s]) == 2:
-                return [[(g, 0), (g, 1)] for g in range(KD)]
-            return [[(0, 0), (1, 0)], [(2, 0)]]
-
-        def q_turn(s, n):
-            bank = psum.tile([P, 2, 2 * P], F32, name="hbank", bufs=8)
-            q_banks[s, n] = bank
-            for x, (g, i) in enumerate(q_parts(s)[n]):
+        def turn(name, *pieces):
+            bank = psum.tile([P, 2, 2 * P], F32, name="bank")
+            banks[name] = (bank, pieces)
+            for x, piece in enumerate(pieces):
                 for u in range(2):
-                    nc.tensor.transpose(bank[:, u, x * P : (x + 1) * P], q_cast[UNITS[s][i], g][u], ident[:])
+                    nc.tensor.transpose(bank[:, u, x * P : (x + 1) * P], words[piece][u], ident[:])
 
-        def q_exit(s, n):
-            if s not in q_group:
-                q_group[s] = work.tile([P, KD * 4 * width[s]], BF16, name="q_group", align_bytes=64, bufs=2)
-            parts = q_parts(s)[n]
-            nx = len(parts)
-            nb = len(UNITS[s])
-            pieces = q_group[s][:].rearrange("p (g i c u e) -> p g i c u e", g=KD, i=nb, u=2, e=2)
+        def place(piece):
+            kind, j, g = piece
+            if kind == "q":
+                if j // 2 not in q_group:
+                    q_group[j // 2] = work.tile([P, KD * 2 * 512], BF16, name="q_group", align_bytes=64, bufs=2)
+                return q_group[j // 2], 2 * g + j % 2
+            if j // 2 not in p_group:
+                p_group[j // 2] = work.tile([P, KD * 2 * 512], BF16, name="p_group", align_bytes=64, bufs=3)
+            return p_group[j // 2], KD * (j % 2) + g
+
+        def leave(name, engine, x0=0, x1=None):
+            bank, pieces = banks[name]
+            x1 = len(pieces) if x1 is None else x1
+            tile, a = place(pieces[x0])
+            z = place(pieces[x1 - 1])[1]
+            dst = tile[:].bitcast(F32).rearrange("p (x c u) -> p x c u", c=P, u=2)[:, a : z + 1 : max(z - a, 1)]
+            copy(engine, dst, bank[:].rearrange("p u (x c) -> p x c u", x=2)[:, x0:x1])
+
+        def leave_scaled(name, x0=0, x1=None):
+            bank, pieces = banks[name]
+            x1 = len(pieces) if x1 is None else x1
+            tile, a = place(pieces[x0])
+            z = place(pieces[x1 - 1])[1]
+            g0, g1 = pieces[x0][2], pieces[x1 - 1][2]
+            dst = tile[:].rearrange("p (x c u e) -> p x c u e", c=P, u=2, e=2)[:, a : z + 1 : max(z - a, 1)]
             scale = q_scale[:].rearrange("p (g o u e) -> p g o u e", o=1, u=2, e=2)
-            g0, i0 = parts[0]
-            if parts[-1][0] == g0:
-                dst = pieces[:, g0, i0 : i0 + nx]
-            else:
-                dst = pieces[:, g0 : g0 + nx, i0]
-            nc.vector.tensor_tensor(
+            V.tensor_tensor(
                 out=dst,
-                in0=q_banks[s, n][:].rearrange("p u c -> p (u c)").bitcast(BF16).rearrange("p (u x c e) -> p x c u e", u=2, x=2, e=2)[:, 0:nx],
-                in1=scale[:, g0 : parts[-1][0] + 1].to_broadcast([P, nx, P, 2, 2]),
+                in0=bank[:].rearrange("p u c -> p (u c)").bitcast(BF16).rearrange("p (u x c e) -> p x c u e", u=2, x=2, e=2)[:, x0:x1],
+                in1=scale[:, g0 : g1 + 1 : max(g1 - g0, 1)].to_broadcast([P, x1 - x0, P, 2, 2]),
                 op=MULT,
             )
 
-        def quantise(codes, scales, grouped, c0, c1):
-            nc.vector.quantize_mx(out=codes[:, c0:c1].bitcast(FP8X4), scales=scales[:, c0:c1], in_=grouped[:, 4 * c0 : 4 * c1])
-
         def q_quant(s, g0, g1):
-            quantise(q_codes[s], q_scales[s], q_group[s], g0 * width[s], g1 * width[s])
-
-        def p_turn(n, keep_warm=False):
-            bank = psum.tile([P, 512], F32, name="hbank", bufs=8)
-            if keep_warm:
-                nc.tensor.matmul(bank[:], lhsT=zeros[:, 0:P], rhs=zeros[:], start=True, stop=True)
-            for x in range(2):
-                r, g = divmod(2 * n + x, KD)
-                for u in range(2):
-                    nc.tensor.transpose(bank[:, u * 256 + x * P : u * 256 + (x + 1) * P], p_raw[r, g][u], ident[:])
-            if n % 3 == 0:
-                p_group[n // 3] = work.tile([P, 2 * D], BF16, name="p_group", align_bytes=64, bufs=3)
-            dst = p_group[n // 3][:].bitcast(F32)[:, (n % 3) * 512 : (n % 3 + 1) * 512]
-            nc.scalar.copy(out=dst.rearrange("p (c u) -> p c u", u=2), in_=bank[:].rearrange("p (u c) -> p c u", u=2))
+            V.quantize_mx(out=q_codes[s][:, g0 * W : g1 * W].bitcast(FP8X4), scales=q_scales[s][:, g0 * W : g1 * W], in_=q_group[s][:, 4 * g0 * W : 4 * g1 * W])
 
         def p_quant(r):
-            nc.vector.quantize_mx(out=p_codes[r][:].bitcast(FP8X4), scales=p_scales[r][:], in_=p_group[r // 2][:, (r % 2) * D : (r % 2 + 1) * D])
+            V.quantize_mx(out=p_codes[r][:].bitcast(FP8X4), scales=p_scales[r][:], in_=p_group[r // 2][:, (r % 2) * D : (r % 2 + 1) * D])
 
-        def project(s, r0, n, tag="hbank", g0=0, g1=KD):
-            w = width[s]
-            if g0 == 0:
-                h_bank[s, r0] = psum.tile([P, n, w], F32, name="hbank", bufs=8)
-            bank = h_bank[s, r0]
+        def p_turn(n, engine=None):
+            turn(("p", n), *[("p",) + divmod(2 * n + x, KD) for x in range(2)])
+            if engine is not None:
+                leave(("p", n), engine)
+
+        def project(s, r0, n=2):
+            bank = psum.tile([P, n, W], F32, name="bank")
+            h_bank[s, r0] = (bank, n)
             for x in range(n):
                 r = r0 + x
-                for g in range(g0, g1):
+                for g in range(KD):
                     nc.tensor.matmul_mx(
                         out=bank[:, x, :],
                         lhsT=p_codes[r][:, g * P : (g + 1) * P].bitcast(FP8X4),
                         lhsT_scale=p_scales[r][:, g * P : (g + 1) * P],
-                        rhs=q_codes[s][:, g * w : (g + 1) * w].bitcast(FP8X4),
-                        rhs_scale=q_scales[s][:, g * w : (g + 1) * w],
+                        rhs=q_codes[s][:, g * W : (g + 1) * W].bitcast(FP8X4),
+                        rhs_scale=q_scales[s][:, g * W : (g + 1) * W],
                         start=(x == 0 and g == 0),
                         stop=(x == n - 1 and g == KD - 1),
                     )
-            for x in range(n if g1 == KD else 0):
+
+        def soft_sign(s, r0):
+            bank, n = h_bank[s, r0]
+            for x in range(n):
                 r = r0 + x
                 if r % 4 == 0:
-                    tanh_out[s, r // 4] = work.tile([P, 4, w], F32, name="th", bufs=4)
-                nc.scalar.activation(out=tanh_out[s, r // 4][:, r % 4, :], in_=bank[:, x, :], func=ACT.Tanh, bias=off[:, r : r + 1])
+                    tanh_out[s, r // 4] = work.tile([P, 4, W], F32, name="th", bufs=4)
+                S.activation(out=tanh_out[s, r // 4][:, r % 4, :], in_=bank[:, x, :], func=ACT.Tanh, bias=off[:, r : r + 1])
 
-        def weight(s, gb, engine, c0=0, c1=None):
-            w = width[s]
-            c1 = w if c1 is None else c1
+        def project_tanh(s, r0, n=2):
+            project(s, r0, n)
+            soft_sign(s, r0)
+
+        def weight(s, gb, engine, c0=0, c1=W):
             if c0 == 0:
-                z_group[s, gb] = work.tile([P, 4 * w], BF16, name="z_group", align_bytes=64, bufs=2)
+                z_group[s, gb] = work.tile([P, 4 * W], BF16, name="z_group", align_bytes=64, bufs=2)
             walk = WALK if engine is V else 1
             engine.tensor_tensor(
                 out=z_group[s, gb][:, 4 * c0 : 4 * c1].rearrange("p (c i t) -> p c t i", i=walk, t=4),
@@ -215,20 +232,17 @@ def tile_soft_hyperplane_hashing_s13_kernel(tc, planes, queries_bytes, queries_s
                 op=MULT,
             )
 
-        def z_quant(s, gb, c0=0, c1=None):
-            w = width[s]
-            c1 = w if c1 is None else c1
-            cols = slice(gb * w + c0, gb * w + c1)
-            nc.vector.quantize_mx(out=z_codes[s][:, cols].bitcast(FP8X4), scales=z_scales[s][:, cols], in_=z_group[s, gb][:, 4 * c0 : 4 * c1])
+        def z_quant(s, gb, c0=0, c1=W):
+            cols = slice(gb * W + c0, gb * W + c1)
+            V.quantize_mx(out=z_codes[s][:, cols].bitcast(FP8X4), scales=z_scales[s][:, cols], in_=z_group[s, gb][:, 4 * c0 : 4 * c1])
 
-        def score(s, i, d, engine, run, own_queue=False):
-            w = width[s]
-            b = UNITS[s][i]
+        def score(s, i, d, engine, run=2, queue=nc.sync):
+            b = 2 * s + i
             if d % run == 0:
-                o_tile[b] = work.tile([P, run, NB], F32, name="ot%d" % run, bufs={1: 8, 2: 5, 4: 2}[run])
-            bank = psum.tile([P, NB], F32, name="hbank", bufs=8)
+                o_tile[b] = work.tile([P, run, NB], F32, name="ot%d" % run, bufs={1: 4, 2: 5, 4: 2}[run])
+            bank = psum.tile([P, NB], F32, name="bank")
             for gb in range(KB):
-                cols = slice(gb * w + i * P, gb * w + (i + 1) * P)
+                cols = slice(gb * W + i * P, gb * W + (i + 1) * P)
                 nc.tensor.matmul_mx(
                     out=bank[:],
                     lhsT=z_codes[s][:, cols].bitcast(FP8X4),
@@ -238,17 +252,13 @@ def tile_soft_hyperplane_hashing_s13_kernel(tc, planes, queries_bytes, queries_s
                     start=(gb == 0),
                     stop=(gb == KB - 1),
                 )
-            if engine == "s":
-                nc.scalar.copy(out=o_tile[b][:, d % run, :], in_=bank[:])
-            else:
-                nc.vector.tensor_copy(out=o_tile[b][:, d % run, :], in_=bank[:])
+            copy(engine, o_tile[b][:, d % run, :], bank[:])
             if d % run == run - 1:
-                queue = nc.scalar if own_queue else nc.sync
-                queue.dma_start(out=out_view[b // 2, b % 2][:, (d + 1 - run) * NB : (d + 1) * NB], in_=o_tile[b][:].rearrange("p e n -> p (e n)"))
+                queue.dma_start(out=out_view[s, i][:, (d + 1 - run) * NB : (d + 1) * NB], in_=o_tile[b][:].rearrange("p e n -> p (e n)"))
 
-        def scores(s, i, engines="ssss", run=2, two_queues=False):
+        def scores(s, i, engines, two_queues=False):
             for d in range(ND):
-                score(s, i, d, engines[d], run, two_queues and d == 1)
+                score(s, i, d, engines[d], 2, S if two_queues and d == 1 else nc.sync)
 
         def load_vec(dst, src):
             nc.sync.dma_start(out=dst[:].rearrange("p (g t) -> p g t", t=4), in_=src.rearrange("(g p t) -> p g t", p=P, t=4))
@@ -264,17 +274,13 @@ def tile_soft_hyperplane_hashing_s13_kernel(tc, planes, queries_bytes, queries_s
         def load_scale(queue):
             queue.dma_start(out=q_scale[:].rearrange("p (g t) -> p g t", t=4), in_=queries_scale.rearrange("o (g p t) -> p (o g) t", p=P, t=4))
 
-        def setup():
-            nc.vector.memset(zeros[:], 0.0)
-            nc.vector.memset(ones[:], 1.0)
-            nc.scalar.activation(out=warm[:], in_=ones[:], func=ACT.Tanh)
-            make_identity(nc, ident[:])
-            nc.vector.memset(c_scales[:].rearrange("p g n -> p (g n)").bitcast(U32), 0)
-
-        V, G = nc.vector, nc.gpsimd
         with tc.manual_schedule():
             load_q(0, 1)
-            setup()
+            V.memset(zeros[:], 0.0)
+            V.memset(ones[:], 1.0)
+            make_identity(nc, ident[:])
+            S.activation(out=warm[:], in_=ones[:], func=ACT.Tanh)
+            V.memset(c_scales[:].rearrange("p g n -> p (g n)").bitcast(U32), 0)
             for b in range(1, 4):
                 load_q(b, 1)
             load_scale(nc.sync)
@@ -288,52 +294,56 @@ def tile_soft_hyperplane_hashing_s13_kernel(tc, planes, queries_bytes, queries_s
             load_c()
             load_q(6, 2)
             warm_up(7)
+
             cast(0)
             cast(1)
             cast_plain(2)
-            cast(3)
-            q_turn(0, 0)
-            q_turn(0, 2)
-            q_turn(0, 1)
-            p_turn(0)
-            q_turn(1, 0)
-            q_exit(0, 0)
-            q_exit(0, 2)
-            q_exit(0, 1)
+            cast_plain(3, 0, 1)
+            turn("a", ("q", 0, 0), ("q", 0, 1))
+            turn("c", ("q", 0, 2), ("q", 1, 2))
+            turn("b", ("q", 1, 0), ("q", 1, 1))
+            p_turn(0, S)
+            turn("d", ("q", 2, 0), ("q", 3, 0))
+            cast_plain(3, 1, 2)
+            leave_scaled("a")
+            leave_scaled("c")
+            leave_scaled("b")
             for n in range(1, 4):
-                p_turn(n)
-            q_turn(1, 1)
-            q_exit(1, 0)
+                p_turn(n, S)
+            turn("e", ("q", 2, 1), ("q", 3, 1))
+            cast_plain(3, 2, 3)
+            leave_scaled("d")
             for n in range(4, 7):
-                p_turn(n)
+                p_turn(n, S)
             q_quant(0, 0, 2)
             p_quant(0)
             q_quant(0, 2, 3)
             p_quant(1)
-            q_exit(1, 1)
-            sort_p(6)
-            q_turn(1, 2)
-            p_turn(7)
-            sort_p(7)
-            p_turn(8)
-            project(0, 0, 2)
+            leave_scaled("e")
+            sort_p(6, S)
+            turn("f", ("q", 2, 2), ("q", 3, 2))
+            p_turn(7, S)
+            sort_p(7, S)
+            p_turn(8, S)
+            project_tanh(0, 0)
             p_quant(2)
             p_quant(3)
-            q_exit(1, 2)
+            leave_scaled("f")
             p_quant(4)
             p_quant(5)
             q_quant(1, 0, 2)
             q_quant(1, 2, 3)
             for n in range(9, 12):
-                p_turn(n)
+                p_turn(n, S)
             p_quant(6)
             p_quant(7)
-            project(0, 2, 2)
-            project(0, 4, 2)
-            project(1, 0, 2)
-            project(0, 6, 2)
+            project_tanh(0, 2)
+            project_tanh(0, 4)
+            project_tanh(1, 0)
+            project_tanh(0, 6)
             for r in range(2, 8, 2):
-                project(1, r, 2)
+                project_tanh(1, r)
+
             cast(4)
             weight(0, 0, V)
             cast(5)
@@ -341,46 +351,46 @@ def tile_soft_hyperplane_hashing_s13_kernel(tc, planes, queries_bytes, queries_s
             z_quant(0, 0)
             z_quant(0, 1)
             weight(1, 0, G)
-            for n in range(3):
-                q_turn(2, n)
-            for n in range(3):
-                q_exit(2, n)
+            for g in range(KD):
+                turn(("q", 2, g), ("q", 4, g), ("q", 5, g))
+            for g in range(KD):
+                leave_scaled(("q", 2, g))
             q_quant(2, 0, 2)
             q_quant(2, 2, 3)
-            scores(0, 0)
-            scores(0, 1)
+            scores(0, 0, [S] * 4)
+            scores(0, 1, [S] * 4)
             cast(6)
             cast(7)
             weight(1, 1, V)
             z_quant(1, 0)
             z_quant(1, 1)
             for r in range(0, 6, 2):
-                project(2, r, 2)
+                project_tanh(2, r)
             weight(2, 0, G)
-            for n in range(3):
-                q_turn(3, n)
-            for n in range(3):
-                q_exit(3, n)
+            for g in range(KD):
+                turn(("q", 3, g), ("q", 6, g), ("q", 7, g))
+            for g in range(KD):
+                leave_scaled(("q", 3, g))
             q_quant(3, 0, 2)
             q_quant(3, 2, 3)
-            scores(1, 0)
-            project(2, 6, 2)
-            scores(1, 1)
+            scores(1, 0, [S] * 4)
+            project_tanh(2, 6)
+            scores(1, 1, [S] * 4)
             weight(2, 1, V)
             z_quant(2, 0)
             z_quant(2, 1)
-            project(3, 0, 2)
-            project(3, 2, 2)
-            score(2, 0, 0, "v", 2)
-            score(2, 0, 1, "v", 2)
+            project_tanh(3, 0)
+            project_tanh(3, 2)
+            score(2, 0, 0, V)
+            score(2, 0, 1, V)
             weight(3, 0, V)
-            project(3, 4, 2)
-            project(3, 6, 2)
+            project_tanh(3, 4)
+            project_tanh(3, 6)
             z_quant(3, 0)
-            score(2, 0, 2, "v", 2)
-            score(2, 0, 3, "s", 2)
+            score(2, 0, 2, V)
+            score(2, 0, 3, S)
             weight(3, 1, V)
             z_quant(3, 1)
-            scores(2, 1, "ssvs", 2, True)
-            scores(3, 0, "vsvs", 2, True)
-            scores(3, 1, "vsvs", 2, True)
+            scores(2, 1, [S, S, V, S], True)
+            scores(3, 0, [V, S, V, S], True)
+            scores(3, 1, [V, S, V, S], True)

@@ -42,7 +42,6 @@ def tile_soft_hyperplane_hashing_s13_kernel(tc, planes, queries_bytes, queries_s
         ones = keep.tile([P, 1], F32, name="ones")
         warm = keep.tile([P, 1], F32, name="warm")
         q_scale = keep.tile([P, KD * 4], F32, name="q_scale")
-        spread = [keep.tile([P, 512], F32, name="spread%d" % g) for g in range(KD)]
         off = keep.tile([P, KB * 4], BF16, name="off")
         gain = keep.tile([P, KB * 4], BF16, name="gain")
         p_codes = [keep.tile([P, KD * P], U32, name="p_codes%d" % r, align_bytes=64) for r in range(NT)]
@@ -114,15 +113,9 @@ def tile_soft_hyperplane_hashing_s13_kernel(tc, planes, queries_bytes, queries_s
             for j in range(n):
                 nc.tensor.matmul(bank[:], lhsT=zeros[:, 0:P], rhs=zeros[:], start=True, stop=True)
 
-        def spread_turn(g):
-            bank = psum.tile([P, 4, P], F32, name="bank")
-            banks["s", g] = bank
-            for t in range(4):
-                nc.tensor.transpose(bank[:, t, :], q_scale[:, 4 * g + t : 4 * g + t + 1].to_broadcast([P, P]), ident[:])
-
         def cast(b, g0=0, g1=KD):
             n = g1 - g0
-            wide = work.tile([P, 2, n * P, 2], BF16, name="q_cast%d" % n, bufs=4)
+            wide = work.tile([P, 2, n * P, 2], BF16, name="q_cast%d" % n, bufs={1: 2, 2: 2, 3: 4}[n])
             raw, c0 = q_bytes[b, g0]
             V.tensor_scalar(
                 out=wide[:].rearrange("p u w e -> p w u e"),
@@ -136,7 +129,7 @@ def tile_soft_hyperplane_hashing_s13_kernel(tc, planes, queries_bytes, queries_s
 
         def cast_plain(b, g0=0, g1=KD):
             n = g1 - g0
-            wide = work.tile([P, n * 512], BF16, name="q_plain%d" % n, bufs=3)
+            wide = work.tile([P, n * 512], BF16, name="q_plain%d" % n, bufs={1: 6, 2: 2, 3: 2}[n])
             raw, c0 = q_bytes[b, g0]
             S.copy(out=wide[:], in_=raw[:, c0 : c0 + n * 512].bitcast(FP8))
             for g in range(g0, g1):
@@ -239,7 +232,7 @@ def tile_soft_hyperplane_hashing_s13_kernel(tc, planes, queries_bytes, queries_s
         def score(s, i, d, engine, run=2, queue=nc.sync):
             b = 2 * s + i
             if d % run == 0:
-                o_tile[b] = work.tile([P, run, NB], F32, name="ot%d" % run, bufs={1: 4, 2: 5, 4: 2}[run])
+                o_tile[b] = work.tile([P, run, NB], F32, name="ot%d" % run, bufs={1: 3, 2: 5, 4: 2}[run])
             bank = psum.tile([P, NB], F32, name="bank")
             for gb in range(KB):
                 cols = slice(gb * W + i * P, gb * W + (i + 1) * P)
@@ -281,10 +274,11 @@ def tile_soft_hyperplane_hashing_s13_kernel(tc, planes, queries_bytes, queries_s
             make_identity(nc, ident[:])
             S.activation(out=warm[:], in_=ones[:], func=ACT.Tanh)
             V.memset(c_scales[:].rearrange("p g n -> p (g n)").bitcast(U32), 0)
-            for b in range(1, 4):
-                load_q(b, 1)
+            load_q(1, 1)
+            load_q(2, 1)
             load_scale(nc.sync)
             load_p(0, 1, 0, 2)
+            load_q(3, 1)
             load_p(0, 1, 2, 3)
             for r in range(1, 8):
                 load_p(r, 1)
@@ -293,26 +287,31 @@ def tile_soft_hyperplane_hashing_s13_kernel(tc, planes, queries_bytes, queries_s
             load_vec(gain, bit_gain)
             load_c()
             load_q(6, 2)
-            warm_up(7)
-
-            cast(0)
-            cast(1)
-            cast_plain(2)
-            cast_plain(3, 0, 1)
+            warm_up(5)
+            cast_plain(0, 0, 1)
+            cast(0, 1, 3)
+            cast_plain(1, 2, 3)
+            cast(1, 0, 2)
+            cast_plain(2, 0, 2)
             turn("a", ("q", 0, 0), ("q", 0, 1))
             turn("c", ("q", 0, 2), ("q", 1, 2))
             turn("b", ("q", 1, 0), ("q", 1, 1))
-            p_turn(0, S)
+            p_turn(0)
+            cast_plain(3, 0, 1)
+            leave(("p", 0), S)
             turn("d", ("q", 2, 0), ("q", 3, 0))
             cast_plain(3, 1, 2)
             leave_scaled("a")
             leave_scaled("c")
             leave_scaled("b")
-            for n in range(1, 4):
-                p_turn(n, S)
+            p_turn(1, S)
+            p_turn(2, S)
+            cast_plain(2, 2, 3)
+            p_turn(3, S)
             turn("e", ("q", 2, 1), ("q", 3, 1))
             cast_plain(3, 2, 3)
             leave_scaled("d")
+
             for n in range(4, 7):
                 p_turn(n, S)
             q_quant(0, 0, 2)
@@ -320,7 +319,7 @@ def tile_soft_hyperplane_hashing_s13_kernel(tc, planes, queries_bytes, queries_s
             q_quant(0, 2, 3)
             p_quant(1)
             leave_scaled("e")
-            sort_p(6, S)
+            sort_p(6, V)
             turn("f", ("q", 2, 2), ("q", 3, 2))
             p_turn(7, S)
             sort_p(7, S)
@@ -340,13 +339,15 @@ def tile_soft_hyperplane_hashing_s13_kernel(tc, planes, queries_bytes, queries_s
             project_tanh(0, 2)
             project_tanh(0, 4)
             project_tanh(1, 0)
+            cast_plain(5, 2, 3)
             project_tanh(0, 6)
+            cast_plain(4, 2, 3)
             for r in range(2, 8, 2):
                 project_tanh(1, r)
 
-            cast(4)
+            cast(4, 0, 2)
             weight(0, 0, V)
-            cast(5)
+            cast(5, 0, 2)
             weight(0, 1, V)
             z_quant(0, 0)
             z_quant(0, 1)

@@ -16,7 +16,6 @@ FP8X4 = mybir.dt.float8_e4m3fn_x4
 FP4X4 = mybir.dt.float4_e2m1fn_x4
 ACT = mybir.ActivationFunctionType
 MULT = mybir.AluOpType.mult
-ADD = mybir.AluOpType.add
 
 P = 128
 KD = D // 512
@@ -35,7 +34,7 @@ def tile_soft_hyperplane_hashing_s13_kernel(tc, planes, queries_bytes, queries_s
     with ExitStack() as ctx:
         keep = ctx.enter_context(tc.tile_pool(name="keep", bufs=1))
         work = ctx.enter_context(tc.tile_pool(name="work", bufs=3))
-        psum = ctx.enter_context(tc.psum_pool(name="psum", bufs=8))
+        psum = ctx.enter_context(tc.psum_pool(name="psum", bufs=1))
 
         ident = keep.tile([P, P], F32, name="ident")
         zeros = keep.tile([P, 512], BF16, name="zeros")
@@ -68,6 +67,12 @@ def tile_soft_hyperplane_hashing_s13_kernel(tc, planes, queries_bytes, queries_s
         z_group = {}
         o_tile = {}
 
+        free_banks = list(range(8))
+
+        def take_bank(shape):
+            j = free_banks.pop(0)
+            return j, psum.tile(shape, F32, name="bank%d" % j)
+
         def copy(engine, dst, src):
             if engine is S:
                 S.copy(out=dst, in_=src)
@@ -90,32 +95,23 @@ def tile_soft_hyperplane_hashing_s13_kernel(tc, planes, queries_bytes, queries_s
                     p_rows[r + i, g] = (raw, w0)
                     words["p", r + i, g] = [raw[:].bitcast(F32)[:, w0 + u : w0 + 256 : 2] for u in range(2)]
 
-        def sort_p(r, engine, g0=0, g1=KD):
+        def sort_p(r, engine, name=None, g0=0, g1=KD):
             n = g1 - g0
-            wide = work.tile([P, 2, n * P], F32, name="p_sorted%d" % n, bufs=4)
+            wide = keep.tile([P, 2, n * P], F32, name=name or "p_sorted%d" % r, align_bytes=64)
             raw, w0 = p_rows[r, g0]
-            if engine is G:
-                G.tensor_scalar(
-                    out=wide[:].rearrange("p u w -> p (u w)").bitcast(BF16).rearrange("p (u w e) -> p u w e", u=2, e=2),
-                    in0=raw[:, 2 * w0 : 2 * w0 + n * 512].rearrange("p (w u e) -> p u w e", u=2, e=2),
-                    scalar1=1.0,
-                    scalar2=0.0,
-                    op0=MULT,
-                    op1=ADD,
-                )
-            else:
-                copy(engine, wide[:], raw[:].bitcast(F32)[:, w0 : w0 + n * 256].rearrange("p (w u) -> p u w", u=2))
+            copy(engine, wide[:], raw[:].bitcast(F32)[:, w0 : w0 + n * 256].rearrange("p (w u) -> p u w", u=2))
             for g in range(g0, g1):
                 words["p", r, g] = [wide[:, u, (g - g0) * P : (g - g0 + 1) * P] for u in range(2)]
 
         def warm_up(n):
-            bank = psum.tile([P, 512], F32, name="bank")
-            for j in range(n):
+            j, bank = take_bank([P, 512])
+            for x in range(n):
                 nc.tensor.matmul(bank[:], lhsT=zeros[:, 0:P], rhs=zeros[:], start=True, stop=True)
+            free_banks.append(j)
 
         def cast(b, g0=0, g1=KD):
             n = g1 - g0
-            wide = work.tile([P, 2, n * P, 2], BF16, name="q_cast%d" % n, bufs={1: 2, 2: 2, 3: 4}[n])
+            wide = work.tile([P, 2, n * P, 2], BF16, name="q_cast%d" % n, bufs={1: 2, 2: 3, 3: 2}[n])
             raw, c0 = q_bytes[b, g0]
             V.tensor_scalar(
                 out=wide[:].rearrange("p u w e -> p w u e"),
@@ -127,18 +123,18 @@ def tile_soft_hyperplane_hashing_s13_kernel(tc, planes, queries_bytes, queries_s
             for g in range(g0, g1):
                 words["q", b, g] = [wide[:, u, :, :].rearrange("p w e -> p (w e)").bitcast(F32)[:, (g - g0) * P : (g - g0 + 1) * P] for u in range(2)]
 
-        def cast_plain(b, g0=0, g1=KD):
+        def cast_plain(b, g0=0, g1=KD, engine=S):
             n = g1 - g0
             wide = work.tile([P, n * 512], BF16, name="q_plain%d" % n, bufs={1: 6, 2: 2, 3: 2}[n])
             raw, c0 = q_bytes[b, g0]
-            S.copy(out=wide[:], in_=raw[:, c0 : c0 + n * 512].bitcast(FP8))
+            copy(engine, wide[:], raw[:, c0 : c0 + n * 512].bitcast(FP8))
             for g in range(g0, g1):
                 words["q", b, g] = [wide[:].bitcast(F32)[:, 256 * (g - g0) + u : 256 * (g - g0 + 1) : 2] for u in range(2)]
 
-        def turn(name, *pieces):
-            bank = psum.tile([P, 2, 2 * P], F32, name="bank")
-            banks[name] = (bank, pieces)
-            for x, piece in enumerate(pieces):
+        def turn(name, *pieces, last_first=False):
+            j, bank = take_bank([P, 2, 2 * P])
+            banks[name] = (j, bank, pieces)
+            for x, piece in sorted(enumerate(pieces), reverse=last_first):
                 for u in range(2):
                     nc.tensor.transpose(bank[:, u, x * P : (x + 1) * P], words[piece][u], ident[:])
 
@@ -149,19 +145,21 @@ def tile_soft_hyperplane_hashing_s13_kernel(tc, planes, queries_bytes, queries_s
                     q_group[j // 2] = work.tile([P, KD * 2 * 512], BF16, name="q_group", align_bytes=64, bufs=2)
                 return q_group[j // 2], 2 * g + j % 2
             if j // 2 not in p_group:
-                p_group[j // 2] = work.tile([P, KD * 2 * 512], BF16, name="p_group", align_bytes=64, bufs=3)
+                p_group[j // 2] = keep.tile([P, KD * 2 * 512], BF16, name="p_group%d" % (j // 2), align_bytes=64)
             return p_group[j // 2], KD * (j % 2) + g
 
         def leave(name, engine, x0=0, x1=None):
-            bank, pieces = banks[name]
+            j, bank, pieces = banks[name]
             x1 = len(pieces) if x1 is None else x1
             tile, a = place(pieces[x0])
             z = place(pieces[x1 - 1])[1]
             dst = tile[:].bitcast(F32).rearrange("p (x c u) -> p x c u", c=P, u=2)[:, a : z + 1 : max(z - a, 1)]
             copy(engine, dst, bank[:].rearrange("p u (x c) -> p x c u", x=2)[:, x0:x1])
+            if x1 == len(pieces):
+                free_banks.append(j)
 
         def leave_scaled(name, x0=0, x1=None):
-            bank, pieces = banks[name]
+            j, bank, pieces = banks[name]
             x1 = len(pieces) if x1 is None else x1
             tile, a = place(pieces[x0])
             z = place(pieces[x1 - 1])[1]
@@ -174,6 +172,8 @@ def tile_soft_hyperplane_hashing_s13_kernel(tc, planes, queries_bytes, queries_s
                 in1=scale[:, g0 : g1 + 1 : max(g1 - g0, 1)].to_broadcast([P, x1 - x0, P, 2, 2]),
                 op=MULT,
             )
+            if x1 == len(pieces):
+                free_banks.append(j)
 
         def q_quant(s, g0, g1):
             V.quantize_mx(out=q_codes[s][:, g0 * W : g1 * W].bitcast(FP8X4), scales=q_scales[s][:, g0 * W : g1 * W], in_=q_group[s][:, 4 * g0 * W : 4 * g1 * W])
@@ -187,8 +187,8 @@ def tile_soft_hyperplane_hashing_s13_kernel(tc, planes, queries_bytes, queries_s
                 leave(("p", n), engine)
 
         def project(s, r0, n=2):
-            bank = psum.tile([P, n, W], F32, name="bank")
-            h_bank[s, r0] = (bank, n)
+            j, bank = take_bank([P, n, W])
+            h_bank[s, r0] = (j, bank, n)
             for x in range(n):
                 r = r0 + x
                 for g in range(KD):
@@ -203,12 +203,13 @@ def tile_soft_hyperplane_hashing_s13_kernel(tc, planes, queries_bytes, queries_s
                     )
 
         def soft_sign(s, r0):
-            bank, n = h_bank[s, r0]
+            j, bank, n = h_bank[s, r0]
             for x in range(n):
                 r = r0 + x
                 if r % 4 == 0:
                     tanh_out[s, r // 4] = work.tile([P, 4, W], F32, name="th", bufs=4)
                 S.activation(out=tanh_out[s, r // 4][:, r % 4, :], in_=bank[:, x, :], func=ACT.Tanh, bias=off[:, r : r + 1])
+            free_banks.append(j)
 
         def project_tanh(s, r0, n=2):
             project(s, r0, n)
@@ -233,7 +234,7 @@ def tile_soft_hyperplane_hashing_s13_kernel(tc, planes, queries_bytes, queries_s
             b = 2 * s + i
             if d % run == 0:
                 o_tile[b] = work.tile([P, run, NB], F32, name="ot%d" % run, bufs={1: 3, 2: 5, 4: 2}[run])
-            bank = psum.tile([P, NB], F32, name="bank")
+            j, bank = take_bank([P, NB])
             for gb in range(KB):
                 cols = slice(gb * W + i * P, gb * W + (i + 1) * P)
                 nc.tensor.matmul_mx(
@@ -246,6 +247,7 @@ def tile_soft_hyperplane_hashing_s13_kernel(tc, planes, queries_bytes, queries_s
                     stop=(gb == KB - 1),
                 )
             copy(engine, o_tile[b][:, d % run, :], bank[:])
+            free_banks.append(j)
             if d % run == run - 1:
                 queue.dma_start(out=out_view[s, i][:, (d + 1 - run) * NB : (d + 1) * NB], in_=o_tile[b][:].rearrange("p e n -> p (e n)"))
 
@@ -269,8 +271,8 @@ def tile_soft_hyperplane_hashing_s13_kernel(tc, planes, queries_bytes, queries_s
 
         with tc.manual_schedule():
             load_q(0, 1)
-            V.memset(zeros[:], 0.0)
             V.memset(ones[:], 1.0)
+            V.memset(zeros[:], 0.0)
             make_identity(nc, ident[:])
             S.activation(out=warm[:], in_=ones[:], func=ACT.Tanh)
             V.memset(c_scales[:].rearrange("p g n -> p (g n)").bitcast(U32), 0)
@@ -287,9 +289,9 @@ def tile_soft_hyperplane_hashing_s13_kernel(tc, planes, queries_bytes, queries_s
             load_vec(gain, bit_gain)
             load_c()
             load_q(6, 2)
-            warm_up(5)
-            cast_plain(0, 0, 1)
-            cast(0, 1, 3)
+            warm_up(3)
+            cast(0, 0, 2)
+            cast_plain(0, 2, 3)
             cast_plain(1, 2, 3)
             cast(1, 0, 2)
             cast_plain(2, 0, 2)
@@ -297,21 +299,24 @@ def tile_soft_hyperplane_hashing_s13_kernel(tc, planes, queries_bytes, queries_s
             turn("c", ("q", 0, 2), ("q", 1, 2))
             turn("b", ("q", 1, 0), ("q", 1, 1))
             p_turn(0)
+            turn("d", ("q", 2, 0), ("q", 2, 1))
+            cast_plain(2, 2, 3)
             cast_plain(3, 0, 1)
-            leave(("p", 0), S)
-            turn("d", ("q", 2, 0), ("q", 3, 0))
-            cast_plain(3, 1, 2)
             leave_scaled("a")
             leave_scaled("c")
             leave_scaled("b")
-            p_turn(1, S)
-            p_turn(2, S)
-            cast_plain(2, 2, 3)
-            p_turn(3, S)
-            turn("e", ("q", 2, 1), ("q", 3, 1))
-            cast_plain(3, 2, 3)
+            turn("p02", ("p", 0, 2))
+            turn("e", ("q", 3, 0), ("q", 2, 2), last_first=True)
+            cast_plain(3, 1, 3)
+            leave(("p", 0), S)
+            leave("p02", S)
+            turn("p10", ("p", 1, 0), ("p", 1, 1))
+            turn("p12", ("p", 1, 2))
+            leave("p10", S)
+            leave("p12", S)
+            turn("f", ("q", 3, 1), ("q", 3, 2))
             leave_scaled("d")
-
+            p_turn(3, S)
             for n in range(4, 7):
                 p_turn(n, S)
             q_quant(0, 0, 2)
@@ -319,8 +324,6 @@ def tile_soft_hyperplane_hashing_s13_kernel(tc, planes, queries_bytes, queries_s
             q_quant(0, 2, 3)
             p_quant(1)
             leave_scaled("e")
-            sort_p(6, V)
-            turn("f", ("q", 2, 2), ("q", 3, 2))
             p_turn(7, S)
             sort_p(7, S)
             p_turn(8, S)

@@ -289,7 +289,7 @@ def tile_soft_hyperplane_hashing_s13_kernel(tc, planes, queries_bytes, queries_s
             load_vec(gain, bit_gain)
             load_c()
             load_q(6, 2)
-            warm_up(3)
+            warm_up(5)
             cast(0, 0, 2)
             cast_plain(0, 2, 3)
             cast_plain(1, 2, 3)

@@ -34,7 +34,7 @@ def tile_soft_hyperplane_hashing_s13_kernel(tc, planes, queries_bytes, queries_s
     with ExitStack() as ctx:
         keep = ctx.enter_context(tc.tile_pool(name="keep", bufs=1))
         work = ctx.enter_context(tc.tile_pool(name="work", bufs=3))
-        psum = ctx.enter_context(tc.psum_pool(name="psum", bufs=1))
+        psum = ctx.enter_context(tc.psum_pool(name="psum", bufs=8))
 
         ident = keep.tile([P, P], F32, name="ident")
         zeros = keep.tile([P, 512], BF16, name="zeros")
@@ -67,12 +67,6 @@ def tile_soft_hyperplane_hashing_s13_kernel(tc, planes, queries_bytes, queries_s
         z_group = {}
         o_tile = {}
 
-        free_banks = list(range(8))
-
-        def take_bank(shape):
-            j = free_banks.pop(0)
-            return j, psum.tile(shape, F32, name="bank%d" % j)
-
         def copy(engine, dst, src):
             if engine is S:
                 S.copy(out=dst, in_=src)
@@ -99,15 +93,18 @@ def tile_soft_hyperplane_hashing_s13_kernel(tc, planes, queries_bytes, queries_s
             n = g1 - g0
             wide = keep.tile([P, 2, n * P], F32, name=name or "p_sorted%d" % r, align_bytes=64)
             raw, w0 = p_rows[r, g0]
-            copy(engine, wide[:], raw[:].bitcast(F32)[:, w0 : w0 + n * 256].rearrange("p (w u) -> p u w", u=2))
+            copy(
+                engine,
+                wide[:].rearrange("p u (a i) -> p a u i", i=4),
+                raw[:].bitcast(F32)[:, w0 : w0 + n * 256].rearrange("p (a i u) -> p a u i", i=4, u=2),
+            )
             for g in range(g0, g1):
                 words["p", r, g] = [wide[:, u, (g - g0) * P : (g - g0 + 1) * P] for u in range(2)]
 
         def warm_up(n):
-            j, bank = take_bank([P, 512])
+            bank = psum.tile([P, 512], F32, name="bank")
             for x in range(n):
                 nc.tensor.matmul(bank[:], lhsT=zeros[:, 0:P], rhs=zeros[:], start=True, stop=True)
-            free_banks.append(j)
 
         def cast(b, g0=0, g1=KD):
             n = g1 - g0
@@ -132,8 +129,8 @@ def tile_soft_hyperplane_hashing_s13_kernel(tc, planes, queries_bytes, queries_s
                 words["q", b, g] = [wide[:].bitcast(F32)[:, 256 * (g - g0) + u : 256 * (g - g0 + 1) : 2] for u in range(2)]
 
         def turn(name, *pieces, last_first=False):
-            j, bank = take_bank([P, 2, 2 * P])
-            banks[name] = (j, bank, pieces)
+            bank = psum.tile([P, 2, 2 * P], F32, name="bank")
+            banks[name] = (bank, pieces)
             for x, piece in sorted(enumerate(pieces), reverse=last_first):
                 for u in range(2):
                     nc.tensor.transpose(bank[:, u, x * P : (x + 1) * P], words[piece][u], ident[:])
@@ -149,17 +146,15 @@ def tile_soft_hyperplane_hashing_s13_kernel(tc, planes, queries_bytes, queries_s
             return p_group[j // 2], KD * (j % 2) + g
 
         def leave(name, engine, x0=0, x1=None):
-            j, bank, pieces = banks[name]
+            bank, pieces = banks[name]
             x1 = len(pieces) if x1 is None else x1
             tile, a = place(pieces[x0])
             z = place(pieces[x1 - 1])[1]
             dst = tile[:].bitcast(F32).rearrange("p (x c u) -> p x c u", c=P, u=2)[:, a : z + 1 : max(z - a, 1)]
             copy(engine, dst, bank[:].rearrange("p u (x c) -> p x c u", x=2)[:, x0:x1])
-            if x1 == len(pieces):
-                free_banks.append(j)
 
         def leave_scaled(name, x0=0, x1=None):
-            j, bank, pieces = banks[name]
+            bank, pieces = banks[name]
             x1 = len(pieces) if x1 is None else x1
             tile, a = place(pieces[x0])
             z = place(pieces[x1 - 1])[1]
@@ -172,8 +167,6 @@ def tile_soft_hyperplane_hashing_s13_kernel(tc, planes, queries_bytes, queries_s
                 in1=scale[:, g0 : g1 + 1 : max(g1 - g0, 1)].to_broadcast([P, x1 - x0, P, 2, 2]),
                 op=MULT,
             )
-            if x1 == len(pieces):
-                free_banks.append(j)
 
         def q_quant(s, g0, g1):
             V.quantize_mx(out=q_codes[s][:, g0 * W : g1 * W].bitcast(FP8X4), scales=q_scales[s][:, g0 * W : g1 * W], in_=q_group[s][:, 4 * g0 * W : 4 * g1 * W])
@@ -187,8 +180,8 @@ def tile_soft_hyperplane_hashing_s13_kernel(tc, planes, queries_bytes, queries_s
                 leave(("p", n), engine)
 
         def project(s, r0, n=2):
-            j, bank = take_bank([P, n, W])
-            h_bank[s, r0] = (j, bank, n)
+            bank = psum.tile([P, n, W], F32, name="bank")
+            h_bank[s, r0] = (bank, n)
             for x in range(n):
                 r = r0 + x
                 for g in range(KD):
@@ -203,13 +196,12 @@ def tile_soft_hyperplane_hashing_s13_kernel(tc, planes, queries_bytes, queries_s
                     )
 
         def soft_sign(s, r0):
-            j, bank, n = h_bank[s, r0]
+            bank, n = h_bank[s, r0]
             for x in range(n):
                 r = r0 + x
                 if r % 4 == 0:
                     tanh_out[s, r // 4] = work.tile([P, 4, W], F32, name="th", bufs=4)
                 S.activation(out=tanh_out[s, r // 4][:, r % 4, :], in_=bank[:, x, :], func=ACT.Tanh, bias=off[:, r : r + 1])
-            free_banks.append(j)
 
         def project_tanh(s, r0, n=2):
             project(s, r0, n)
@@ -234,7 +226,7 @@ def tile_soft_hyperplane_hashing_s13_kernel(tc, planes, queries_bytes, queries_s
             b = 2 * s + i
             if d % run == 0:
                 o_tile[b] = work.tile([P, run, NB], F32, name="ot%d" % run, bufs={1: 3, 2: 5, 4: 2}[run])
-            j, bank = take_bank([P, NB])
+            bank = psum.tile([P, NB], F32, name="bank")
             for gb in range(KB):
                 cols = slice(gb * W + i * P, gb * W + (i + 1) * P)
                 nc.tensor.matmul_mx(
@@ -247,7 +239,6 @@ def tile_soft_hyperplane_hashing_s13_kernel(tc, planes, queries_bytes, queries_s
                     stop=(gb == KB - 1),
                 )
             copy(engine, o_tile[b][:, d % run, :], bank[:])
-            free_banks.append(j)
             if d % run == run - 1:
                 queue.dma_start(out=out_view[s, i][:, (d + 1 - run) * NB : (d + 1) * NB], in_=o_tile[b][:].rearrange("p e n -> p (e n)"))
 
@@ -290,8 +281,9 @@ def tile_soft_hyperplane_hashing_s13_kernel(tc, planes, queries_bytes, queries_s
             load_c()
             load_q(6, 2)
             warm_up(5)
-            cast(0, 0, 2)
-            cast_plain(0, 2, 3)
+            cast(0, 0, 1)
+            cast_plain(0, 1, 2)
+            cast(0, 2, 3)
             cast_plain(1, 2, 3)
             cast(1, 0, 2)
             cast_plain(2, 0, 2)
@@ -325,8 +317,10 @@ def tile_soft_hyperplane_hashing_s13_kernel(tc, planes, queries_bytes, queries_s
             p_quant(1)
             leave_scaled("e")
             p_turn(7, S)
-            sort_p(7, S)
             p_turn(8, S)
+            p_turn(9)
+            sort_p(7, S)
+            leave(("p", 9), S)
             project_tanh(0, 0)
             p_quant(2)
             p_quant(3)
@@ -335,16 +329,17 @@ def tile_soft_hyperplane_hashing_s13_kernel(tc, planes, queries_bytes, queries_s
             p_quant(5)
             q_quant(1, 0, 2)
             q_quant(1, 2, 3)
-            for n in range(9, 12):
+            for n in range(10, 12):
                 p_turn(n, S)
             p_quant(6)
             p_quant(7)
             project_tanh(0, 2)
             project_tanh(0, 4)
-            project_tanh(1, 0)
             cast_plain(5, 2, 3)
+            project(1, 0)
             project_tanh(0, 6)
             cast_plain(4, 2, 3)
+            soft_sign(1, 0)
             for r in range(2, 8, 2):
                 project_tanh(1, r)
 
@@ -391,8 +386,8 @@ def tile_soft_hyperplane_hashing_s13_kernel(tc, planes, queries_bytes, queries_s
             project_tanh(3, 4)
             project_tanh(3, 6)
             z_quant(3, 0)
-            score(2, 0, 2, V)
-            score(2, 0, 3, S)
+            score(2, 0, 2, V, 1)
+            score(2, 0, 3, S, 1)
             weight(3, 1, V)
             z_quant(3, 1)
             scores(2, 1, [S, S, V, S], True)

from contextlib import ExitStack

import concourse.mybir as mybir
from concourse.masks import make_identity

BITS, D, Q, DOCS = 1024, 1536, 1024, 2048
FLOPS = 2 * BITS * D * Q + 2 * Q * BITS * DOCS

F32 = mybir.dt.float32
BF16 = mybir.dt.bfloat16
I32 = mybir.dt.int32
U32 = mybir.dt.uint32
U8 = mybir.dt.uint8
FP8 = mybir.dt.float8_e4m3fn
FP8X4 = mybir.dt.float8_e4m3fn_x4
FP4X4 = mybir.dt.float4_e2m1fn_x4
ACT = mybir.ActivationFunctionType
MULT = mybir.AluOpType.mult

P = 128
KD = D // 512
KB = BITS // 512
NB = 512
ND = DOCS // NB
WALK = 2
NT = BITS // P
NS = Q // (2 * P)
W = 2 * P


def tile_soft_hyperplane_hashing_s13_kernel(tc, planes, queries_bytes, queries_scale, offset, bit_gain, codes_words, codes_scales, out):
    nc = tc.nc
    V, S, G = nc.vector, nc.scalar, nc.gpsimd
    with ExitStack() as ctx:
        keep = ctx.enter_context(tc.tile_pool(name="keep", bufs=1))
        work = ctx.enter_context(tc.tile_pool(name="work", bufs=3))
        psum = ctx.enter_context(tc.psum_pool(name="psum", bufs=8))

        ident = keep.tile([P, P], F32, name="ident")
        zeros = keep.tile([P, 512], BF16, name="zeros")
        ones = keep.tile([P, 1], F32, name="ones")
        warm = keep.tile([P, 1], F32, name="warm")
        q_scale = keep.tile([P, KD * 4], F32, name="q_scale")
        off = keep.tile([P, KB * 4], BF16, name="off")
        gain = keep.tile([P, KB * 4], BF16, name="gain")
        p_codes = [keep.tile([P, KD * P], U32, name="p_codes%d" % r, align_bytes=64) for r in range(NT)]
        p_scales = [keep.tile([P, KD * P], U8, name="p_scales%d" % r, align_bytes=64) for r in range(NT)]
        q_codes = [keep.tile([P, KD * W], U32, name="q_codes%d" % s, align_bytes=64) for s in range(NS)]
        q_scales = [keep.tile([P, KD * W], U8, name="q_scales%d" % s, align_bytes=64) for s in range(NS)]
        z_codes = [keep.tile([P, KB * W], U32, name="z_codes%d" % s, align_bytes=64) for s in range(NS)]
        z_scales = [keep.tile([P, KB * W], U8, name="z_scales%d" % s, align_bytes=64) for s in range(NS)]
        c_codes = keep.tile([P, KB, 2 * DOCS], U8, name="c_codes", align_bytes=64)
        c_scales = keep.tile([P, KB, DOCS], U8, name="c_scales", align_bytes=64)

        q_view = queries_bytes.rearrange("(s p i) k -> s p i k", p=P, i=2)
        p_view = planes.rearrange("(g m t) k -> g m t k", m=P, t=4)
        out_view = out.rearrange("(s p i) d -> s i p d", p=P, i=2)

        q_bytes = {}
        p_rows = {}
        words = {}
        banks = {}
        p_group = {}
        q_group = {}
        h_bank = {}
        tanh_out = {}
        z_group = {}
        o_tile = {}

        def copy(engine, dst, src):
            if engine is S:
                S.copy(out=dst, in_=src)
            else:
                engine.tensor_copy(out=dst, in_=src)

        def load_q(b, n, g0=0, g1=KD, queue=nc.sync):
            raw = keep.tile([P, n * (g1 - g0) * 512], U8, name="q_bytes%d%d" % (b, g0))
            queue.dma_start(out=raw[:].rearrange("p (n k) -> p n k", n=n), in_=q_view[b // 2][:, b % 2 : b % 2 + n, g0 * 512 : g1 * 512])
            for i in range(n):
                for g in range(g0, g1):
                    q_bytes[b + i, g] = (raw, (i * (g1 - g0) + g - g0) * 512)

        def load_p(r, n, g0=0, g1=KD):
            raw = keep.tile([P, n * (g1 - g0) * 512], BF16, name="p_raw%d%d" % (r, g0))
            nc.sync.dma_start(out=raw[:].rearrange("p (n k) -> p n k", n=n), in_=p_view[r // 4][:, r % 4 : r % 4 + n, g0 * 512 : g1 * 512])
            for i in range(n):
                for g in range(g0, g1):
                    w0 = (i * (g1 - g0) + g - g0) * 256
                    p_rows[r + i, g] = (raw, w0)
                    words["p", r + i, g] = [raw[:].bitcast(F32)[:, w0 + u : w0 + 256 : 2] for u in range(2)]

        def sort_p(r, engine, name=None, g0=0, g1=KD):
            n = g1 - g0
            wide = keep.tile([P, 2, n * P], F32, name=name or "p_sorted%d" % r, align_bytes=64)
            raw, w0 = p_rows[r, g0]
            copy(
                engine,
                wide[:].rearrange("p u (a i) -> p a u i", i=4),
                raw[:].bitcast(F32)[:, w0 : w0 + n * 256].rearrange("p (a i u) -> p a u i", i=4, u=2),
            )
            for g in range(g0, g1):
                words["p", r, g] = [wide[:, u, (g - g0) * P : (g - g0 + 1) * P] for u in range(2)]

        def warm_up(n):
            bank = psum.tile([P, 512], F32, name="bank")
            for x in range(n):
                nc.tensor.matmul(bank[:], lhsT=zeros[:, 0:P], rhs=zeros[:], start=True, stop=True)

        def cast(b, g0=0, g1=KD):
            n = g1 - g0
            wide = work.tile([P, 2, n * P, 2], BF16, name="q_cast%d" % n, bufs={1: 2, 2: 3, 3: 2}[n])
            raw, c0 = q_bytes[b, g0]
            V.tensor_scalar(
                out=wide[:].rearrange("p u w e -> p w u e"),
                in0=raw[:, c0 : c0 + n * 512].bitcast(FP8).rearrange("p (w u e) -> p w u e", u=2, e=2),
                scalar1=ones[:, 0:1],
                scalar2=None,
                op0=MULT,
            )
            for g in range(g0, g1):
                words["q", b, g] = [wide[:, u, :, :].rearrange("p w e -> p (w e)").bitcast(F32)[:, (g - g0) * P : (g - g0 + 1) * P] for u in range(2)]

        def cast_plain(b, g0=0, g1=KD, engine=S):
            n = g1 - g0
            wide = work.tile([P, n * 512], BF16, name="q_plain%d" % n, bufs={1: 6, 2: 2, 3: 2}[n])
            raw, c0 = q_bytes[b, g0]
            copy(engine, wide[:], raw[:, c0 : c0 + n * 512].bitcast(FP8))
            for g in range(g0, g1):
                words["q", b, g] = [wide[:].bitcast(F32)[:, 256 * (g - g0) + u : 256 * (g - g0 + 1) : 2] for u in range(2)]

        def turn(name, *pieces, last_first=False):
            bank = psum.tile([P, 2, 2 * P], F32, name="bank")
            banks[name] = (bank, pieces)
            for x, piece in sorted(enumerate(pieces), reverse=last_first):
                for u in range(2):
                    nc.tensor.transpose(bank[:, u, x * P : (x + 1) * P], words[piece][u], ident[:])

        def place(piece):
            kind, j, g = piece
            if kind == "q":
                if j // 2 not in q_group:
                    q_group[j // 2] = work.tile([P, KD * 2 * 512], BF16, name="q_group", align_bytes=64, bufs=2)
                return q_group[j // 2], 2 * g + j % 2
            if j // 2 not in p_group:
                p_group[j // 2] = keep.tile([P, KD * 2 * 512], BF16, name="p_group%d" % (j // 2), align_bytes=64)
            return p_group[j // 2], KD * (j % 2) + g

        def leave(name, engine, x0=0, x1=None):
            bank, pieces = banks[name]
            x1 = len(pieces) if x1 is None else x1
            tile, a = place(pieces[x0])
            z = place(pieces[x1 - 1])[1]
            dst = tile[:].bitcast(F32).rearrange("p (x c u) -> p x c u", c=P, u=2)[:, a : z + 1 : max(z - a, 1)]
            copy(engine, dst, bank[:].rearrange("p u (x c) -> p x c u", x=2)[:, x0:x1])

        def leave_scaled(name, x0=0, x1=None):
            bank, pieces = banks[name]
            x1 = len(pieces) if x1 is None else x1
            tile, a = place(pieces[x0])
            z = place(pieces[x1 - 1])[1]
            g0, g1 = pieces[x0][2], pieces[x1 - 1][2]
            dst = tile[:].rearrange("p (x c u e) -> p x c u e", c=P, u=2, e=2)[:, a : z + 1 : max(z - a, 1)]
            scale = q_scale[:].rearrange("p (g o u e) -> p g o u e", o=1, u=2, e=2)
            V.tensor_tensor(
                out=dst,
                in0=bank[:].rearrange("p u c -> p (u c)").bitcast(BF16).rearrange("p (u x c e) -> p x c u e", u=2, x=2, e=2)[:, x0:x1],
                in1=scale[:, g0 : g1 + 1 : max(g1 - g0, 1)].to_broadcast([P, x1 - x0, P, 2, 2]),
                op=MULT,
            )

        def q_quant(s, g0, g1):
            V.quantize_mx(out=q_codes[s][:, g0 * W : g1 * W].bitcast(FP8X4), scales=q_scales[s][:, g0 * W : g1 * W], in_=q_group[s][:, 4 * g0 * W : 4 * g1 * W])

        def p_quant(r):
            V.quantize_mx(out=p_codes[r][:].bitcast(FP8X4), scales=p_scales[r][:], in_=p_group[r // 2][:, (r % 2) * D : (r % 2 + 1) * D])

        def p_turn(n, engine=None):
            turn(("p", n), *[("p",) + divmod(2 * n + x, KD) for x in range(2)])
            if engine is not None:
                leave(("p", n), engine)

        def project(s, r0, n=2):
            bank = psum.tile([P, n, W], F32, name="bank")
            h_bank[s, r0] = (bank, n)
            for x in range(n):
                r = r0 + x
                for g in range(KD):
                    nc.tensor.matmul_mx(
                        out=bank[:, x, :],
                        lhsT=p_codes[r][:, g * P : (g + 1) * P].bitcast(FP8X4),
                        lhsT_scale=p_scales[r][:, g * P : (g + 1) * P],
                        rhs=q_codes[s][:, g * W : (g + 1) * W].bitcast(FP8X4),
                        rhs_scale=q_scales[s][:, g * W : (g + 1) * W],
                        start=(x == 0 and g == 0),
                        stop=(x == n - 1 and g == KD - 1),
                    )

        def soft_sign(s, r0):
            bank, n = h_bank[s, r0]
            for x in range(n):
                r = r0 + x
                if r % 4 == 0:
                    tanh_out[s, r // 4] = work.tile([P, 4, W], F32, name="th", bufs=4)
                S.activation(out=tanh_out[s, r // 4][:, r % 4, :], in_=bank[:, x, :], func=ACT.Tanh, bias=off[:, r : r + 1])

        def project_tanh(s, r0, n=2):
            project(s, r0, n)
            soft_sign(s, r0)

        def weight(s, gb, engine, c0=0, c1=W):
            if c0 == 0:
                z_group[s, gb] = work.tile([P, 4 * W], BF16, name="z_group", align_bytes=64, bufs=2)
            walk = WALK if engine is V else 1
            engine.tensor_tensor(
                out=z_group[s, gb][:, 4 * c0 : 4 * c1].rearrange("p (c i t) -> p c t i", i=walk, t=4),
                in0=tanh_out[s, gb][:, :, c0:c1].rearrange("p t (c i) -> p c t i", i=walk),
                in1=gain[:, gb * 4 : gb * 4 + 4].rearrange("p (o t i) -> p o t i", o=1, i=1).to_broadcast([P, (c1 - c0) // walk, 4, walk]),
                op=MULT,
            )

        def z_quant(s, gb, c0=0, c1=W):
            cols = slice(gb * W + c0, gb * W + c1)
            V.quantize_mx(out=z_codes[s][:, cols].bitcast(FP8X4), scales=z_scales[s][:, cols], in_=z_group[s, gb][:, 4 * c0 : 4 * c1])

        def score(s, i, d, engine, run=2, queue=nc.sync):
            b = 2 * s + i
            if d % run == 0:
                o_tile[b] = work.tile([P, run, NB], F32, name="ot%d" % run, bufs={1: 3, 2: 5, 4: 2}[run])
            bank = psum.tile([P, NB], F32, name="bank")
            for gb in range(KB):
                cols = slice(gb * W + i * P, gb * W + (i + 1) * P)
                nc.tensor.matmul_mx(
                    out=bank[:],
                    lhsT=z_codes[s][:, cols].bitcast(FP8X4),
                    lhsT_scale=z_scales[s][:, cols],
                    rhs=c_codes[:, gb, d * 2 * NB : (d + 1) * 2 * NB].bitcast(FP4X4),
                    rhs_scale=c_scales[:, gb, d * NB : (d + 1) * NB],
                    start=(gb == 0),
                    stop=(gb == KB - 1),
                )
            copy(engine, o_tile[b][:, d % run, :], bank[:])
            if d % run == run - 1:
                queue.dma_start(out=out_view[s, i][:, (d + 1 - run) * NB : (d + 1) * NB], in_=o_tile[b][:].rearrange("p e n -> p (e n)"))

        def scores(s, i, engines, two_queues=False):
            for d in range(ND):
                score(s, i, d, engines[d], 2, S if two_queues and d == 1 else nc.sync)

        def load_vec(dst, src):
            nc.sync.dma_start(out=dst[:].rearrange("p (g t) -> p g t", t=4), in_=src.rearrange("(g p t) -> p g t", p=P, t=4))

        def load_c():
            nc.sync.dma_start(out=c_codes[:].bitcast(I32), in_=codes_words.rearrange("g p n -> p g n").bitcast(I32))
            for qd in range(4):
                nc.sync.dma_start(
                    out=c_scales[32 * qd : 32 * qd + 4, :, :].bitcast(I32),
                    in_=codes_scales.rearrange("g q n -> q g n")[4 * qd : 4 * qd + 4].bitcast(I32),
                )

        def load_scale(queue):
            queue.dma_start(out=q_scale[:].rearrange("p (g t) -> p g t", t=4), in_=queries_scale.rearrange("o (g p t) -> p (o g) t", p=P, t=4))

        with tc.manual_schedule():
            load_q(0, 1)
            V.memset(ones[:], 1.0)
            V.memset(zeros[:], 0.0)
            make_identity(nc, ident[:])
            S.activation(out=warm[:], in_=ones[:], func=ACT.Tanh)
            V.memset(c_scales[:].rearrange("p g n -> p (g n)").bitcast(U32), 0)
            load_q(1, 1)
            load_q(2, 1)
            load_scale(nc.sync)
            load_p(0, 1, 0, 2)
            load_q(3, 1)
            load_p(0, 1, 2, 3)
            for r in range(1, 8):
                load_p(r, 1)
            load_vec(off, offset)
            load_q(4, 2)
            load_vec(gain, bit_gain)
            load_c()
            load_q(6, 2)
            warm_up(5)
            cast(0, 0, 1)
            cast_plain(0, 1, 2)
            cast(0, 2, 3)
            cast_plain(1, 2, 3)
            cast(1, 0, 2)
            cast_plain(2, 0, 2)
            turn("a", ("q", 0, 0), ("q", 0, 1))
            turn("c", ("q", 0, 2), ("q", 1, 2))
            turn("b", ("q", 1, 0), ("q", 1, 1))
            p_turn(0)
            turn("d", ("q", 2, 0), ("q", 2, 1))
            cast_plain(2, 2, 3)
            cast_plain(3, 0, 1)
            leave_scaled("a")
            leave_scaled("c")
            leave_scaled("b")
            turn("p02", ("p", 0, 2))
            turn("e", ("q", 3, 0), ("q", 2, 2), last_first=True)
            cast_plain(3, 1, 3)
            leave(("p", 0), S)
            leave("p02", S)
            turn("p10", ("p", 1, 0), ("p", 1, 1))
            turn("p12", ("p", 1, 2))
            leave("p10", S)
            leave("p12", S)
            turn("f", ("q", 3, 1), ("q", 3, 2))
            leave_scaled("d")
            p_turn(3, S)
            for n in range(4, 7):
                p_turn(n, S)
            q_quant(0, 0, 2)
            p_quant(0)
            q_quant(0, 2, 3)
            p_quant(1)
            leave_scaled("e")
            p_turn(7, S)
            p_turn(8, S)
            p_turn(9)
            sort_p(7, S)
            leave(("p", 9), S)
            project_tanh(0, 0)
            p_quant(2)
            p_quant(3)
            leave_scaled("f")
            p_quant(4)
            p_quant(5)
            q_quant(1, 0, 2)
            q_quant(1, 2, 3)
            for n in range(10, 12):
                p_turn(n, S)
            p_quant(6)
            p_quant(7)
            project_tanh(0, 2)
            project_tanh(0, 4)
            cast_plain(5, 2, 3)
            project(1, 0)
            project_tanh(0, 6)
            cast_plain(4, 2, 3)
            soft_sign(1, 0)
            for r in range(2, 8, 2):
                project_tanh(1, r)

            cast(4, 0, 2)
            weight(0, 0, V)
            cast(5, 0, 2)
            weight(0, 1, V)
            z_quant(0, 0)
            z_quant(0, 1)
            weight(1, 0, G)
            for g in range(KD):
                turn(("q", 2, g), ("q", 4, g), ("q", 5, g))
            for g in range(KD):
                leave_scaled(("q", 2, g))
            q_quant(2, 0, 2)
            q_quant(2, 2, 3)
            scores(0, 0, [S] * 4)
            scores(0, 1, [S] * 4)
            cast(6)
            cast(7)
            weight(1, 1, V)
            z_quant(1, 0)
            z_quant(1, 1)
            for r in range(0, 6, 2):
                project_tanh(2, r)
            weight(2, 0, G)
            for g in range(KD):
                turn(("q", 3, g), ("q", 6, g), ("q", 7, g))
            for g in range(KD):
                leave_scaled(("q", 3, g))
            q_quant(3, 0, 2)
            q_quant(3, 2, 3)
            scores(1, 0, [S] * 4)
            project_tanh(2, 6)
            scores(1, 1, [S] * 4)
            weight(2, 1, V)
            z_quant(2, 0)
            z_quant(2, 1)
            project_tanh(3, 0)
            project_tanh(3, 2)
            score(2, 0, 0, V)
            score(2, 0, 1, V)
            weight(3, 0, V)
            project_tanh(3, 4)
            project_tanh(3, 6)
            z_quant(3, 0)
            score(2, 0, 2, V, 1)
            score(2, 0, 3, S, 1)
            weight(3, 1, V)
            z_quant(3, 1)
            scores(2, 1, [S, S, V, S], True)
            scores(3, 0, [V, S, V, S], True)
            scores(3, 1, [V, S, V, S], True)
